import numpy as np, ml_dtypes
CORES = [3,7,11,15,131,135,139,143]
N = 8
BF = ml_dtypes.bfloat16
L0, CAP, RO, B, OFF, H = 640, 96, 4, 256, (7, 4), 64
G = B * len(OFF); LM = L0 + RO * CAP; W0 = G + L0
Q0 = B // 2
def fit(x):
    return np.minimum(np.maximum(x, 0.0009765625), 2.0).astype(np.float32)
def places(lev, a):
    return np.concatenate([lev[(a + o) % N, :B] for o in OFF] + [lev[a]])
def body(rng, lev, lo, hi):
    gf = np.exp2(rng.uniform(-0.4, 0.4, (N, 8, 1, L0)))
    return fit((lev[:, None, None, :] * gf * rng.uniform(lo, hi, (N, 8, 16, L0))).reshape(N, 128, L0))
def weave(rng, lev, l, share):
    for a in range(N):
        key = np.log2(places(lev, a))
        for g in range(8):
            o = np.argsort(key + 0.4 * rng.standard_normal(W0)); at = np.argsort(o)[G:]
            near = o[np.clip(at + rng.integers(-48, 49, (16, L0)), 0, W0 - 1)]
            l[a, g] = np.where(rng.random(L0) < share, near, l[a, g])
    return l
def two(rng, n):
    i = rng.integers(0, 16, (8, 1, n)); return i, (i + rng.integers(1, 16, (8, 1, n))) % 16
def knife(rng, n):
    F = np.float32; h = F(0.5); q = F(0.75); z = rng.uniform(0.1, 0.6, (8192, 1)).astype(np.float32)
    x = (0.5 * np.reciprocal(1.0 - 0.75 * z.astype(np.float64))).astype(np.float32) + F(2.0 ** -24) * np.arange(-8, 9).astype(np.float32)
    say = ((x + h) - q * (z * x)) > 1; xs = []; zs = []
    for o in (((x + h) - (q * z) * x) > 1, ((x + h) - z * (q * x)) > 1, (x * (F(1) - q * z) + h) > 1, ((x - q * (z * x)) + h) > 1):
        i, j = np.nonzero(say != o); s = rng.integers(0, len(i), n)
        xs.append(x[i[s], j[s]]); zs.append(z[i[s], 0])
    return np.concatenate(xs), np.concatenate(zs)
def late(rng, x, l):
    alt = np.arange(16)[None, :, None] % 2; hub = 2 + np.arange(8)[:, None, None] // 3; D = 2 ** (RO - 1); f = 8 * RO
    x[:, :8] = 0.5 * (4 - RO); l[:, :, :8] = Q0 + alt * hub
    v = np.arange(8, f); rk = np.argsort(rng.random((128, len(v))), axis=0)
    x[:, v] = np.where(rk < H - 1, 1.5, np.where(rk == H - 1, 1.0 + 2.0 ** -24 * (v % 4) - 0.125 * (v // 8 + 1), 0.0)); l[:, :, v] = Q0 + alt
    o = rng.permutation(np.concatenate([np.arange(f, Q0), np.arange(Q0 + 5, L0)]))
    for s in range(RO - 2):
        c = o[s * CAP:(s + 1) * CAP]; rk = np.argsort(rng.random((128, CAP)), axis=0); n = rng.choice(np.array([H, H + 1, 128]), CAP)
        x[:, c] = np.where(rk < n, rng.uniform(1.001, 1.015, (128, CAP)) - 0.125 * (s + 1), 0.0); l[:, :, c] = Q0 + alt
    o = o[(RO - 2) * CAP:]
    for i in range(6):
        c = o[(D + 1) * i:(D + 1) * (i + 1)]; x[:, c] = 0.0; l[:, :, c[:D]] = G + c[1:]; l[:, :, c[D]] = Q0
        if i < 3:
            l[:, :, c[D - 1]] = G + Q0 + 2 + i; x[48 * i:48 * i + 48, c[0]] = 2.0
        else:
            b = rng.uniform(0.004, 0.03, 128).astype(np.float32); hit = (np.arange(16)[None, :] == rng.integers(0, 16, (8, 1))).reshape(-1); up = np.repeat((np.arange(8) + i) % 2 == 1, 16)
            x[:, c[0]] = b; x[:, c[D]] = np.where(hit & up, np.nextafter(b, np.float32(1)), np.where(hit, np.nextafter(b, np.float32(0)), b))
    o = o[6 * (D + 1):]; c = o[:24]; e = o[24:]
    x[:, c] = np.where(rng.random((128, 24)) < 0.1, 0.0009765625, 0.0); l[:, :, c] = G + c[rng.integers(0, 24, (8, 16, 24))]
    l[:, :, e] = G + e[rng.integers(0, len(e), (8, 16, len(e)))]
def pack(x, l):
    return {"x0": np.ascontiguousarray(x).astype(np.float32), "nb": np.ascontiguousarray(l.reshape(N, 128, L0)).astype(np.int32)}
def setup_inputs(rng):
    lev = np.exp2(rng.uniform(-3, 0.8, (N, L0)))
    return pack(body(rng, lev, 0.7, 1.3), weave(rng, lev, rng.integers(0, W0, (N, 8, 16, L0)), 0.4))
def setup_inputs_spread(rng):
    lev = np.exp2(rng.uniform(-9, 1, (N, L0))); l = np.minimum((W0 * rng.random((N, 8, 16, L0)) ** 3).astype(np.int64), W0 - 1)
    q = rng.permutation(N)[:N // 4]; lev[q] = np.exp2(rng.uniform(-9, -3, (len(q), L0)))
    s = rng.permutation(8)[:4]; l[:, s] = W0 - 1 - l[:, s]
    x = body(rng, lev, 0.25, 2.0); l = weave(rng, lev, l, 0.3)
    x[:, :, Q0:Q0 + 5] = 0.0; x[:, :, Q0 + 1] = 0.5; l[:, :, :, Q0:Q0 + 5] = Q0
    for j in range(3): x[:, 48 * j:48 * j + 48, Q0 + 2 + j] = 2.0
    for a in q: late(rng, x[a], l[a])
    return pack(x, l)
def setup_inputs_ends(rng):
    x = np.zeros((N, 128, L0)); l = np.zeros((N, 8, 16, L0), np.int64)
    for a in range(N):
        odd = a % 2; o = 1 + rng.permutation(L0 - 2); n = CAP - 2 if odd else CAP + 1 + int(rng.integers(0, L0 // 8))
        c = rng.choice(np.array([0, H - 1, H - 1]), L0); c[o[:n]] = rng.choice(np.array([H, H, 128]), n)
        c[0] = 128 * odd; c[L0 - 1] = 128 * odd
        x[a] = 2.0 * (np.argsort(rng.random((128, L0)), axis=0) < c)
        e = np.where(rng.random((8, 16, L0)) < 0.5, 0, W0 - 1)
        k = np.where(rng.random((8, 16, L0)) < 0.72, e, rng.integers(0, W0, (8, 16, L0)))
        i, j = two(rng, L0); np.put_along_axis(k, i, 0, 1); np.put_along_axis(k, j, W0 - 1, 1)
        same = (rng.random((8, 1, L0)) < 0.15) & (c < H)
        l[a] = np.where(same, e[:, :1], k)
    return pack(x, l)
def setup_inputs_corners(rng):
    nc = L0 // 8; x = np.zeros((N, 128, L0)); l = rng.integers(0, W0, (N, 8, 16, L0)); me = G + np.arange(L0)
    want = np.array([CAP, CAP + 1, L0 - nc, CAP - 1, 0, 1, CAP, L0 - nc])[:N][rng.permutation(N)]
    for a in range(N):
        o = rng.permutation(L0)
        if want[a] == L0 - nc: o = np.concatenate([o[o >= 256], o[o < 256]])
        cold = o[:nc]; hot = o[nc:nc + int(want[a])]
        c = rng.choice(np.array([0, 1, H - 1, H - 1]), L0); c[hot] = rng.choice(np.array([H, H, H + 1, 127, 128]), len(hot))
        hi = np.where(rng.random((128, L0)) < 0.25, 2.0, rng.uniform(1.5, 2.0, (128, L0)))
        lo = np.where(rng.random((128, L0)) < 0.25, 0.5, rng.uniform(0.0625, 0.5, (128, L0)))
        x[a] = np.where(np.argsort(rng.random((128, L0)), axis=0) < c, hi, lo)
        x[a][:, cold] = rng.uniform(0.015625, 0.03125, (128, nc))
        kd = rng.permutation(8)
        l[a, kd[1]] = me
        l[a, kd[2]] = rng.choice(np.array([G, G + L0 - 1]), (16, L0))
        l[a, kd[3]] = rng.choice(np.array([0, G - 1]), (16, L0))
        l[a, kd[4]] = rng.integers(0, W0, L0)
        l[a, kd[5]] = np.maximum(me - 1, G)
        l[a, kd[6]] = G + (np.arange(L0) ^ 1)
        l[a, kd[7]] = int(rng.integers(0, W0))
        i, j = two(rng, L0); np.put_along_axis(l[a], i, G + cold[rng.integers(0, nc, (8, 1, L0))], 1)
        l[a][:, :, cold] = G + cold[rng.integers(0, nc, (8, 16, nc))]
    return pack(x, l)
def setup_inputs_close(rng):
    nq = L0 // 8; nf = 24; base = rng.uniform(0.25, 1.9, (nf, 128)).astype(np.float32); fam = rng.integers(0, nf, (N, L0))
    base[:, 96:] = base[:, 96:] * np.float32(0.03125)
    v = np.ascontiguousarray(base[fam].transpose(0, 2, 1)).reshape(N, 8, 16, L0)
    hit = np.arange(16)[None, None, :, None] == rng.integers(0, 16, (N, 8, 1, L0)); kind = rng.integers(0, 3, (N, 8, 1, L0))
    v = np.where(hit & (kind == 1), np.nextafter(v, np.float32(4)), np.where(hit & (kind == 2), np.nextafter(v, np.float32(0)), v))
    x = np.ascontiguousarray(v).reshape(N, 128, L0); l = rng.integers(0, W0, (N, 8, 16, L0)); unit = 2.0 ** -24
    for a in range(N):
        pf = places(fam, a); o = np.argsort(pf, kind="stable"); first = np.searchsorted(pf[o], np.arange(nf)); cnt = np.bincount(pf, minlength=nf)
        mates = o[first[fam[a]] + (rng.random((8, 16, L0)) * cnt[fam[a]]).astype(np.int64)]
        l[a] = np.where(rng.random((8, 16, L0)) < 0.75, mates, l[a])
        rk = np.argsort(rng.random((128, nq)), axis=0)
        x[a, :, :nq] = np.where(rk < H - 1, 1.5, np.where(rk == H - 1, 0.5 + unit * rng.integers(0, 4, nq), np.where(rk < H + 3, 0.5 + unit * rng.integers(0, 2, (128, nq)), 0.25)))
        x[a, :, nq:nq + 8] = 2.0; x[a, :, nq + 8:nq + 16] = 0.0
        i, j = two(rng, nq); k = l[a][:, :, :nq].copy()
        np.put_along_axis(k, i, G + nq + rng.integers(0, 8, (8, 1, nq)), 1); np.put_along_axis(k, j, G + nq + 8 + rng.integers(0, 8, (8, 1, nq)), 1)
        l[a][:, :, :nq] = k
        c = nq + 16 + np.arange(48); xe, ze = knife(rng, 12); rk = np.argsort(rng.random((128, 48)), axis=0)
        x[a][:, c] = np.where(rk < H - 1, 1.5, np.where(rk == H - 1, xe, 0.25))
        x[a][:, c + 48] = np.where(rk == H - 1, ze, rng.uniform(0.1, 0.6, (128, 48)))
        i, j = two(rng, 48); k = np.where(rng.random((8, 16, 48)) < 0.5, G + nq + rng.integers(0, 8, (8, 16, 48)), G + c + 48)
        np.put_along_axis(k, i, G + nq + rng.integers(0, 8, (8, 1, 48)), 1); np.put_along_axis(k, j, G + c[None, None, :] + 48, 1)
        l[a][:, :, c] = k
    return pack(x, l)
def setup_inputs_calm(rng):
    lev = rng.uniform(0.1, 0.35, (N, L0)); x = lev[:, None, :] * rng.uniform(0.9, 1.1, (N, 128, L0)); n = rng.permutation(N) % 4
    for a in range(N):
        x[a][:, rng.permutation(L0)[:int(n[a])]] = 2.0
    return pack(x, rng.integers(0, W0, (N, 8, 16, L0)))
def check_inputs(d):
    bad = []; x = np.asarray(d["x0"]).astype(np.float64)
    if not (np.min(x) >= 0 and np.max(x) <= 2): bad.append("range of x0")
    if np.any((x > 0) & (x < 0.0009765625)): bad.append("small numbers of x0")
    if np.min(d["nb"]) < 0 or np.max(d["nb"]) > W0 - 1: bad.append("range of nb")
    return bad
def reference(x0, nb):
    F = np.float32
    x = np.zeros((N, 128, LM), np.float32); x[:, :, :L0] = x0
    l = np.zeros((N, 8, 16, LM), np.int64); l[:, :, :, :L0] = nb.reshape(N, 8, 16, L0)
    live = [L0] * N
    for t in range(RO):
        old = np.array(x)
        for a in range(N):
            n = live[a]; own = old[a, :, :n]
            w = np.concatenate([old[(a + o) % N, :, :B] for o in OFF] + [own], axis=1)
            xn = np.zeros((128, n), np.float32); mv = np.zeros((8, 16, n), np.int64)
            for g in range(8):
                c = own[16 * g:16 * g + 16]; k = np.array(l[a, g, :, :n])
                p = np.take(w[16 * g:16 * g + 16], k, axis=1)
                y = np.maximum.reduce(p, axis=1); z = np.minimum.reduce(p, axis=1)
                xn[16 * g:16 * g + 16] = np.minimum(np.maximum((c + F(0.25) * y) - F(0.75) * (z * c), F(0)), F(2))
                none = np.logical_not(np.any(p > c[:, None, :], axis=0))
                mv[g] = np.where(none & (k >= G), np.take_along_axis(k, np.maximum(k - G, 0), 1), k)
            ready = (np.add.reduce((xn > 1).astype(np.int64), axis=0) >= H).astype(np.int64)
            m = np.flatnonzero((ready == 1) & (np.add.accumulate(ready) <= CAP)); ch = n + np.arange(len(m))
            xn[:, m] = xn[:, m] * F(0.5)
            x[a, :, :n] = xn; x[a][:, ch] = xn[:, m]
            l[a, :, :, :n] = mv; l[a][:, :, ch] = mv[:, :, m]
            l[a][:, t, ch] = G + m; l[a][:, t, m] = G + ch
            live[a] = n + len(m)
    return {"yx": x, "yn": l.reshape(N, 128, LM).astype(np.float32)}

@@ -1,0 +1,545 @@
+from concourse.bass import DstId, RemoteDMATransfer
+from concourse.mybir import AluOpType, ActivationFunctionType
+
+L0N, CAP, RO, GH, LM = 640, 96, 4, 512, 1024
+BASE = [L0N + CAP * t for t in range(RO + 1)]
+PL = GH + LM
+BIG = 4096
+PAR = {
+    "nch": [[128, 256, 256], [128, 224, 192, 192], [128, 256, 256, 192], [160, 256, 224, 144, 144]],
+    "la": [352, 384, 416, 512],
+    "g2": [([128, 96, 256, 96], [], [32], [32]), ([208, 208], [], [64], [256]),
+           ([240, 240], [], [64], [144, 144]), ([256, 256], [], [64], [176, 176])],
+    "g2s": 1, "g2v": 1,
+    "g0v": True,
+    "fill": [3, 2, 3, 3, 1, 1],
+    "diag": 6, "fl_s": True, "off_s": True, "b_s": False, "x1_s": True, "xk": 6,
+}
+
+SCRATCH = {
+    "W0": ("sbuf", [128, PL], "float32"), "W1": ("sbuf", [128, PL], "float32"),
+    "W2": ("sbuf", [128, PL], "float32"), "W3": ("sbuf", [128, PL], "float32"),
+    "La": ("sbuf", [128, PL], "float32"), "Lc": ("sbuf", [128, PL], "float32"),
+    "Lb": ("sbuf", [128, LM], "float32"),
+    "nbi": ("sbuf", [128, L0N], "int32"),
+    "off0": ("sbuf", [128, 928], "uint16"), "off1": ("sbuf", [128, 928], "uint16"),
+    "P": ("sbuf", [128, 16 * 928], "float32"),
+    "Q": ("sbuf", [128, 16 * 928], "float16"),
+    "F": ("sbuf", [128, 16 * 512], "bfloat16"),
+    "SX": ("sbuf", [128, 4096], "float32"), "SN": ("sbuf", [128, 4096], "float32"),
+    "m1": ("sbuf", [128, 4096], "bfloat16"), "m2": ("sbuf", [128, 4096], "bfloat16"),
+    "ab": ("sbuf", [128, 928], "float32"), "db": ("sbuf", [128, 928], "float32"),
+    "fl": ("sbuf", [128, LM], "bfloat16"), "rs": ("sbuf", [128, LM], "bfloat16"),
+    "cum": ("sbuf", [128, LM], "bfloat16"), "ones": ("sbuf", [128, LM], "bfloat16"),
+    "Bm": ("sbuf", [128, 2048], "bfloat16"), "Dm": ("sbuf", [128, 2048], "bfloat16"),
+    "I1": ("sbuf", [128, 128], "float32"), "Iq": ("sbuf", [128, 128], "float32"),
+    "Am": ("sbuf", [128, 128], "float32"), "IOT": ("sbuf", [128, LM], "float32"),
+    "ci": ("sbuf", [128, 4], "int32"), "cf": ("sbuf", [128, 8], "float32"),
+    "mk6": ("sbuf", [128, 8], "float32"), "ew2": ("sbuf", [128, 8], "float32"),
+    "sR": ("sbuf", [128, 4], "float32"), "sX": ("sbuf", [128, 4], "float32"),
+    "e2": ("sbuf", [128, CAP], "float32"), "n2": ("sbuf", [128, 8], "float32"),
+    "cc": ("sbuf", [128, 4], "float32"), "acc": ("sbuf", [128, 4], "float32"),
+    "B6": ("sbuf", [128, 8], "float32"),
+    "offm": ("sbuf", [128, 8], "uint16"), "offc": ("sbuf", [128, 8], "uint16"),
+    "Cx": ("sbuf", [128, CAP], "float32"), "RV": ("sbuf", [128, CAP], "float32"),
+    "LS": ("sbuf", [128, CAP], "float32"), "X1": ("sbuf", [128, CAP], "float32"),
+    "CL": ("sbuf", [128, CAP], "float32"),
+    "xp": ("psum", [128, 1024], "float32"), "cq": ("psum", [128, 1024], "float32"),
+    "xq": ("psum", [128, 1024], "float32"), "vo": ("psum", [128, 1024], "float32"),
+}
+PSUM = ("xp", "cq", "xq", "vo")
+NDMA = 12
+SEMAPHORES = (["cv", "cs", "cp", "cg"] + ["d%d" % i for i in range(NDMA)]
+              + ["arr%d" % t for t in range(RO)] + ["out%d" % t for t in range(RO)])
+
+
+def _plan(g, core, T, topo, rank):
+    A = AluOpType
+    AF = ActivationFunctionType
+    V, S, PE = g.vector, g.scalar, g.tensor
+    LA = PAR["la"]
+    ops = []
+    ndma = [0]
+
+    def ap(name, a, b, step=1):
+        v = T[name][:, a:b] if step == 1 else T[name][:, a:b:step]
+        return (v, [(name, a, b)])
+
+    def ind(win, off):
+        return (win[0].indirect(off[0]), win[1] + off[1])
+
+    def add(q, fn, r, w, tok=None):
+        ops.append({"q": q, "fn": fn, "r": r, "w": w, "tok": tok})
+
+    def col(x):
+        return (x[0], x[1]) if isinstance(x, tuple) else (x, [])
+
+    def tt(out, a, b, op):
+        add("v", lambda: V.tensor_tensor(out[0], a[0], b[0], op), a[1] + b[1], out[1])
+
+    def ts(out, a, s1, op0, s2=None, op1=None):
+        c1, r1 = col(s1)
+        c2, r2 = col(s2)
+        if op1 is None:
+            add("v", lambda: V.tensor_scalar(out[0], a[0], c1, None, op0), a[1] + r1, out[1])
+        else:
+            add("v", lambda: V.tensor_scalar(out[0], a[0], c1, c2, op0, op1), a[1] + r1 + r2, out[1])
+
+    def cp(out, a):
+        add("v", lambda: V.tensor_copy(out[0], a[0]), a[1] + out[1][1:], out[1][:1])
+
+    def scan(out, d0, d1, op0, op1):
+        add("v", lambda: V.tensor_tensor_scan(out[0], d0[0], d1[0], 0.0, op0, op1), d0[1] + d1[1], out[1])
+
+    def mset(out, c):
+        add("v", lambda: V.memset(out[0], c), [], out[1])
+
+    def act(out, a, f, bias=0.0, scale=1.0, acc=None):
+        cb, rb = col(bias)
+        cs, rc = col(scale)
+        if acc is None:
+            add("s", lambda: S.activation(out[0], a[0], f, bias=cb, scale=cs), a[1] + rb + rc, out[1])
+        else:
+            add("s", lambda: S.activation(out[0], a[0], f, bias=cb, scale=cs, accum_out=acc[0]),
+                a[1] + rb + rc, out[1] + acc[1])
+
+    def mm(out, l, r, start, stop):
+        add("p", lambda: PE.matmul(out[0], l[0], r[0], start, stop), l[1] + r[1], out[1])
+
+    def iota(out, pat, base, cm):
+        if out[1][0][0] == "ci":
+            add("g", lambda: g.iota(out[0], pat, base, cm), [], out[1])
+        else:
+            add("g", lambda: g.iota(out[0], pat, base, cm, allow_small_or_imprecise_dtypes=True), [], out[1])
+
+    def sel(out, a, pat, op, base, cm):
+        add("g", lambda: g.affine_select(out[0], a[0], pat, op, 0.0, base, cm), a[1], out[1])
+
+    def dma(q, out, a):
+        name = "d%d" % ndma[0]
+        ndma[0] += 1
+        eng = g.sync if q == "y" else S
+        add(q, lambda: eng.dma_start(out[0], a[0]).then_inc(T.sem[name], 16), a[1], out[1], (name, 16))
+
+    def hbm(name, a, b):
+        return (T[name][:, a:b], [])
+
+    Wn = ["W0", "W1", "W2", "W3", "W0"]
+    Ln = ["La", "Lc", "La", "Lc", "La"]
+    On = ["off0", "off1", "off0", "off1"]
+    N = len(T.cores)
+    dsts = [T.cores[(rank + 1) % N], T.cores[(rank + 4) % N]]
+    order = sorted(range(2), key=lambda d: len(topo.engines(core, dsts[d])))
+    masks = [0, 0]
+    used = []
+    for d in order:
+        free = [e for e in topo.engines(core, dsts[d]) if e not in used]
+        spare = [e for e in free if e not in topo.engines(core, dsts[order[0]])]
+        take = (spare[::2] if len(spare) >= 8 else (free[::2] if len(free) >= 8 else free))[:4]
+        used += take
+        masks[d] = sum(1 << e for e in take)
+
+    def send(t):
+        src = ap(Wn[t], GH, GH + 256)
+
+        def fn():
+            tr = []
+            for d in range(2):
+                rid, pid = topo.addr(dsts[d], core)
+                tr.append(RemoteDMATransfer(dst_ids=[DstId(rid=rid, pnc=pid)], dma_engine_mask=masks[d],
+                                            remote_sem=T.sem["arr%d" % t], src=src[0],
+                                            dst=T[Wn[t]][:, 256 * d:256 * d + 256]))
+            g.remote_dma_fused(tr, local_sem=T.sem["out%d" % t])
+        add("g", fn, src[1], [], ("out%d" % t, 8))
+        add("r", None, [], [(Wn[t], 0, GH)], ("arr%d" % t, 8))
+
+    def bounds(sizes, a=0):
+        out = []
+        for s in sizes:
+            out.append((a, a + s))
+            a += s
+        return out
+
+    nch = [bounds(PAR["nch"][t]) for t in range(RO)]
+    split = [nch[t][1][1] for t in range(RO)]
+    g2 = [[bounds(PAR["g2"][t][i], sum(sum(x) for x in PAR["g2"][t][:i])) for i in range(4)] for t in range(RO)]
+
+    def pcol(name, cut, a, b):
+        return ap(name, a, b) if b <= cut else ap(name, 512 + a - cut, 512 + b - cut)
+
+    def own(name, a, b):
+        return ap(name, GH + a, GH + b)
+
+    def gather(t, c, vec=False):
+        a, b = nch[t][c]
+        src = ind(ap(Wn[t], 0, GH + BASE[t]), ap(On[t], a, b))
+        if vec:
+            ts(ap("P", 16 * a, 16 * b), src, 0.25, A.mult)
+        else:
+            act(ap("P", 16 * a, 16 * b), src, AF.Copy, scale=0.25)
+
+    def gather2(t, a, b, vec=False):
+        src = ind(ap(Ln[t], 0, GH + BASE[t]), ap(On[t], a, b))
+        if vec:
+            ts(ap("Q", 16 * a, 16 * b), src, -1.0 / BIG, A.mult)
+        else:
+            act(ap("Q", 16 * a, 16 * b), src, AF.Copy, scale=-1.0 / BIG)
+
+    def copy_x(t, name, cut, ident):
+        for a, b in ((0, cut), (cut, BASE[t])):
+            mm(pcol(name, cut, a, b), ap(ident, 0, 128), own(Wn[t], a, b), True, True)
+
+    def s_min(t, c):
+        a, b = nch[t][c]
+        n = 16 * (b - a)
+        scan(ap("SN", 0, n), ap("m2", 0, n), ap("P", 16 * a, 16 * b), A.add, A.min)
+
+    def s_max(t, c):
+        a, b = nch[t][c]
+        n = 16 * (b - a)
+        scan(ap("SX", 0, n), ap("m1", 0, n), ap("P", 16 * a, 16 * b), A.mult, A.max)
+
+    def u_a(t, c):
+        a, b = nch[t][c]
+        tt(ap("ab", a, b), ap("SN", 15, 16 * (b - a), 16), pcol("xp", split[t], a, b), A.mult)
+
+    def u_s(t, c):
+        a, b = nch[t][c]
+        x = pcol("xp", split[t], a, b)
+        tt(x, ap("SX", 15, 16 * (b - a), 16), x, A.add)
+
+    def u_b(a, b, on_s):
+        if on_s:
+            act(ap("ab", a, b), ap("ab", a, b), AF.Copy, scale=3.0)
+        else:
+            ts(ap("ab", a, b), ap("ab", a, b), 3.0, A.mult)
+
+    def u_d(t, a, b):
+        tt(ap("db", a, b), pcol("xp", split[t], a, b), ap("ab", a, b), A.subtract)
+
+    def u_flag(t, a, b):
+        if PAR["fl_s"]:
+            act(ap("fl", a, b), ap("db", a, b), AF.Sign, bias=-(3.5 + 2.0 ** -22), scale=3.5)
+        else:
+            ts(ap("fl", a, b), ap("db", a, b), 1.0, A.is_gt)
+        mm(pcol("vo", split[t], a, b), ap("ones", 0, 128), ap("fl", a, b), True, True)
+
+    def u_clip(t, a, b):
+        ts(own(Wn[t + 1], a, b), ap("db", a, b), 0.0, A.max, 2.0, A.min)
+
+    def l_cmp(t, a, b, k, start, stop):
+        f = ap("F", 512 * k, 512 * k + b - a)
+        tt(f, ap("P", 16 * a + k, 16 * b, 16), pcol("cq", LA[t], a, b), A.is_gt)
+        mm(pcol("xq", LA[t], a, b), ap("Bm", 128 * k, 128 * k + 128), f, start, stop)
+
+    def l_diag(t, a, b, first, k0=0, k1=16):
+        for k in range(k0, k1):
+            mm(pcol("xq", LA[t], a, b), ap("Dm", 128 * k, 128 * k + 128), ap("Q", 16 * a + k, 16 * b, 16),
+               first and k == 0, False)
+
+    def l_y(t, a, b):
+        tt(ap("db", a, b), pcol("xq", LA[t], a, b), ap("Lb", a, b), A.min)
+
+    def l_abs(t, a, b):
+        act(own(Ln[t + 1], a, b), ap("db", a, b), AF.Abs)
+
+    def l_off(t, a, b):
+        if PAR["off_s"]:
+            act(ap(On[t + 1], a, b), ap("db", a, b), AF.Abs)
+        else:
+            cp(ap(On[t + 1], a, b), own(Ln[t + 1], a, b))
+
+    dma("y", own("W0", 0, 256), hbm("x0", 0, 256))
+    dma("s", ap("nbi", 0, L0N), hbm("nb", 0, L0N))
+    dma("y", own("W0", 256, L0N), hbm("x0", 256, L0N))
+    iota(ap("La", 0, GH), [[1, GH]], 0, 0)
+    iota(ap("ci", 0, 1), [[0, 1]], 0, 1)
+    mset(ap("m1", 0, 2048), 1.0)
+    mset(ap("m2", 0, 2048), 0.0)
+    mset(ap("m1", 0, 2048, 16), 0.0)
+    mset(ap("m2", 0, 2048, 16), 1.0)
+    mset(ap("n2", 0, 1), 2.0 * (GH + L0N))
+    mset(ap("rs", L0N, LM), -1.0)
+    send(0)
+    dma("y", ap("m1", 2048, 4096), ap("m1", 0, 2048))
+    dma("y", ap("m2", 2048, 4096), ap("m2", 0, 2048))
+    cp(ap("off0", 0, L0N), ap("nbi", 0, L0N))
+    cp(own("La", 0, L0N), ap("nbi", 0, L0N))
+    early = PAR["g2s"] + PAR["g2v"]
+    for a, b in g2[0][0][:PAR["g2s"]]:
+        gather2(0, a, b)
+    iota(ap("I1", 0, 128), [[0, 128]], 1, 0)
+    sel(ap("I1", 0, 128), ap("I1", 0, 128), [[-1, 128]], A.is_equal, 0, 1)
+    iota(ap("Am", 0, 128), [[0, 8], [1, 16]], 0, 0)
+    iota(ap("mk6", 0, 8), [[1, 8]], 0, 0)
+    iota(ap("ew2", 0, 8), [[32, 8]], -2 * (GH + L0N), 0)
+    iota(ap("cf", 4, 5), [[0, 1]], 1, 2)
+    iota(ap("e2", 0, CAP), [[2, CAP]], 0, 0)
+    ts(ap("ci", 1, 2), ap("ci", 0, 1), 15, A.bitwise_and)
+    ts(ap("ci", 2, 3), ap("ci", 0, 1), 4, A.logical_shift_right)
+    cp(ap("cf", 0, 3), ap("ci", 0, 3))
+    copy_x(0, "xp", split[0], "I1")
+    ts(ap("cf", 3, 4), ap("cf", 1, 2), 2.0, A.mult)
+    ts(ap("Iq", 0, 128), ap("I1", 0, 128), 0.25, A.mult)
+    ts(ap("sX", 0, 4), ap("mk6", 0, 4), ap("cf", 1, 2), A.is_equal)
+    ts(ap("Am", 0, 128), ap("Am", 0, 128), ap("cf", 1, 2), A.is_equal)
+    ts(ap("mk6", 0, 8), ap("mk6", 0, 8), ap("cf", 2, 3), A.is_equal)
+    ts(ap("sR", 0, 4), ap("sX", 0, 4), -2.5, A.mult, 2.0, A.add)
+    ts(ap("ew2", 0, 8), ap("ew2", 0, 8), ap("cf", 3, 4), A.add)
+    ts(ap("sX", 0, 4), ap("sX", 0, 4), -3.0, A.mult, 4.0, A.add)
+    for a, b in g2[0][0][PAR["g2s"]:early]:
+        gather2(0, a, b, True)
+    gather(0, 0, PAR["g0v"])
+    gather(0, 1)
+    iota(ap("ones", 0, LM), [[0, LM]], 1, 0)
+    iota(own("La", L0N, LM), [[1, LM - L0N]], GH + L0N, 0)
+    dma("y", ap("Lb", 0, BASE[1]), own("La", 0, BASE[1]))
+    for t in range(RO):
+        iota(own(Wn[t + 1], BASE[t], BASE[t + 1]), [[0, CAP]], 0, 0)
+    bm, dm = ap("Bm", 0, 2048), ap("Dm", 0, 2048)
+    iota(bm, [[0, 2048]], BIG, 0)
+    sel(bm, bm, [[-1, 16], [0, 8], [1, 16]], A.is_equal, 0, 0)
+    sel(dm, bm, [[0, 16], [-1, 128]], A.is_equal, 0, 1)
+    sel(bm, bm, [[0, 16], [-16, 8], [0, 16]], A.is_ge, 0, 1)
+    sel(bm, bm, [[0, 16], [16, 8], [0, 16]], A.is_ge, 15, -1)
+    iota(ap("IOT", 0, LM), [[1, LM]], GH, 0)
+    iota(ap("Lc", 0, GH), [[1, GH]], 0, 0)
+    iota(own("Lc", L0N, LM), [[1, LM - L0N]], GH + L0N, 0)
+
+    offm, offc = ap("offm", 0, 6), ap("offc", 0, 6)
+    fills = PAR["fill"]
+    vote = 1.0 if PAR["fl_s"] else -63.5
+
+    def child_gather(t):
+        tt(ap("CL", 0, CAP), ind(own(Ln[t + 1], 0, BASE[t + 1]), offm), ap("X1", 0, CAP), A.min)
+
+    def child_put(t):
+        if t == 0:
+            cp(own(Ln[1], L0N, BASE[1]), ap("CL", 0, CAP))
+        else:
+            cp(ind(own(Ln[t + 1], L0N, BASE[t + 1]), offc), ap("CL", 0, CAP))
+
+    for t in range(RO):
+        n, nn, sp, la = BASE[t], BASE[t + 1], split[t], LA[t]
+        last = t == RO - 1
+        W1 = Wn[t + 1]
+        nc = len(nch[t])
+        n2 = ap("n2", t, t + 1)
+        s_min(t, 0)
+        if t > 0:
+            l_y(t - 1, LA[t - 1], BASE[t - 1])
+            if PAR["off_s"]:
+                l_off(t - 1, LA[t - 1], L0N)
+            l_abs(t - 1, LA[t - 1], BASE[t - 1])
+        s_max(t, 0)
+        u_a(t, 0)
+        if t > 0 and not PAR["off_s"]:
+            l_off(t - 1, LA[t - 1], L0N)
+        ts(ap("cc", 0, 1), ap("cf", 4, 5), n2, A.add, float(-1 - nn - 2 * GH), A.add)
+        u_s(t, 0)
+        gather(t, 2)
+        copy_x(t, "cq", la, "Iq")
+        s_min(t, 1)
+        if t > 0:
+            child_gather(t - 1)
+        ts(ap("RV", 0, CAP), ap("e2", 0, CAP), n2, A.add, ap("sR", t, t + 1), A.mult)
+        if t > 0:
+            child_put(t - 1)
+        u_a(t, 1)
+        if t > 0:
+            cp(ap(On[t], L0N, n), own(Ln[t], L0N, n))
+            dma("y", ap("Lb", 0, nn), own(Ln[t], 0, nn))
+        s_max(t, 1)
+        if t > 0:
+            ts(offc, ap("ew2", 0, 6), n2, A.add, 0.5, A.mult)
+        u_s(t, 1)
+        for c in range(3, nc):
+            gather(t, c)
+        u_b(0, sp, True)
+        for a, b in g2[t][0][(early if t == 0 else 0):]:
+            gather2(t, a, b)
+        kk = [0]
+
+        def fill(cnt):
+            for _ in range(cnt):
+                if kk[0] < 16:
+                    l_cmp(t, 0, la, kk[0], kk[0] == 0 and PAR["diag"] == 0, kk[0] == 15)
+                    kk[0] += 1
+        for c in range(2, nc):
+            s_min(t, c)
+            if c == nc - 1:
+                u_d(t, 0, sp)
+            s_max(t, c)
+            u_a(t, c)
+            if c == nc - 1:
+                u_clip(t, 0, sp)
+            u_s(t, c)
+        u_flag(t, 0, sp)
+        l_diag(t, 0, la, True, 0, PAR["diag"])
+        u_b(sp, n, PAR["b_s"])
+        act(ap("rs", 0, sp), pcol("vo", sp, 0, sp), AF.Sign, bias=vote)
+        fill(fills[0])
+        u_d(t, sp, n)
+        for a, b in g2[t][1]:
+            gather2(t, a, b)
+        fill(fills[1])
+        u_flag(t, sp, n)
+        u_clip(t, sp, n)
+        act(ap("rs", sp, n), pcol("vo", sp, sp, n), AF.Sign, bias=vote)
+        fill(fills[2])
+        scan(ap("cum", 0, nn), ap("rs", 0, nn), ap("ones", 0, nn), A.add, A.add)
+        for a, b in g2[t][2]:
+            gather2(t, a, b)
+        act(ap("fl", 0, nn), ap("cum", 0, nn), AF.Sign, bias=ap("cf", 4, 5), scale=-1.0, acc=ap("acc", 0, 1))
+        for a, b in g2[t][3]:
+            gather2(t, a, b)
+        fill(fills[3])
+        ts(ap("B6", 0, 6), ap("mk6", 0, 6), ap("acc", 0, 1), A.mult, ap("cc", 0, 1), A.min)
+        mm(ap("vo", 496, 502), ap("Am", 0, 128), ap("B6", 0, 6), True, True)
+        l_diag(t, 0, la, False, PAR["diag"], 16)
+        fill(fills[4])
+        ts(offm, ap("vo", 496, 502), 0.5, A.mult, nn / 2.0, A.add)
+        fill(fills[5])
+        ts(ap("Cx", 0, CAP), ind(own(W1, 0, nn), offm), 0.5, A.mult)
+        tt(ap("LS", 0, CAP), ind(own(Ln[t], 0, nn), offm), ap("RV", 0, CAP), A.min)
+        cp(ind(own(W1, 0, nn), offm), ap("Cx", 0, CAP))
+        cp(ind(ap("Lb", 0, nn), offm), ap("LS", 0, CAP))
+        if t == 0:
+            cp(own(W1, L0N, nn), ap("Cx", 0, CAP))
+        else:
+            cp(ind(own(W1, L0N, nn), offc), ap("Cx", 0, CAP))
+        if last:
+            dma("y", hbm("yx", 0, LM), own(W1, 0, LM))
+        else:
+            send(t + 1)
+        ts(ap("n2", t + 1, t + 2), ap("cum", n - 1, n), 2.0 * CAP, A.min, n2, A.add)
+        fill(16)
+        l_cmp(t, la, n, 0, True, False)
+        if last:
+            ts(ap("xp", 0, LM - L0N), ap("IOT", L0N, LM), 2.0, A.mult, ap("n2", RO, RO + 1), A.is_lt)
+        l_y(t, 0, la)
+        if not last and PAR["off_s"]:
+            l_off(t, 0, la)
+        l_abs(t, 0, la)
+        if PAR["x1_s"]:
+            act(ap("X1", 0, CAP), ind(ap("IOT", 0, nn), offm), AF.Copy, scale=ap("sX", t, t + 1))
+        else:
+            ts(ap("X1", 0, CAP), ind(ap("IOT", 0, nn), offm), ap("sX", t, t + 1), A.mult)
+        if last:
+            dma("y", hbm("yn", 0, la), own(Ln[t + 1], 0, la))
+        l_diag(t, la, n, False)
+        l_cmp(t, la, n, 1, False, False)
+        if not last:
+            if not PAR["off_s"]:
+                l_off(t, 0, la)
+            gather(t + 1, 0)
+            gather(t + 1, 1)
+        for k in range(2, 16):
+            l_cmp(t, la, n, k, False, k == 15)
+            if k == PAR["xk"] and not last:
+                copy_x(t + 1, "xp", split[t + 1], "I1")
+    l_y(RO - 1, LA[RO - 1], BASE[RO - 1])
+    l_abs(RO - 1, LA[RO - 1], BASE[RO - 1])
+    child_gather(RO - 1)
+    child_put(RO - 1)
+    tail = own(Ln[RO], L0N, LM)
+    tt(tail, tail, ap("xp", 0, LM - L0N), A.mult)
+    dma("y", hbm("yn", LA[RO - 1], LM), own(Ln[RO], LA[RO - 1], LM))
+    return ops
+
+
+def _meet(x, y):
+    return x[0] == y[0] and x[1] < y[2] and y[1] < x[2]
+
+
+def _banks(regs):
+    out = []
+    for name, a, b in regs:
+        if name in PSUM:
+            out.append((name, 512 * (a // 512), 512 * ((b - 1) // 512 + 1)))
+    return out
+
+
+def _emit(g, T, ops):
+    queue = {"v": g.vector, "s": g.scalar, "p": g.tensor, "g": g, "y": g.sync}
+    semq = {"v": "cv", "s": "cs", "p": "cp", "g": "cg"}
+    hist = {}
+    deps = []
+    for i, o in enumerate(ops):
+        bk = _banks(o["r"] + o["w"])
+        d = set()
+        for kind, regs in (("r", o["r"]), ("w", o["w"]), ("b", bk)):
+            for x in regs:
+                for j, kj, y in hist.get(x[0], []):
+                    p = ops[j]
+                    same = p["q"] == o["q"] and p["tok"] is None and o["tok"] is None
+                    if kind == "b" or kj == "b":
+                        hit = kind == kj and not same
+                    elif kind == "r" and kj == "r":
+                        hit = False
+                    else:
+                        hit = not (same and o["q"] == "p")
+                    if hit and _meet(x, y):
+                        d.add(j)
+        if o["q"] == "r":
+            d = set()
+        for kind, regs in (("r", o["r"]), ("w", o["w"]), ("b", bk)):
+            for x in regs:
+                hist.setdefault(x[0], []).append((i, kind, x))
+        top = {}
+        keep = []
+        for j in sorted(d):
+            if ops[j]["tok"] is None:
+                top[ops[j]["q"]] = j
+            else:
+                keep.append(j)
+        deps.append(keep + sorted(top.values()))
+    known = {q: {} for q in queue}
+    seen = []
+    waits = []
+    needed = set()
+    for i, o in enumerate(ops):
+        w = []
+        if o["q"] != "r":
+            kn = known[o["q"]]
+            for j in sorted(deps[i], reverse=True):
+                key = ops[j]["q"] if ops[j]["tok"] is None else ops[j]["tok"][0]
+                if kn.get(key, -1) >= j:
+                    continue
+                w.append(j)
+                needed.add(j)
+                kn[key] = j
+                for k2, v2 in seen[j].items():
+                    if kn.get(k2, -1) < v2:
+                        kn[k2] = v2
+            seen.append(dict(kn))
+        else:
+            seen.append({})
+        waits.append(w)
+    count = {q: 0 for q in semq}
+    token = {}
+    for i, o in enumerate(ops):
+        if o["q"] == "r":
+            token[i] = o["tok"]
+            continue
+        for j in waits[i]:
+            queue[o["q"]].wait_ge(T.sem[token[j][0]], token[j][1])
+        if o["tok"] is not None:
+            o["fn"]()
+            token[i] = o["tok"]
+        else:
+            ins = o["fn"]()
+            if i in needed:
+                count[o["q"]] += 1
+                token[i] = (semq[o["q"]], count[o["q"]])
+                ins.then_inc(T.sem[semq[o["q"]]], 1)
+    for i, o in enumerate(ops):
+        if o["tok"] is not None and i not in needed:
+            queue["g" if o["q"] == "g" else "y"].wait_ge(T.sem[o["tok"][0]], o["tok"][1])
+
+
+def rank_program(g, core, T, topo):
+    rank = T.rank_of(core)
+    if rank is None:
+        return
+    _emit(g, T, _plan(g, core, T, topo, rank))

@@ -5,16 +5,23 @@ L0N, CAP, RO, GH, LM = 640, 96, 4, 512, 1024
 BASE = [L0N + CAP * t for t in range(RO + 1)]
 PL = GH + LM
 BIG = 4096
+MM = 384
+PAD = 16
 PAR = {
-    "nch": [[128, 256, 256], [128, 224, 192, 192], [128, 256, 256, 192], [160, 256, 224, 144, 144]],
-    "la": [352, 384, 416, 512],
-    "g2": [([128, 96, 256, 96], [], [32], [32]), ([208, 208], [], [64], [256]),
-           ([240, 240], [], [64], [144, 144]), ([256, 256], [], [64], [176, 176])],
-    "g2s": 1, "g2v": 1,
-    "g0v": True,
-    "fill": [3, 2, 3, 3, 1, 1],
-    "diag": 6, "fl_s": True, "off_s": True, "b_s": False, "x1_s": True, "xk": 6,
+    "blocks": [256, 128],
+    "nblk": [1, 1, 1, 1],
+    "nch": [[128, 128, 128], [128, 96, 128, 128], [160, 64, 192, 160], [160, 96, 256, 160]],
+    "nv": [1, 1, 1, 1],
+    "ncut": [1, 2, 2, 2],
+    "split": False, "feng": 16, "heng": 8,
+    "q": [[0, 0, 32, 32, 0, 0, 128], [128, 0, 32, 64, 128, 128, 64], [128, 0, 32, 64, 128, 192, 64],
+          [128, 0, 32, 64, 128, 256, 64]],
+    "fv": [128, 128, 128, 128], "fa": [[4, 4], [4, 2], [4, 2], [4, 2]],
+    "qs0": [128, 128], "qv0": [128],
+    "fill": [2, 2, 2, 2, 3, 3, 1, 1, 2, 3],
+    "xk": 4, "b_last_v": True,
 }
+PAR.update({"nch": [[128, 192, 64], [48, 80, 224, 128], [96, 96, 176, 208], [96, 160, 160, 256]], "split": True, "q": [[48, 16, 16, 64, 0, 0, 128], [160, 64, 32, 48, 112, 128, 80], [240, 112, 32, 0, 128, 192, 32], [208, 96, 48, 64, 144, 256, 16]], "fv": [128, 96, 128, 96], "fa": [[7, 6], [6, 6], [5, 7], [1, 4]], "qs0": [128, 128], "qv0": [96], "fill": [2, 5, 1, 7, 1, 0, 4, 1, 5, 3], "xk": 0})
 
 SCRATCH = {
     "W0": ("sbuf", [128, PL], "float32"), "W1": ("sbuf", [128, PL], "float32"),
@@ -28,13 +35,16 @@ SCRATCH = {
     "F": ("sbuf", [128, 16 * 512], "bfloat16"),
     "SX": ("sbuf", [128, 4096], "float32"), "SN": ("sbuf", [128, 4096], "float32"),
     "m1": ("sbuf", [128, 4096], "bfloat16"), "m2": ("sbuf", [128, 4096], "bfloat16"),
-    "ab": ("sbuf", [128, 928], "float32"), "db": ("sbuf", [128, 928], "float32"),
+    "ab": ("sbuf", [128, 928], "float32"), "db": ("sbuf", [128, PAD + 928], "float32"),
+    "TT": ("sbuf", [128, 2 * MM + 32], "float32"), "lst": ("sbuf", [128, MM // 16], "uint16"),
+    "lsf": ("sbuf", [128, MM // 16], "float32"),
+    "Y": ("sbuf", [128, MM], "float32"), "Z": ("sbuf", [128, MM], "float32"),
     "fl": ("sbuf", [128, LM], "bfloat16"), "rs": ("sbuf", [128, LM], "bfloat16"),
     "cum": ("sbuf", [128, LM], "bfloat16"), "ones": ("sbuf", [128, LM], "bfloat16"),
-    "Bm": ("sbuf", [128, 2048], "bfloat16"), "Dm": ("sbuf", [128, 2048], "bfloat16"),
+    "Bm": ("sbuf", [128, 144], "bfloat16"), "Dm": ("sbuf", [128, 2048], "bfloat16"),
     "I1": ("sbuf", [128, 128], "float32"), "Iq": ("sbuf", [128, 128], "float32"),
-    "Am": ("sbuf", [128, 128], "float32"), "IOT": ("sbuf", [128, LM], "float32"),
-    "ci": ("sbuf", [128, 4], "int32"), "cf": ("sbuf", [128, 8], "float32"),
+    "Am": ("sbuf", [128, 144], "float32"), "IOT": ("sbuf", [128, LM], "float32"),
+    "ci": ("sbuf", [128, 8], "int32"), "cf": ("sbuf", [128, 12], "float32"),
     "mk6": ("sbuf", [128, 8], "float32"), "ew2": ("sbuf", [128, 8], "float32"),
     "sR": ("sbuf", [128, 4], "float32"), "sX": ("sbuf", [128, 4], "float32"),
     "e2": ("sbuf", [128, CAP], "float32"), "n2": ("sbuf", [128, 8], "float32"),
@@ -44,20 +54,39 @@ SCRATCH = {
     "Cx": ("sbuf", [128, CAP], "float32"), "RV": ("sbuf", [128, CAP], "float32"),
     "LS": ("sbuf", [128, CAP], "float32"), "X1": ("sbuf", [128, CAP], "float32"),
     "CL": ("sbuf", [128, CAP], "float32"),
-    "xp": ("psum", [128, 1024], "float32"), "cq": ("psum", [128, 1024], "float32"),
-    "xq": ("psum", [128, 1024], "float32"), "vo": ("psum", [128, 1024], "float32"),
+    "xp": ("psum", [128, 1024], "float32"), "xq": ("psum", [128, 1024], "float32"),
+    "sf": ("psum", [128, 512], "float32"), "se": ("psum", [128, 512], "float32"),
+    "sl": ("psum", [128, 512], "float32"), "vo": ("psum", [128, 512], "float32"),
 }
-PSUM = ("xp", "cq", "xq", "vo")
+PSUM = ("xp", "xq", "sf", "se", "sl", "vo")
 NDMA = 12
+FOLDS = [(t, i, w) for t in range(RO) for i in range(2) for w in "ZY"]
 SEMAPHORES = (["cv", "cs", "cp", "cg"] + ["d%d" % i for i in range(NDMA)]
-              + ["arr%d" % t for t in range(RO)] + ["out%d" % t for t in range(RO)])
+              + ["arr%d" % t for t in range(RO)] + ["out%d" % t for t in range(RO)]
+              + ["%s%d%d%s" % (s, t, i, w) for s in ("fo", "fa", "fb") for t, i, w in FOLDS] + ["ho"])
+
+
+def _blocks(t):
+    out, a = [], 0
+    for s in PAR["blocks"][:PAR["nblk"][t]]:
+        out.append((a, a + s))
+        a += s
+    return out
+
+
+def _helpers(core, T, topo):
+    near = [c for c in topo.cores_of(core) if topo.die(c) == topo.die(core) and T.rank_of(c) is None]
+    return {"Z": near[-1], "Y": near[-2]}
+
+
+def _mask(engines):
+    return sum(1 << e for e in engines)
 
 
 def _plan(g, core, T, topo, rank):
     A = AluOpType
     AF = ActivationFunctionType
     V, S, PE = g.vector, g.scalar, g.tensor
-    LA = PAR["la"]
     ops = []
     ndma = [0]
 
@@ -87,6 +116,9 @@ def _plan(g, core, T, topo, rank):
 
     def cp(out, a):
         add("v", lambda: V.tensor_copy(out[0], a[0]), a[1] + out[1][1:], out[1][:1])
+
+    def turn(out, a):
+        add("v", lambda: V.transpose(out[0], a[0]), a[1], out[1])
 
     def scan(out, d0, d1, op0, op1):
         add("v", lambda: V.tensor_tensor_scan(out[0], d0[0], d1[0], 0.0, op0, op1), d0[1] + d1[1], out[1])
@@ -137,7 +169,7 @@ def _plan(g, core, T, topo, rank):
         spare = [e for e in free if e not in topo.engines(core, dsts[order[0]])]
         take = (spare[::2] if len(spare) >= 8 else (free[::2] if len(free) >= 8 else free))[:4]
         used += take
-        masks[d] = sum(1 << e for e in take)
+        masks[d] = _mask(take)
 
     def send(t):
         src = ap(Wn[t], GH, GH + 256)
@@ -153,6 +185,28 @@ def _plan(g, core, T, topo, rank):
         add("g", fn, src[1], [], ("out%d" % t, 8))
         add("r", None, [], [(Wn[t], 0, GH)], ("arr%d" % t, 8))
 
+    helper = _helpers(core, T, topo)
+
+    def fold(t, i):
+        a, b = blk[t][i]
+        n = b - a
+        eng = topo.engines(core, helper["Z"])[:PAR["feng"]]
+        calls = [("Z",), ("Y",)] if PAR["split"] else [("Z", "Y")]
+        for call in calls:
+            def fn(call=call):
+                tr = []
+                for j, w in enumerate(call):
+                    rid, pid = topo.addr(helper[w], core)
+                    tr.append(RemoteDMATransfer(
+                        dst_ids=[DstId(rid=rid, pnc=pid)], dma_engine_mask=_mask(eng[j::len(call)]),
+                        remote_sem=T.sem["fa%d%d%s" % (t, i, w)],
+                        srcs=[T.P[:, 16 * a + k * n:16 * a + (k + 1) * n] for k in range(16)],
+                        dst=T.P[:, MM * t + a:MM * t + b], alu_op=3 if w == "Z" else 2))
+                g.remote_dma_fused(tr, local_sem=T.sem["fo%d%d%s" % (t, i, call[0])])
+            add("g", fn, [("P", 16 * a, 16 * b)], [], ("fo%d%d%s" % (t, i, call[0]), len(eng)))
+        for w in "ZY":
+            add("r", None, [], [(w, a, b)], ("fb%d%d%s" % (t, i, w), PAR["heng"]))
+
     def bounds(sizes, a=0):
         out = []
         for s in sizes:
@@ -160,155 +214,242 @@ def _plan(g, core, T, topo, rank):
             a += s
         return out
 
-    nch = [bounds(PAR["nch"][t]) for t in range(RO)]
-    split = [nch[t][1][1] for t in range(RO)]
-    g2 = [[bounds(PAR["g2"][t][i], sum(sum(x) for x in PAR["g2"][t][:i])) for i in range(4)] for t in range(RO)]
+    blk = [_blocks(t) for t in range(RO)]
+    M = [blk[t][-1][1] for t in range(RO)] + [0]
+    nch = [bounds(PAR["nch"][t], M[t]) for t in range(RO)]
+    cut = [nch[t][PAR["ncut"][t] - 1][1] for t in range(RO)]
+    late = [nch[t][-1][0] for t in range(RO)]
+    rng = [[(0, M[t]), (M[t], cut[t]), (cut[t], BASE[t])] for t in range(RO)]
+    for t in range(RO):
+        assert nch[t][-1][1] == BASE[t] and cut[t] <= 512 and BASE[t] - cut[t] <= 512 and late[t] - M[t] <= 512
 
-    def pcol(name, cut, a, b):
-        return ap(name, a, b) if b <= cut else ap(name, 512 + a - cut, 512 + b - cut)
+    def xcol(t, a, b):
+        return ap("xp", a, b) if b <= cut[t] else ap("xp", 512 + a - cut[t], 512 + b - cut[t])
+
+    def scol(t, a, b):
+        if b <= M[t]:
+            return ap("sf", a, b)
+        return ap("se", a - M[t], b - M[t]) if b <= late[t] else ap("sl", a - late[t], b - late[t])
+
+    def qcol(t, r, a, b):
+        o = 512 * (r % 2) - rng[t][r][0]
+        return ap("xq", o + a, o + b)
 
     def own(name, a, b):
         return ap(name, GH + a, GH + b)
 
-    def gather(t, c, vec=False):
-        a, b = nch[t][c]
+    def dbc(a, b):
+        return ap("db", PAD + a, PAD + b)
+
+    def pieces(t, r):
+        return [(a, b, True) for a, b in blk[t]] if r == 0 else [rng[t][r] + (False,)]
+
+    def link(name, a, b, k, major):
+        if major:
+            return ap(name, 16 * a + k * (b - a), 16 * a + (k + 1) * (b - a))
+        return ap(name, 16 * a + k, 16 * b, 16)
+
+    def gather(t, a, b, vec=False):
         src = ind(ap(Wn[t], 0, GH + BASE[t]), ap(On[t], a, b))
         if vec:
-            ts(ap("P", 16 * a, 16 * b), src, 0.25, A.mult)
+            cp(ap("P", 16 * a, 16 * b), src)
         else:
-            act(ap("P", 16 * a, 16 * b), src, AF.Copy, scale=0.25)
+            act(ap("P", 16 * a, 16 * b), src, AF.Copy)
 
-    def gather2(t, a, b, vec=False):
-        src = ind(ap(Ln[t], 0, GH + BASE[t]), ap(On[t], a, b))
-        if vec:
-            ts(ap("Q", 16 * a, 16 * b), src, -1.0 / BIG, A.mult)
-        else:
-            act(ap("Q", 16 * a, 16 * b), src, AF.Copy, scale=-1.0 / BIG)
+    qleft = [[[0, BASE[t]]] for t in range(RO)]
+    qleft[0] = [[M[0], L0N], [0, M[0]]]
 
-    def copy_x(t, name, cut, ident):
-        for a, b in ((0, cut), (cut, BASE[t])):
-            mm(pcol(name, cut, a, b), ap(ident, 0, 128), own(Wn[t], a, b), True, True)
+    def gather2(t, cells, vec=False):
+        while cells > 0 and qleft[t]:
+            a = qleft[t][0][0]
+            b = min(qleft[t][0][1], a + cells, a + 256)
+            cells -= b - a
+            qleft[t][0][0] = b
+            if b == qleft[t][0][1]:
+                qleft[t].pop(0)
+            src = ind(ap(Ln[t], 0, GH + BASE[t]), ap(On[t], a, b))
+            if vec:
+                ts(ap("Q", 16 * a, 16 * b), src, -1.0, A.mult)
+            else:
+                act(ap("Q", 16 * a, 16 * b), src, AF.Copy, scale=-1.0)
 
-    def s_min(t, c):
-        a, b = nch[t][c]
+    def gather2_upto(t, r):
+        while any(a < rng[t][r][1] and b > rng[t][r][0] for a, b in qleft[t]):
+            a, b = qleft[t][0]
+            gather2(t, min(256, (rng[t][r][1] if a < rng[t][r][1] else b) - a, b - a))
+
+    def copy_x(t, bank):
+        a, b = ((0, cut[t]), (cut[t], BASE[t]))[bank]
+        mm(xcol(t, a, b), ap("I1", 0, 128), own(Wn[t], a, b), True, True)
+
+    def start_s(t, a, b):
+        mm(scol(t, a, b), ap("I1", 0, 128), own(Wn[t], a, b), True, False)
+
+    def s_min(a, b):
         n = 16 * (b - a)
         scan(ap("SN", 0, n), ap("m2", 0, n), ap("P", 16 * a, 16 * b), A.add, A.min)
 
-    def s_max(t, c):
-        a, b = nch[t][c]
+    def s_max(t, a, b):
         n = 16 * (b - a)
         scan(ap("SX", 0, n), ap("m1", 0, n), ap("P", 16 * a, 16 * b), A.mult, A.max)
+        mm(scol(t, a, b), ap("Iq", 0, 128), ap("SX", 15, n, 16), False, False)
 
-    def u_a(t, c):
-        a, b = nch[t][c]
-        tt(ap("ab", a, b), ap("SN", 15, 16 * (b - a), 16), pcol("xp", split[t], a, b), A.mult)
+    def u_a(t, a, b):
+        z = ap("Z", a, b) if b <= M[t] else ap("SN", 15, 16 * (b - a), 16)
+        tt(ap("ab", a, b), z, xcol(t, a, b), A.mult)
 
-    def u_s(t, c):
-        a, b = nch[t][c]
-        x = pcol("xp", split[t], a, b)
-        tt(x, ap("SX", 15, 16 * (b - a), 16), x, A.add)
-
-    def u_b(a, b, on_s):
+    def u_b(a, b, on_s=True):
         if on_s:
-            act(ap("ab", a, b), ap("ab", a, b), AF.Copy, scale=3.0)
+            act(ap("ab", a, b), ap("ab", a, b), AF.Copy, scale=-0.75)
         else:
-            ts(ap("ab", a, b), ap("ab", a, b), 3.0, A.mult)
+            ts(ap("ab", a, b), ap("ab", a, b), -0.75, A.mult)
 
     def u_d(t, a, b):
-        tt(ap("db", a, b), pcol("xp", split[t], a, b), ap("ab", a, b), A.subtract)
+        mm(scol(t, a, b), ap("I1", 0, 128), ap("ab", a, b), False, True)
 
     def u_flag(t, a, b):
-        if PAR["fl_s"]:
-            act(ap("fl", a, b), ap("db", a, b), AF.Sign, bias=-(3.5 + 2.0 ** -22), scale=3.5)
-        else:
-            ts(ap("fl", a, b), ap("db", a, b), 1.0, A.is_gt)
-        mm(pcol("vo", split[t], a, b), ap("ones", 0, 128), ap("fl", a, b), True, True)
+        act(ap("fl", a, b), scol(t, a, b), AF.Sign, bias=-(3.5 + 2.0 ** -22), scale=3.5)
+
+    def vote(a, b, at):
+        mm(ap("vo", at, at + b - a), ap("ones", 0, 128), ap("fl", a, b), True, True)
+
+    def ready(a, b, at):
+        act(ap("rs", a, b), ap("vo", at, at + b - a), AF.Sign, bias=1.0)
 
     def u_clip(t, a, b):
-        ts(own(Wn[t + 1], a, b), ap("db", a, b), 0.0, A.max, 2.0, A.min)
+        ts(own(Wn[t + 1], a, b), scol(t, a, b), 0.0, A.max, 2.0, A.min)
 
-    def l_cmp(t, a, b, k, start, stop):
-        f = ap("F", 512 * k, 512 * k + b - a)
-        tt(f, ap("P", 16 * a + k, 16 * b, 16), pcol("cq", LA[t], a, b), A.is_gt)
-        mm(pcol("xq", LA[t], a, b), ap("Bm", 128 * k, 128 * k + 128), f, start, stop)
+    opened = {}
 
-    def l_diag(t, a, b, first, k0=0, k1=16):
-        for k in range(k0, k1):
-            mm(pcol("xq", LA[t], a, b), ap("Dm", 128 * k, 128 * k + 128), ap("Q", 16 * a + k, 16 * b, 16),
-               first and k == 0, False)
+    def first(t, r):
+        f = (t, r) not in opened
+        opened[t, r] = opened.get((t, r), 0) + 1
+        return f, opened[t, r] == 16 + 16 * len(pieces(t, r))
 
-    def l_y(t, a, b):
-        tt(ap("db", a, b), pcol("xq", LA[t], a, b), ap("Lb", a, b), A.min)
+    def l_cmp(t, r, k):
+        a0 = rng[t][r][0]
+        for a, b, major in pieces(t, r):
+            tt(ap("F", 512 * k + a - a0, 512 * k + b - a0), link("P", a, b, k, major), xcol(t, a, b), A.is_gt)
+        a, b = rng[t][r]
+        mm(qcol(t, r, a, b), ap("Bm", 16 - k, 144 - k), ap("F", 512 * k, 512 * k + b - a), *first(t, r))
 
-    def l_abs(t, a, b):
-        act(own(Ln[t + 1], a, b), ap("db", a, b), AF.Abs)
+    def l_diag(t, r):
+        gather2_upto(t, r)
+        for k in range(16):
+            for a, b, major in pieces(t, r):
+                mm(qcol(t, r, a, b), ap("Dm", 128 * k, 128 * k + 128), link("Q", a, b, k, major), *first(t, r))
 
-    def l_off(t, a, b):
-        if PAR["off_s"]:
-            act(ap(On[t + 1], a, b), ap("db", a, b), AF.Abs)
-        else:
-            cp(ap(On[t + 1], a, b), own(Ln[t + 1], a, b))
+    def l_y(t, r):
+        a, b = rng[t][r]
+        tt(dbc(a, b), qcol(t, r, a, b), ap("Lb", a, b), A.min)
+
+    def l_abs(t, r):
+        a, b = rng[t][r]
+        act(own(Ln[t + 1], a, b), dbc(a, b), AF.Abs)
+
+    def l_off(t, r):
+        a, b = max(rng[t][r][0], M[t + 1]), min(rng[t][r][1], L0N)
+        if a < b:
+            act(ap(On[t + 1], a, b), dbc(a, b), AF.Abs)
+
+    def l_turn(t, name, o):
+        turn(ap("TT", 0, M[t]), ap(name, o, o + M[t]))
+        turn(ap("TT", MM, MM + M[t] + 32), ap(name, o - 16, o + M[t] + 16))
+
+    def l_list(t):
+        act(ap(On[t], 0, M[t]), ind(ap("TT", 0, MM + M[t] + 32), ap("lst", 0, M[t] // 16)), AF.Abs)
+
+    def folds(t):
+        for i, (a, b) in enumerate(blk[t]):
+            h = b - (PAR["fv"][t] if i == 0 else 0)
+            if h > a:
+                gather(t, a, h)
+            if h < b:
+                gather(t, h, b, True)
+            fold(t, i)
 
     dma("y", own("W0", 0, 256), hbm("x0", 0, 256))
     dma("s", ap("nbi", 0, L0N), hbm("nb", 0, L0N))
     dma("y", own("W0", 256, L0N), hbm("x0", 256, L0N))
-    iota(ap("La", 0, GH), [[1, GH]], 0, 0)
     iota(ap("ci", 0, 1), [[0, 1]], 0, 1)
+    iota(ap("La", 0, GH), [[1, GH]], 0, 0)
+    allb = bounds(PAR["blocks"][:max(PAR["nblk"])])
+    for a, b in allb:
+        c = (b - a) // 16
+        iota(ap("lsf", a // 16, b // 16), [[16 // c, c]], a, 0)
     mset(ap("m1", 0, 2048), 1.0)
+    ts(ap("ci", 1, 2), ap("ci", 0, 1), 15, A.bitwise_and)
+    ts(ap("ci", 2, 3), ap("ci", 0, 1), 4, A.logical_shift_right)
     mset(ap("m2", 0, 2048), 0.0)
+    tt(ap("ci", 3, 4), ap("ci", 0, 1), ap("ci", 2, 3), A.add)
     mset(ap("m1", 0, 2048, 16), 0.0)
-    mset(ap("m2", 0, 2048, 16), 1.0)
+    ts(ap("ci", 3, 4), ap("ci", 3, 4), 1, A.bitwise_and)
+    mset(ap("m2", 0, 2048, 16), 4.0)
+    for j, (a, b) in enumerate(allb):
+        c = (b - a) // 16
+        ts(ap("ci", 4 + 2 * j, 5 + 2 * j), ap("ci", 0, 1), c - 1, A.bitwise_and)
+        ts(ap("ci", 5 + 2 * j, 6 + 2 * j), ap("ci", 1, 2), c.bit_length() - 1, A.logical_shift_right)
     mset(ap("n2", 0, 1), 2.0 * (GH + L0N))
+    cp(ap("cf", 0, 4 + 2 * len(allb)), ap("ci", 0, 4 + 2 * len(allb)))
+    mset(ap("TT", 0, 2 * MM + 32), 0.0)
+    for j, (a, b) in enumerate(allb):
+        f = ap("cf", 4 + 2 * j, 5 + 2 * j)
+        ts(f, f, 16.0, A.mult, ap("cf", 5 + 2 * j, 6 + 2 * j), A.add)
+    mset(ap("db", 0, PAD + MM + 16), 0.0)
+    for j, (a, b) in enumerate(allb):
+        ts(ap("cf", 5 + 2 * j, 6 + 2 * j), ap("cf", 3, 4), MM + 16.0, A.mult, ap("cf", 4 + 2 * j, 5 + 2 * j), A.add)
     mset(ap("rs", L0N, LM), -1.0)
+    for j, (a, b) in enumerate(allb):
+        ts(ap("lst", a // 16, b // 16), ap("lsf", a // 16, b // 16), ap("cf", 5 + 2 * j, 6 + 2 * j), A.add)
     send(0)
     dma("y", ap("m1", 2048, 4096), ap("m1", 0, 2048))
     dma("y", ap("m2", 2048, 4096), ap("m2", 0, 2048))
-    cp(ap("off0", 0, L0N), ap("nbi", 0, L0N))
+    cp(ap("off0", M[0], L0N), ap("nbi", M[0], L0N))
     cp(own("La", 0, L0N), ap("nbi", 0, L0N))
-    early = PAR["g2s"] + PAR["g2v"]
-    for a, b in g2[0][0][:PAR["g2s"]]:
-        gather2(0, a, b)
+    l_turn(0, "La", GH)
+    for j, cells in enumerate(PAR["qs0"]):
+        gather2(0, cells)
+        if j == 0:
+            l_list(0)
     iota(ap("I1", 0, 128), [[0, 128]], 1, 0)
     sel(ap("I1", 0, 128), ap("I1", 0, 128), [[-1, 128]], A.is_equal, 0, 1)
-    iota(ap("Am", 0, 128), [[0, 8], [1, 16]], 0, 0)
+    iota(ap("Am", 0, 144), [[1, 144]], -16, 0)
     iota(ap("mk6", 0, 8), [[1, 8]], 0, 0)
     iota(ap("ew2", 0, 8), [[32, 8]], -2 * (GH + L0N), 0)
-    iota(ap("cf", 4, 5), [[0, 1]], 1, 2)
+    iota(ap("cf", 8, 9), [[0, 1]], 1, 2)
     iota(ap("e2", 0, CAP), [[2, CAP]], 0, 0)
-    ts(ap("ci", 1, 2), ap("ci", 0, 1), 15, A.bitwise_and)
-    ts(ap("ci", 2, 3), ap("ci", 0, 1), 4, A.logical_shift_right)
-    cp(ap("cf", 0, 3), ap("ci", 0, 3))
-    copy_x(0, "xp", split[0], "I1")
-    ts(ap("cf", 3, 4), ap("cf", 1, 2), 2.0, A.mult)
+    iota(ap("ones", 0, LM), [[0, LM]], 1, 0)
+    ts(ap("cf", 9, 11), ap("cf", 1, 3), 2.0, A.mult)
     ts(ap("Iq", 0, 128), ap("I1", 0, 128), 0.25, A.mult)
+    ts(ap("cf", 10, 11), ap("cf", 10, 11), 8.0, A.mult)
     ts(ap("sX", 0, 4), ap("mk6", 0, 4), ap("cf", 1, 2), A.is_equal)
-    ts(ap("Am", 0, 128), ap("Am", 0, 128), ap("cf", 1, 2), A.is_equal)
+    ts(ap("Bm", 0, 144), ap("Am", 0, 144), ap("cf", 10, 11), A.is_equal, float(BIG), A.mult)
+    iota(ap("Am", 0, 128), [[0, 8], [1, 16]], 0, 0)
     ts(ap("mk6", 0, 8), ap("mk6", 0, 8), ap("cf", 2, 3), A.is_equal)
     ts(ap("sR", 0, 4), ap("sX", 0, 4), -2.5, A.mult, 2.0, A.add)
-    ts(ap("ew2", 0, 8), ap("ew2", 0, 8), ap("cf", 3, 4), A.add)
+    ts(ap("ew2", 0, 8), ap("ew2", 0, 8), ap("cf", 9, 10), A.add)
     ts(ap("sX", 0, 4), ap("sX", 0, 4), -3.0, A.mult, 4.0, A.add)
-    for a, b in g2[0][0][PAR["g2s"]:early]:
-        gather2(0, a, b, True)
-    gather(0, 0, PAR["g0v"])
-    gather(0, 1)
-    iota(ap("ones", 0, LM), [[0, LM]], 1, 0)
+    ts(ap("Am", 0, 128), ap("Am", 0, 128), ap("cf", 1, 2), A.is_equal)
+    copy_x(0, 0)
+    copy_x(0, 1)
+    for a, b in ((M[0], late[0]), (0, M[0]), (late[0], L0N)):
+        start_s(0, a, b)
+    for cells in PAR["qv0"]:
+        gather2(0, cells, True)
     iota(own("La", L0N, LM), [[1, LM - L0N]], GH + L0N, 0)
     dma("y", ap("Lb", 0, BASE[1]), own("La", 0, BASE[1]))
+    for h in range(2):
+        sel(ap("Dm", 1024 * h, 1024 * h + 1024), ap("ones", 0, 1024), [[-256, 8], [16, 8], [257, 16]], A.is_equal,
+            -2048 * h, -1)
+    folds(0)
     for t in range(RO):
         iota(own(Wn[t + 1], BASE[t], BASE[t + 1]), [[0, CAP]], 0, 0)
-    bm, dm = ap("Bm", 0, 2048), ap("Dm", 0, 2048)
-    iota(bm, [[0, 2048]], BIG, 0)
-    sel(bm, bm, [[-1, 16], [0, 8], [1, 16]], A.is_equal, 0, 0)
-    sel(dm, bm, [[0, 16], [-1, 128]], A.is_equal, 0, 1)
-    sel(bm, bm, [[0, 16], [-16, 8], [0, 16]], A.is_ge, 0, 1)
-    sel(bm, bm, [[0, 16], [16, 8], [0, 16]], A.is_ge, 15, -1)
     iota(ap("IOT", 0, LM), [[1, LM]], GH, 0)
     iota(ap("Lc", 0, GH), [[1, GH]], 0, 0)
     iota(own("Lc", L0N, LM), [[1, LM - L0N]], GH + L0N, 0)
 
     offm, offc = ap("offm", 0, 6), ap("offc", 0, 6)
     fills = PAR["fill"]
-    vote = 1.0 if PAR["fl_s"] else -63.5
 
     def child_gather(t):
         tt(ap("CL", 0, CAP), ind(own(Ln[t + 1], 0, BASE[t + 1]), offm), ap("X1", 0, CAP), A.min)
@@ -320,90 +461,100 @@ def _plan(g, core, T, topo, rank):
             cp(ind(own(Ln[t + 1], L0N, BASE[t + 1]), offc), ap("CL", 0, CAP))
 
     for t in range(RO):
-        n, nn, sp, la = BASE[t], BASE[t + 1], split[t], LA[t]
+        n, nn, m, lt = BASE[t], BASE[t + 1], M[t], late[t]
         last = t == RO - 1
         W1 = Wn[t + 1]
-        nc = len(nch[t])
+        ch = nch[t]
+        nv = PAR["nv"][t]
+        q = PAR["q"][t]
         n2 = ap("n2", t, t + 1)
-        s_min(t, 0)
-        if t > 0:
-            l_y(t - 1, LA[t - 1], BASE[t - 1])
-            if PAR["off_s"]:
-                l_off(t - 1, LA[t - 1], L0N)
-            l_abs(t - 1, LA[t - 1], BASE[t - 1])
-        s_max(t, 0)
-        u_a(t, 0)
-        if t > 0 and not PAR["off_s"]:
-            l_off(t - 1, LA[t - 1], L0N)
-        ts(ap("cc", 0, 1), ap("cf", 4, 5), n2, A.add, float(-1 - nn - 2 * GH), A.add)
-        u_s(t, 0)
-        gather(t, 2)
-        copy_x(t, "cq", la, "Iq")
-        s_min(t, 1)
-        if t > 0:
-            child_gather(t - 1)
-        ts(ap("RV", 0, CAP), ap("e2", 0, CAP), n2, A.add, ap("sR", t, t + 1), A.mult)
-        if t > 0:
-            child_put(t - 1)
-        u_a(t, 1)
-        if t > 0:
-            cp(ap(On[t], L0N, n), own(Ln[t], L0N, n))
-            dma("y", ap("Lb", 0, nn), own(Ln[t], 0, nn))
-        s_max(t, 1)
-        if t > 0:
-            ts(offc, ap("ew2", 0, 6), n2, A.add, 0.5, A.mult)
-        u_s(t, 1)
-        for c in range(3, nc):
-            gather(t, c)
-        u_b(0, sp, True)
-        for a, b in g2[t][0][(early if t == 0 else 0):]:
-            gather2(t, a, b)
-        kk = [0]
+        todo = [(r, k) for r in range(3) for k in range(16)]
 
-        def fill(cnt):
-            for _ in range(cnt):
-                if kk[0] < 16:
-                    l_cmp(t, 0, la, kk[0], kk[0] == 0 and PAR["diag"] == 0, kk[0] == 15)
-                    kk[0] += 1
-        for c in range(2, nc):
-            s_min(t, c)
-            if c == nc - 1:
-                u_d(t, 0, sp)
-            s_max(t, c)
-            u_a(t, c)
-            if c == nc - 1:
-                u_clip(t, 0, sp)
-            u_s(t, c)
-        u_flag(t, 0, sp)
-        l_diag(t, 0, la, True, 0, PAR["diag"])
-        u_b(sp, n, PAR["b_s"])
-        act(ap("rs", 0, sp), pcol("vo", sp, 0, sp), AF.Sign, bias=vote)
+        def fill(cnt, upto=2):
+            while cnt > 0 and todo and todo[0][0] < upto:
+                r, k = todo.pop(0)
+                l_cmp(t, r, k)
+                cnt -= 1
+        gathered = [0]
+
+        def gathers(upto):
+            for c in range(max(nv, gathered[0]), len(ch)):
+                if ch[c][1] <= upto:
+                    gather(t, *ch[c])
+                    gathered[0] = c + 1
+        if nv > 0:
+            gather(t, *ch[0], True)
+        if t > 0:
+            gathers(cut[t - 1])
+            l_y(t - 1, 2)
+            l_off(t - 1, 2)
+            l_abs(t - 1, 2)
+        gathers(L0N)
+        fill(PAR["fa"][t][0])
+        for c, (a, b) in enumerate(ch):
+            if 0 < c < nv:
+                gather(t, a, b, True)
+            s_min(a, b)
+            if c == 0:
+                ts(ap("cc", 0, 1), ap("cf", 8, 9), n2, A.add, float(-1 - nn - 2 * GH), A.add)
+                ts(ap("RV", 0, CAP), ap("e2", 0, CAP), n2, A.add, ap("sR", t, t + 1), A.mult)
+                if t > 0:
+                    child_gather(t - 1)
+            u_a(t, a, b)
+            if c == 0 and t > 0:
+                child_put(t - 1)
+            if c == len(ch) - 2:
+                gather2(t, q[0])
+                u_b(m, lt)
+            if c == len(ch) - 1 and PAR["b_last_v"]:
+                u_b(a, b, False)
+            s_max(t, a, b)
+            if c == 0 and t > 0:
+                cp(ap(On[t], L0N, n), own(Ln[t], L0N, n))
+                ts(offc, ap("ew2", 0, 6), n2, A.add, 0.5, A.mult)
+                gathers(n)
+                dma("y", ap("Lb", 0, nn), own(Ln[t], 0, nn))
+            if c == len(ch) - 2:
+                u_d(t, m, lt)
+                u_flag(t, m, lt)
+                vote(m, lt, 0)
+                gather2(t, q[1])
+                ready(m, lt, 0)
+        if not PAR["b_last_v"]:
+            u_b(lt, n)
+        u_d(t, lt, n)
+        u_flag(t, lt, n)
+        u_clip(t, m, lt)
+        fill(PAR["fa"][t][1])
+        gather2(t, q[6])
+        for a, b in blk[t]:
+            u_a(t, a, b)
+            mm(scol(t, a, b), ap("Iq", 0, 128), ap("Y", a, b), False, False)
+        u_b(0, m)
+        u_d(t, 0, m)
+        vote(lt, n, m)
         fill(fills[0])
-        u_d(t, sp, n)
-        for a, b in g2[t][1]:
-            gather2(t, a, b)
+        u_clip(t, lt, n)
+        u_flag(t, 0, m)
+        vote(0, m, 0)
         fill(fills[1])
-        u_flag(t, sp, n)
-        u_clip(t, sp, n)
-        act(ap("rs", sp, n), pcol("vo", sp, sp, n), AF.Sign, bias=vote)
+        u_clip(t, 0, m)
+        ready(lt, n, m)
+        ready(0, m, 0)
         fill(fills[2])
         scan(ap("cum", 0, nn), ap("rs", 0, nn), ap("ones", 0, nn), A.add, A.add)
-        for a, b in g2[t][2]:
-            gather2(t, a, b)
-        act(ap("fl", 0, nn), ap("cum", 0, nn), AF.Sign, bias=ap("cf", 4, 5), scale=-1.0, acc=ap("acc", 0, 1))
-        for a, b in g2[t][3]:
-            gather2(t, a, b)
+        gather2(t, q[2])
+        act(ap("fl", 0, nn), ap("cum", 0, nn), AF.Sign, bias=ap("cf", 8, 9), scale=-1.0, acc=ap("acc", 0, 1))
+        gather2(t, q[3])
         fill(fills[3])
         ts(ap("B6", 0, 6), ap("mk6", 0, 6), ap("acc", 0, 1), A.mult, ap("cc", 0, 1), A.min)
         mm(ap("vo", 496, 502), ap("Am", 0, 128), ap("B6", 0, 6), True, True)
-        l_diag(t, 0, la, False, PAR["diag"], 16)
         fill(fills[4])
         ts(offm, ap("vo", 496, 502), 0.5, A.mult, nn / 2.0, A.add)
         fill(fills[5])
         ts(ap("Cx", 0, CAP), ind(own(W1, 0, nn), offm), 0.5, A.mult)
         tt(ap("LS", 0, CAP), ind(own(Ln[t], 0, nn), offm), ap("RV", 0, CAP), A.min)
         cp(ind(own(W1, 0, nn), offm), ap("Cx", 0, CAP))
-        cp(ind(ap("Lb", 0, nn), offm), ap("LS", 0, CAP))
         if t == 0:
             cp(own(W1, L0N, nn), ap("Cx", 0, CAP))
         else:
@@ -412,39 +563,51 @@ def _plan(g, core, T, topo, rank):
             dma("y", hbm("yx", 0, LM), own(W1, 0, LM))
         else:
             send(t + 1)
+        cp(ind(ap("Lb", 0, nn), offm), ap("LS", 0, CAP))
         ts(ap("n2", t + 1, t + 2), ap("cum", n - 1, n), 2.0 * CAP, A.min, n2, A.add)
-        fill(16)
-        l_cmp(t, la, n, 0, True, False)
+        l_diag(t, 0)
+        fill(16, 1)
+        gather2(t, q[4])
+        fill(fills[6])
         if last:
-            ts(ap("xp", 0, LM - L0N), ap("IOT", L0N, LM), 2.0, A.mult, ap("n2", RO, RO + 1), A.is_lt)
-        l_y(t, 0, la)
-        if not last and PAR["off_s"]:
-            l_off(t, 0, la)
-        l_abs(t, 0, la)
-        if PAR["x1_s"]:
-            act(ap("X1", 0, CAP), ind(ap("IOT", 0, nn), offm), AF.Copy, scale=ap("sX", t, t + 1))
-        else:
-            ts(ap("X1", 0, CAP), ind(ap("IOT", 0, nn), offm), ap("sX", t, t + 1), A.mult)
-        if last:
-            dma("y", hbm("yn", 0, la), own(Ln[t + 1], 0, la))
-        l_diag(t, la, n, False)
-        l_cmp(t, la, n, 1, False, False)
+            ts(ap("se", 0, LM - L0N), ap("IOT", L0N, LM), 2.0, A.mult, ap("n2", RO, RO + 1), A.is_lt)
+        l_y(t, 0)
+        turn_after = 0 if M[t + 1] <= m else 1
+        if not last and turn_after == 0:
+            l_turn(t + 1, "db", PAD)
+        l_off(t, 0) if not last else None
+        l_abs(t, 0)
+        act(ap("X1", 0, CAP), ind(ap("IOT", 0, nn), offm), AF.Copy, scale=ap("sX", t, t + 1))
+        fill(16, 2)
+        l_diag(t, 1)
+        gather2(t, q[5])
+        fill(fills[8], 3)
+        l_y(t, 1)
         if not last:
-            if not PAR["off_s"]:
-                l_off(t, 0, la)
-            gather(t + 1, 0)
-            gather(t + 1, 1)
-        for k in range(2, 16):
-            l_cmp(t, la, n, k, False, k == 15)
-            if k == PAR["xk"] and not last:
-                copy_x(t + 1, "xp", split[t + 1], "I1")
-    l_y(RO - 1, LA[RO - 1], BASE[RO - 1])
-    l_abs(RO - 1, LA[RO - 1], BASE[RO - 1])
+            l_off(t, 1)
+            if turn_after == 1:
+                l_turn(t + 1, "db", PAD)
+            l_list(t + 1)
+        l_abs(t, 1)
+        if last:
+            dma("y", hbm("yn", 0, cut[t]), own(Ln[t + 1], 0, cut[t]))
+        fill(PAR["xk"], 3)
+        if not last:
+            copy_x(t + 1, 0)
+            for a, b in ((M[t + 1], late[t + 1]), (0, M[t + 1]), (late[t + 1], nn)):
+                start_s(t + 1, a, b)
+        fill(16, 3)
+        l_diag(t, 2)
+        if not last:
+            copy_x(t + 1, 1)
+            folds(t + 1)
+    l_y(RO - 1, 2)
+    l_abs(RO - 1, 2)
     child_gather(RO - 1)
     child_put(RO - 1)
     tail = own(Ln[RO], L0N, LM)
-    tt(tail, tail, ap("xp", 0, LM - L0N), A.mult)
-    dma("y", hbm("yn", LA[RO - 1], LM), own(Ln[RO], LA[RO - 1], LM))
+    tt(tail, tail, ap("se", 0, LM - L0N), A.mult)
+    dma("y", hbm("yn", cut[RO - 1], LM), own(Ln[RO], cut[RO - 1], LM))
     return ops
 
 
@@ -538,8 +701,29 @@ def _emit(g, T, ops):
             queue["g" if o["q"] == "g" else "y"].wait_ge(T.sem[o["tok"][0]], o["tok"][1])
 
 
+def _hand_back(g, core, T, topo):
+    for home in topo.cores_of(core):
+        if T.rank_of(home) is None:
+            continue
+        for w, h in _helpers(home, T, topo).items():
+            if h != core:
+                continue
+            rid, pid = topo.addr(home, core)
+            got = PAR["feng"] if PAR["split"] else PAR["feng"] // 2
+            eng = topo.engines(core, home)[:PAR["heng"]]
+            sent = 0
+            for t in range(RO):
+                for i, (a, b) in enumerate(_blocks(t)):
+                    g.wait_ge(T.sem["fa%d%d%s" % (t, i, w)], got)
+                    g.remote_dma(T[w][:, a:b], T.P[:, MM * t + a:MM * t + b], T.sem["fb%d%d%s" % (t, i, w)],
+                                 T.sem.ho, pid, rid, _mask(eng))
+                    sent += len(eng)
+            g.wait_ge(T.sem.ho, sent)
+
+
 def rank_program(g, core, T, topo):
     rank = T.rank_of(core)
     if rank is None:
+        _hand_back(g, core, T, topo)
         return
     _emit(g, T, _plan(g, core, T, topo, rank))

@@ -7,21 +7,18 @@ PL = GH + LM
 BIG = 4096
 MM = 384
 PAD = 16
+UNIT = 32
 PAR = {
-    "blocks": [256, 128],
-    "nblk": [1, 1, 1, 1],
-    "nch": [[128, 128, 128], [128, 96, 128, 128], [160, 64, 192, 160], [160, 96, 256, 160]],
-    "nv": [1, 1, 1, 1],
-    "ncut": [1, 2, 2, 2],
-    "split": False, "feng": 16, "heng": 8,
-    "q": [[0, 0, 32, 32, 0, 0, 128], [128, 0, 32, 64, 128, 128, 64], [128, 0, 32, 64, 128, 192, 64],
-          [128, 0, 32, 64, 128, 256, 64]],
-    "fv": [128, 128, 128, 128], "fa": [[4, 4], [4, 2], [4, 2], [4, 2]],
-    "qs0": [128, 128], "qv0": [128],
-    "fill": [2, 2, 2, 2, 3, 3, 1, 1, 2, 3],
-    "xk": 4, "b_last_v": True,
+    "m": [128, 224, 224, 224],
+    "nch": [[128, 128, 192, 64], [128, 128, 128, 128], [128, 128, 192, 160], [128, 160, 224, 192]],
+    "ncut": [2, 2, 2, 2],
+    "heng": 8, "mw": 4096, "dw": 128, "q0": 448, "rho_s": 1.0, "rho_c": 1.0,
+    "small": 10.0, "tolv": 0.3, "tols": 0.3, "tolp": 0.1, "tolg": 0.2, "toly": 0.0,
+    "gam": 1.56, "wake": 0.06, "fold": 0.033, "back": 2.6, "ghost": [6.5, 3.8], "rho_p": 0.6, "rho_q": 0.8,
+    "run_p": 128, "run_q": 256, "run_v": 128, "vbias": 0.0, "beta": 1.0, "look": 4,
 }
-PAR.update({"nch": [[128, 192, 64], [48, 80, 224, 128], [96, 96, 176, 208], [96, 160, 160, 256]], "split": True, "q": [[48, 16, 16, 64, 0, 0, 128], [160, 64, 32, 48, 112, 128, 80], [240, 112, 32, 0, 128, 192, 32], [208, 96, 48, 64, 144, 256, 16]], "fv": [128, 96, 128, 96], "fa": [[7, 6], [6, 6], [5, 7], [1, 4]], "qs0": [128, 128], "qv0": [96], "fill": [2, 5, 1, 7, 1, 0, 4, 1, 5, 3], "xk": 0})
+PAR.update({"early": 16, "peb": 0, "e_b0": "ssss", "e_b1": "svvv", "e_b2": "ssss", "e_cx": "svvv", "e_c0": "sss", "e_oc": "svvv", "share_P": [128, 160, 192, 192], "share_Q": [0, 64, 64, 64], "m": [160, 224, 256, 224], "nch": [[96, 128, 208, 48], [144, 144, 144, 80], [96, 128, 176, 176], [112, 160, 208, 224]], "ncut": [2, 2, 2, 2], "heng": 16, "mw": 4096, "dw": 128, "q0": 384, "rho_s": 1.0, "rho_c": 1.04, "small": 5, "tolv": 0.1, "tols": 0.25, "tolp": 0.05, "tolg": 0.0, "toly": 0.0, "gam": 1.56, "wake": 0.06, "fold": 0.035, "back": [5.0, 2.8], "ghost": [6, 3.8], "rho_p": 1.0, "rho_q": 1.0, "run_p": 128, "run_q": 256, "run_v": 128, "vbias": [5, 5, 5, 5], "beta": 1, "look": 4})
+PAR.update({"m": [128, 224, 256, 256], "nch": [[96, 144, 208, 64], [144, 144, 144, 80], [96, 160, 112, 208], [112, 128, 224, 208]], "ncut": [2, 1, 2, 2], "heng": 16, "mw": 4096, "dw": 64, "q0": 352, "rho_s": 1.16, "rho_c": 1.04, "small": 5, "tolv": 0.1, "tols": 0.25, "tolp": 0.1, "tolg": 0.0, "toly": 0.0, "gam": 1.56, "wake": 0.06, "fold": 0.035, "back": [5.0, 2.8], "ghost": [6, 4.05], "rho_p": 1.0, "rho_q": 0.92, "run_p": 128, "run_q": 256, "run_v": 128, "vbias": [5, 13, 5, 5], "beta": 1, "look": 4, "early": 0, "peb": 1, "e_b0": "ssss", "e_b1": "vvvv", "e_b2": "ssss", "e_cx": "svvs", "e_c0": "vss", "e_oc": "vsvv", "share_P": [128, 160, 192, 192], "share_Q": [0, 64, 64, 64]})
 
 SCRATCH = {
     "W0": ("sbuf", [128, PL], "float32"), "W1": ("sbuf", [128, PL], "float32"),
@@ -36,14 +33,16 @@ SCRATCH = {
     "SX": ("sbuf", [128, 4096], "float32"), "SN": ("sbuf", [128, 4096], "float32"),
     "m1": ("sbuf", [128, 4096], "bfloat16"), "m2": ("sbuf", [128, 4096], "bfloat16"),
     "ab": ("sbuf", [128, 928], "float32"), "db": ("sbuf", [128, PAD + 928], "float32"),
-    "TT": ("sbuf", [128, 2 * MM + 32], "float32"), "lst": ("sbuf", [128, MM // 16], "uint16"),
-    "lsf": ("sbuf", [128, MM // 16], "float32"),
+    "TT": ("sbuf", [128, 2 * MM + 32], "float32"), "lst": ("sbuf", [128, MM // 4], "uint16"),
+    "lsf": ("sbuf", [128, MM // 4], "float32"), "lsj": ("sbuf", [128, MM // 4], "float32"),
+    "lsk": ("sbuf", [128, MM // 4], "int32"), "Bi": ("sbuf", [128, 144], "float32"),
     "Y": ("sbuf", [128, MM], "float32"), "Z": ("sbuf", [128, MM], "float32"),
     "fl": ("sbuf", [128, LM], "bfloat16"), "rs": ("sbuf", [128, LM], "bfloat16"),
     "cum": ("sbuf", [128, LM], "bfloat16"), "ones": ("sbuf", [128, LM], "bfloat16"),
     "Bm": ("sbuf", [128, 144], "bfloat16"), "Dm": ("sbuf", [128, 2048], "bfloat16"),
     "I1": ("sbuf", [128, 128], "float32"), "Iq": ("sbuf", [128, 128], "float32"),
-    "Am": ("sbuf", [128, 144], "float32"), "IOT": ("sbuf", [128, LM], "float32"),
+    "Ib": ("sbuf", [128, 128], "float32"),
+    "Am": ("sbuf", [128, 128], "float32"), "IOT": ("sbuf", [128, LM], "float32"),
     "ci": ("sbuf", [128, 8], "int32"), "cf": ("sbuf", [128, 12], "float32"),
     "mk6": ("sbuf", [128, 8], "float32"), "ew2": ("sbuf", [128, 8], "float32"),
     "sR": ("sbuf", [128, 4], "float32"), "sX": ("sbuf", [128, 4], "float32"),
@@ -59,19 +58,11 @@ SCRATCH = {
     "sl": ("psum", [128, 512], "float32"), "vo": ("psum", [128, 512], "float32"),
 }
 PSUM = ("xp", "xq", "sf", "se", "sl", "vo")
-NDMA = 12
-FOLDS = [(t, i, w) for t in range(RO) for i in range(2) for w in "ZY"]
-SEMAPHORES = (["cv", "cs", "cp", "cg"] + ["d%d" % i for i in range(NDMA)]
-              + ["arr%d" % t for t in range(RO)] + ["out%d" % t for t in range(RO)]
-              + ["%s%d%d%s" % (s, t, i, w) for s in ("fo", "fa", "fb") for t, i, w in FOLDS] + ["ho"])
-
-
-def _blocks(t):
-    out, a = [], 0
-    for s in PAR["blocks"][:PAR["nblk"][t]]:
-        out.append((a, a + s))
-        a += s
-    return out
+NDMA = 16
+SEMAPHORES = (["cv", "cs", "cp", "cg", "ho"] + ["d%d" % i for i in range(NDMA)]
+              + ["%s%d" % (s, t) for s in ("arr", "out") for t in range(RO)]
+              + ["%s%d%s" % (s, t, w) for s in ("fo", "fa", "fb") for t in range(RO) for w in "ZY"])
+CYC, PECYC = 0.83e-3, 0.42e-3
 
 
 def _helpers(core, T, topo):
@@ -92,69 +83,93 @@ def _plan(g, core, T, topo, rank):
 
     def ap(name, a, b, step=1):
         v = T[name][:, a:b] if step == 1 else T[name][:, a:b:step]
-        return (v, [(name, a, b)])
+        return (v, [(name, a, b, step == 1)], (b - a + step - 1) // step)
 
     def ind(win, off):
-        return (win[0].indirect(off[0]), win[1] + off[1])
+        return (win[0].indirect(off[0]), win[1] + off[1], 16 * off[2])
 
-    def add(q, fn, r, w, tok=None):
-        ops.append({"q": q, "fn": fn, "r": r, "w": w, "tok": tok})
+    def add(q, fn, r, w, cost, **more):
+        o = {"q": q, "fn": fn, "r": r, "w": w, "cost": cost, "tok": None, "lat": 0.0, "dma": 0.0}
+        o.update(more)
+        ops.append(o)
+        return len(ops) - 1
 
     def col(x):
         return (x[0], x[1]) if isinstance(x, tuple) else (x, [])
 
-    def tt(out, a, b, op):
-        add("v", lambda: V.tensor_tensor(out[0], a[0], b[0], op), a[1] + b[1], out[1])
+    def kind(x):
+        return SCRATCH[x[1][0][0]]
+
+    def price(out, *ins):
+        if len(out[1]) > 1:
+            return 0.05 + 3.0 * CYC * out[2]
+        if len(ins[0][1]) > 1:
+            return 0.06 + PAR["gam"] * CYC * out[2]
+        half = all(kind(x)[2] in ("bfloat16", "float16", "uint16") for x in (out,) + ins)
+        return 0.01 + CYC * max(64, out[2] * (0.5 if half else 1))
+
+    def tt(out, a, b, op, **more):
+        c = price(out, a)
+        if len(a[1]) == 1 and kind(a)[0] == kind(b)[0]:
+            c = 0.01 + CYC * max(64, 2 * out[2])
+        add("v", lambda o: V.tensor_tensor(out[0], a[0], b[0], op), a[1] + b[1], out[1], c, **more)
 
     def ts(out, a, s1, op0, s2=None, op1=None):
         c1, r1 = col(s1)
         c2, r2 = col(s2)
         if op1 is None:
-            add("v", lambda: V.tensor_scalar(out[0], a[0], c1, None, op0), a[1] + r1, out[1])
+            add("v", lambda o: V.tensor_scalar(out[0], a[0], c1, None, op0), a[1] + r1, out[1], price(out, a))
         else:
-            add("v", lambda: V.tensor_scalar(out[0], a[0], c1, c2, op0, op1), a[1] + r1 + r2, out[1])
+            add("v", lambda o: V.tensor_scalar(out[0], a[0], c1, c2, op0, op1), a[1] + r1 + r2, out[1], price(out, a))
 
     def cp(out, a):
-        add("v", lambda: V.tensor_copy(out[0], a[0]), a[1] + out[1][1:], out[1][:1])
+        add("v", lambda o: V.tensor_copy(out[0], a[0]), a[1] + out[1][1:],
+            [out[1][0][:3] + (len(out[1]) == 1,)], price(out, a))
 
     def turn(out, a):
-        add("v", lambda: V.transpose(out[0], a[0]), a[1], out[1])
+        add("v", lambda o: V.transpose(out[0], a[0]), a[1], out[1], price(out, a))
 
-    def scan(out, d0, d1, op0, op1):
-        add("v", lambda: V.tensor_tensor_scan(out[0], d0[0], d1[0], 0.0, op0, op1), d0[1] + d1[1], out[1])
+    def scan(out, d0, d1, op0, op1, **more):
+        add("v", lambda o: V.tensor_tensor_scan(out[0], d0[0], d1[0], 0.0, op0, op1), d0[1] + d1[1], out[1],
+            price(out, d0, d1), **more)
 
     def mset(out, c):
-        add("v", lambda: V.memset(out[0], c), [], out[1])
+        add("v", lambda o: V.memset(out[0], c), [], out[1], price(out, out))
 
     def act(out, a, f, bias=0.0, scale=1.0, acc=None):
         cb, rb = col(bias)
         cs, rc = col(scale)
+        c = price(out, a) if len(a[1]) > 1 else 0.01 + CYC * max(64, out[2])
         if acc is None:
-            add("s", lambda: S.activation(out[0], a[0], f, bias=cb, scale=cs), a[1] + rb + rc, out[1])
+            add("s", lambda o: S.activation(out[0], a[0], f, bias=cb, scale=cs), a[1] + rb + rc, out[1], c)
         else:
-            add("s", lambda: S.activation(out[0], a[0], f, bias=cb, scale=cs, accum_out=acc[0]),
-                a[1] + rb + rc, out[1] + acc[1])
+            add("s", lambda o: S.activation(out[0], a[0], f, bias=cb, scale=cs, accum_out=acc[0]),
+                a[1] + rb + rc, out[1] + acc[1], c)
 
-    def mm(out, l, r, start, stop):
-        add("p", lambda: PE.matmul(out[0], l[0], r[0], start, stop), l[1] + r[1], out[1])
+    def mm(out, l, r, start, stop, **more):
+        c = PECYC * max(64, out[2]) * (4 if kind(l)[2] == "float32" else 1)
+        add("p", lambda o: PE.matmul(out[0], l[0], r[0], start, o["stop"]), l[1] + r[1], out[1], c,
+            stop=stop, start=start, **more)
 
     def iota(out, pat, base, cm):
-        if out[1][0][0] == "ci":
-            add("g", lambda: g.iota(out[0], pat, base, cm), [], out[1])
+        c = 0.15 + 2 * CYC * out[2]
+        if kind(out)[2] == "int32":
+            add("g", lambda o: g.iota(out[0], pat, base, cm), [], out[1], c)
         else:
-            add("g", lambda: g.iota(out[0], pat, base, cm, allow_small_or_imprecise_dtypes=True), [], out[1])
+            add("g", lambda o: g.iota(out[0], pat, base, cm, allow_small_or_imprecise_dtypes=True), [], out[1], c)
 
     def sel(out, a, pat, op, base, cm):
-        add("g", lambda: g.affine_select(out[0], a[0], pat, op, 0.0, base, cm), a[1], out[1])
+        add("g", lambda o: g.affine_select(out[0], a[0], pat, op, 0.0, base, cm), a[1], out[1], 0.17 + 2 * CYC * out[2])
 
-    def dma(q, out, a):
+    def dma(q, out, a, tie=()):
         name = "d%d" % ndma[0]
         ndma[0] += 1
         eng = g.sync if q == "y" else S
-        add(q, lambda: eng.dma_start(out[0], a[0]).then_inc(T.sem[name], 16), a[1], out[1], (name, 16))
+        add(q, lambda o: eng.dma_start(out[0], a[0]).then_inc(T.sem[name], 16), a[1], out[1] + list(tie), 0.1,
+            tok=(name, 16), lat=1.3, dma=0.2 + 0.0015 * out[2])
 
     def hbm(name, a, b):
-        return (T[name][:, a:b], [])
+        return (T[name][:, a:b], [], b - a)
 
     Wn = ["W0", "W1", "W2", "W3", "W0"]
     Ln = ["La", "Lc", "La", "Lc", "La"]
@@ -174,7 +189,7 @@ def _plan(g, core, T, topo, rank):
     def send(t):
         src = ap(Wn[t], GH, GH + 256)
 
-        def fn():
+        def fn(o):
             tr = []
             for d in range(2):
                 rid, pid = topo.addr(dsts[d], core)
@@ -182,30 +197,26 @@ def _plan(g, core, T, topo, rank):
                                             remote_sem=T.sem["arr%d" % t], src=src[0],
                                             dst=T[Wn[t]][:, 256 * d:256 * d + 256]))
             g.remote_dma_fused(tr, local_sem=T.sem["out%d" % t])
-        add("g", fn, src[1], [], ("out%d" % t, 8))
-        add("r", None, [], [(Wn[t], 0, GH)], ("arr%d" % t, 8))
+        i = add("g", fn, src[1], [], 0.5, tok=("out%d" % t, 8), lat=PAR["ghost"][min(t, 1)] - 0.5)
+        add("r", None, [], [(Wn[t], 0, GH, True)], 0.3, tok=("arr%d" % t, 8), src=i)
 
     helper = _helpers(core, T, topo)
 
-    def fold(t, i):
-        a, b = blk[t][i]
-        n = b - a
-        eng = topo.engines(core, helper["Z"])[:PAR["feng"]]
-        calls = [("Z",), ("Y",)] if PAR["split"] else [("Z", "Y")]
-        for call in calls:
-            def fn(call=call):
-                tr = []
-                for j, w in enumerate(call):
-                    rid, pid = topo.addr(helper[w], core)
-                    tr.append(RemoteDMATransfer(
-                        dst_ids=[DstId(rid=rid, pnc=pid)], dma_engine_mask=_mask(eng[j::len(call)]),
-                        remote_sem=T.sem["fa%d%d%s" % (t, i, w)],
-                        srcs=[T.P[:, 16 * a + k * n:16 * a + (k + 1) * n] for k in range(16)],
-                        dst=T.P[:, MM * t + a:MM * t + b], alu_op=3 if w == "Z" else 2))
-                g.remote_dma_fused(tr, local_sem=T.sem["fo%d%d%s" % (t, i, call[0])])
-            add("g", fn, [("P", 16 * a, 16 * b)], [], ("fo%d%d%s" % (t, i, call[0]), len(eng)))
+    def fold(t):
+        m = M[t]
         for w in "ZY":
-            add("r", None, [], [(w, a, b)], ("fb%d%d%s" % (t, i, w), PAR["heng"]))
+            eng = topo.engines(core, helper[w])
+
+            def fn(o, w=w, eng=eng):
+                rid, pid = topo.addr(helper[w], core)
+                tr = RemoteDMATransfer(dst_ids=[DstId(rid=rid, pnc=pid)], dma_engine_mask=_mask(eng),
+                                       remote_sem=T.sem["fa%d%s" % (t, w)],
+                                       srcs=[T.P[:, k * m:(k + 1) * m] for k in range(16)],
+                                       dst=T.P[:, MM * t:MM * t + m], alu_op=3 if w == "Z" else 2)
+                g.remote_dma_fused([tr], local_sem=T.sem["fo%d%s" % (t, w)])
+            i = add("g", fn, [("P", 0, 16 * m, True), ("tie", t, t + 1, True)], [], 0.5,
+                    tok=("fo%d%s" % (t, w), len(eng)), lat=0.7 if t else 1.3, dma=PAR["fold"] * m, chain="fold")
+            add("r", None, [], [(w, 0, m, True)], PAR["back"][min(t, 1)], tok=("fb%d%s" % (t, w), PAR["heng"]), src=i)
 
     def bounds(sizes, a=0):
         out = []
@@ -214,14 +225,14 @@ def _plan(g, core, T, topo, rank):
             a += s
         return out
 
-    blk = [_blocks(t) for t in range(RO)]
-    M = [blk[t][-1][1] for t in range(RO)] + [0]
+    M = PAR["m"] + [0]
     nch = [bounds(PAR["nch"][t], M[t]) for t in range(RO)]
     cut = [nch[t][PAR["ncut"][t] - 1][1] for t in range(RO)]
     late = [nch[t][-1][0] for t in range(RO)]
     rng = [[(0, M[t]), (M[t], cut[t]), (cut[t], BASE[t])] for t in range(RO)]
     for t in range(RO):
         assert nch[t][-1][1] == BASE[t] and cut[t] <= 512 and BASE[t] - cut[t] <= 512 and late[t] - M[t] <= 512
+        assert M[t + 1] <= cut[t] and M[t] + BASE[t] - late[t] <= 512 and len(nch[t]) > 1
 
     def xcol(t, a, b):
         return ap("xp", a, b) if b <= cut[t] else ap("xp", 512 + a - cut[t], 512 + b - cut[t])
@@ -241,42 +252,27 @@ def _plan(g, core, T, topo, rank):
     def dbc(a, b):
         return ap("db", PAD + a, PAD + b)
 
-    def pieces(t, r):
-        return [(a, b, True) for a, b in blk[t]] if r == 0 else [rng[t][r] + (False,)]
-
-    def link(name, a, b, k, major):
-        if major:
-            return ap(name, 16 * a + k * (b - a), 16 * a + (k + 1) * (b - a))
+    def link(name, r, a, b, k):
+        if r == 0:
+            return ap(name, k * b, (k + 1) * b)
         return ap(name, 16 * a + k, 16 * b, 16)
 
-    def gather(t, a, b, vec=False):
-        src = ind(ap(Wn[t], 0, GH + BASE[t]), ap(On[t], a, b))
-        if vec:
-            cp(ap("P", 16 * a, 16 * b), src)
-        else:
-            act(ap("P", 16 * a, 16 * b), src, AF.Copy)
+    def gather(name, t, a, b, q):
+        win = Wn[t] if name == "P" else Ln[t]
+        src = ind(ap(win, 0, GH + BASE[t]), ap(On[t], a, b))
+        out = ap(name, 16 * a, 16 * b)
+        sign = 1.0 if name == "P" else -1.0
+        if q == "v":
+            return V.tensor_scalar(out[0], src[0], sign, None, A.mult)
+        return S.activation(out[0], src[0], AF.Copy, bias=0.0, scale=sign)
 
-    qleft = [[[0, BASE[t]]] for t in range(RO)]
-    qleft[0] = [[M[0], L0N], [0, M[0]]]
-
-    def gather2(t, cells, vec=False):
-        while cells > 0 and qleft[t]:
-            a = qleft[t][0][0]
-            b = min(qleft[t][0][1], a + cells, a + 256)
-            cells -= b - a
-            qleft[t][0][0] = b
-            if b == qleft[t][0][1]:
-                qleft[t].pop(0)
-            src = ind(ap(Ln[t], 0, GH + BASE[t]), ap(On[t], a, b))
-            if vec:
-                ts(ap("Q", 16 * a, 16 * b), src, -1.0, A.mult)
-            else:
-                act(ap("Q", 16 * a, 16 * b), src, AF.Copy, scale=-1.0)
-
-    def gather2_upto(t, r):
-        while any(a < rng[t][r][1] and b > rng[t][r][0] for a, b in qleft[t]):
-            a, b = qleft[t][0]
-            gather2(t, min(256, (rng[t][r][1] if a < rng[t][r][1] else b) - a, b - a))
+    def stream(name, t, parts):
+        for a0, b0 in parts:
+            for a in range(a0, b0, UNIT):
+                b = min(a + UNIT, b0)
+                win = Wn[t] if name == "P" else Ln[t]
+                add("vs", gather, ap(win, 0, GH + BASE[t])[1] + ap(On[t], a, b)[1], ap(name, 16 * a, 16 * b)[1],
+                    PAR["gam"] * CYC * 16 * (b - a), unit=(name, t, a, b), chain=name)
 
     def copy_x(t, bank):
         a, b = ((0, cut[t]), (cut[t], BASE[t]))[bank]
@@ -287,25 +283,29 @@ def _plan(g, core, T, topo, rank):
 
     def s_min(a, b):
         n = 16 * (b - a)
-        scan(ap("SN", 0, n), ap("m2", 0, n), ap("P", 16 * a, 16 * b), A.add, A.min)
+        scan(ap("SN", 0, n), ap("m2", 0, n), ap("P", 16 * a, 16 * b), A.add, A.min, chain="scan")
 
     def s_max(t, a, b):
         n = 16 * (b - a)
-        scan(ap("SX", 0, n), ap("m1", 0, n), ap("P", 16 * a, 16 * b), A.mult, A.max)
+        scan(ap("SX", 0, n), ap("m1", 0, n), ap("P", 16 * a, 16 * b), A.mult, A.max, chain="scan")
         mm(scol(t, a, b), ap("Iq", 0, 128), ap("SX", 15, n, 16), False, False)
 
     def u_a(t, a, b):
         z = ap("Z", a, b) if b <= M[t] else ap("SN", 15, 16 * (b - a), 16)
         tt(ap("ab", a, b), z, xcol(t, a, b), A.mult)
 
-    def u_b(a, b, on_s=True):
-        if on_s:
-            act(ap("ab", a, b), ap("ab", a, b), AF.Copy, scale=-0.75)
+    def scaled(what, t, out, a, c):
+        if PAR[what][t] == "s":
+            act(out, a, AF.Copy, scale=c)
         else:
-            ts(ap("ab", a, b), ap("ab", a, b), -0.75, A.mult)
+            ts(out, a, c, A.mult)
 
-    def u_d(t, a, b):
-        mm(scol(t, a, b), ap("I1", 0, 128), ap("ab", a, b), False, True)
+    def u_d(what, t, a, b):
+        if PAR["peb"]:
+            mm(scol(t, a, b), ap("Ib", 0, 128), ap("ab", a, b), False, True)
+        else:
+            scaled(what, t, ap("ab", a, b), ap("ab", a, b), -0.75)
+            mm(scol(t, a, b), ap("I1", 0, 128), ap("ab", a, b), False, True)
 
     def u_flag(t, a, b):
         act(ap("fl", a, b), scol(t, a, b), AF.Sign, bias=-(3.5 + 2.0 ** -22), scale=3.5)
@@ -319,25 +319,23 @@ def _plan(g, core, T, topo, rank):
     def u_clip(t, a, b):
         ts(own(Wn[t + 1], a, b), scol(t, a, b), 0.0, A.max, 2.0, A.min)
 
-    opened = {}
-
-    def first(t, r):
-        f = (t, r) not in opened
-        opened[t, r] = opened.get((t, r), 0) + 1
-        return f, opened[t, r] == 16 + 16 * len(pieces(t, r))
-
     def l_cmp(t, r, k):
-        a0 = rng[t][r][0]
-        for a, b, major in pieces(t, r):
-            tt(ap("F", 512 * k + a - a0, 512 * k + b - a0), link("P", a, b, k, major), xcol(t, a, b), A.is_gt)
         a, b = rng[t][r]
-        mm(qcol(t, r, a, b), ap("Bm", 16 - k, 144 - k), ap("F", 512 * k, 512 * k + b - a), *first(t, r))
+        f = ap("F", 512 * k, 512 * k + b - a)
+        if t == 0 and r == 0 and k < PAR["early"]:
+            c = b // 16
+            tt(f, ind(own("W0", 0, L0N), ap("off1", k * c, k * c + c)), own("W0", a, b), A.is_gt)
+        else:
+            tt(f, link("P", r, a, b, k), xcol(t, a, b), A.is_gt, chain="cmp")
+        mm(qcol(t, r, a, b), ap("Bm", 16 - k, 144 - k), f, k == 0, False, grp=(t, r))
 
     def l_diag(t, r):
-        gather2_upto(t, r)
-        for k in range(16):
-            for a, b, major in pieces(t, r):
-                mm(qcol(t, r, a, b), ap("Dm", 128 * k, 128 * k + 128), link("Q", a, b, k, major), *first(t, r))
+        a0, b0 = rng[t][r]
+        w = b0 if r == 0 else PAR["dw"]
+        for a in range(a0, b0, w):
+            b = min(a + w, b0)
+            for k in range(16):
+                mm(qcol(t, r, a, b), ap("Dm", 128 * k, 128 * k + 128), link("Q", r, a, b, k), False, False, grp=(t, r))
 
     def l_y(t, r):
         a, b = rng[t][r]
@@ -352,320 +350,381 @@ def _plan(g, core, T, topo, rank):
         if a < b:
             act(ap(On[t + 1], a, b), dbc(a, b), AF.Abs)
 
-    def l_turn(t, name, o):
-        turn(ap("TT", 0, M[t]), ap(name, o, o + M[t]))
-        turn(ap("TT", MM, MM + M[t] + 32), ap(name, o - 16, o + M[t] + 16))
+    lso = {}
+    for m in sorted(set(M[:RO])):
+        lso[m] = sum(lso) // 16
 
-    def l_list(t):
-        act(ap(On[t], 0, M[t]), ind(ap("TT", 0, MM + M[t] + 32), ap("lst", 0, M[t] // 16)), AF.Abs)
-
-    def folds(t):
-        for i, (a, b) in enumerate(blk[t]):
-            h = b - (PAR["fv"][t] if i == 0 else 0)
-            if h > a:
-                gather(t, a, h)
-            if h < b:
-                gather(t, h, b, True)
-            fold(t, i)
+    def l_list(t, name, o):
+        m = M[t]
+        turn(ap("TT", 0, m), ap(name, o, o + m))
+        turn(ap("TT", m, 2 * m + 32), ap(name, o - 16, o + m + 16))
+        act(ap(On[t], 0, m), ind(ap("TT", 0, 2 * m + 32), ap("lst", lso[m], lso[m] + m // 16)), AF.Abs)
 
     dma("y", own("W0", 0, 256), hbm("x0", 0, 256))
     dma("s", ap("nbi", 0, L0N), hbm("nb", 0, L0N))
     dma("y", own("W0", 256, L0N), hbm("x0", 256, L0N))
+    send(0)
     iota(ap("ci", 0, 1), [[0, 1]], 0, 1)
-    iota(ap("La", 0, GH), [[1, GH]], 0, 0)
-    allb = bounds(PAR["blocks"][:max(PAR["nblk"])])
-    for a, b in allb:
-        c = (b - a) // 16
-        iota(ap("lsf", a // 16, b // 16), [[16 // c, c]], a, 0)
-    mset(ap("m1", 0, 2048), 1.0)
     ts(ap("ci", 1, 2), ap("ci", 0, 1), 15, A.bitwise_and)
     ts(ap("ci", 2, 3), ap("ci", 0, 1), 4, A.logical_shift_right)
-    mset(ap("m2", 0, 2048), 0.0)
     tt(ap("ci", 3, 4), ap("ci", 0, 1), ap("ci", 2, 3), A.add)
-    mset(ap("m1", 0, 2048, 16), 0.0)
     ts(ap("ci", 3, 4), ap("ci", 3, 4), 1, A.bitwise_and)
-    mset(ap("m2", 0, 2048, 16), 4.0)
-    for j, (a, b) in enumerate(allb):
-        c = (b - a) // 16
-        ts(ap("ci", 4 + 2 * j, 5 + 2 * j), ap("ci", 0, 1), c - 1, A.bitwise_and)
-        ts(ap("ci", 5 + 2 * j, 6 + 2 * j), ap("ci", 1, 2), c.bit_length() - 1, A.logical_shift_right)
-    mset(ap("n2", 0, 1), 2.0 * (GH + L0N))
-    cp(ap("cf", 0, 4 + 2 * len(allb)), ap("ci", 0, 4 + 2 * len(allb)))
-    mset(ap("TT", 0, 2 * MM + 32), 0.0)
-    for j, (a, b) in enumerate(allb):
-        f = ap("cf", 4 + 2 * j, 5 + 2 * j)
-        ts(f, f, 16.0, A.mult, ap("cf", 5 + 2 * j, 6 + 2 * j), A.add)
-    mset(ap("db", 0, PAD + MM + 16), 0.0)
-    for j, (a, b) in enumerate(allb):
-        ts(ap("cf", 5 + 2 * j, 6 + 2 * j), ap("cf", 3, 4), MM + 16.0, A.mult, ap("cf", 4 + 2 * j, 5 + 2 * j), A.add)
-    mset(ap("rs", L0N, LM), -1.0)
-    for j, (a, b) in enumerate(allb):
-        ts(ap("lst", a // 16, b // 16), ap("lsf", a // 16, b // 16), ap("cf", 5 + 2 * j, 6 + 2 * j), A.add)
-    send(0)
-    dma("y", ap("m1", 2048, 4096), ap("m1", 0, 2048))
-    dma("y", ap("m2", 2048, 4096), ap("m2", 0, 2048))
+    cp(ap("cf", 0, 4), ap("ci", 0, 4))
+    nl = sum(lso) // 16
+    for m in lso:
+        iota(ap("lsj", lso[m], lso[m] + m // 16), [[16, m // 16]], 0, 0)
+    ts(ap("lsj", 0, nl), ap("lsj", 0, nl), ap("cf", 1, 2), A.add)
+    for j, m in enumerate(lso):
+        c, o = m // 16, lso[m]
+        ts(ap("lsk", o, o + c), ap("lsj", o, o + c), 1.0 / c, A.mult, 0.5 / c - 0.5, A.add)
+        ts(ap("cf", 4 + j, 5 + j), ap("cf", 3, 4), m + 16.0, A.mult)
+        ts(ap("lsf", o, o + c), ap("lsk", o, o + c), 1.0 - m, A.mult, ap("cf", 4 + j, 5 + j), A.add)
+    ts(ap("lsj", 0, nl), ap("lsj", 0, nl), 16.0, A.mult)
+    tt(ap("lsf", 0, nl), ap("lsf", 0, nl), ap("lsj", 0, nl), A.add)
+    cp(ap("lst", 0, nl), ap("lsf", 0, nl))
+    iota(ap("La", 0, GH), [[1, GH]], 0, 0)
+    iota(own("La", L0N, LM), [[1, LM - L0N]], GH + L0N, 0)
     cp(ap("off0", M[0], L0N), ap("nbi", M[0], L0N))
     cp(own("La", 0, L0N), ap("nbi", 0, L0N))
-    l_turn(0, "La", GH)
-    for j, cells in enumerate(PAR["qs0"]):
-        gather2(0, cells)
-        if j == 0:
-            l_list(0)
-    iota(ap("I1", 0, 128), [[0, 128]], 1, 0)
-    sel(ap("I1", 0, 128), ap("I1", 0, 128), [[-1, 128]], A.is_equal, 0, 1)
-    iota(ap("Am", 0, 144), [[1, 144]], -16, 0)
+    l_list(0, "La", GH)
+    if PAR["early"]:
+        ts(ap("off1", 0, M[0]), ap("off0", 0, M[0]), float(-GH), A.add)
+    mset(ap("ones", 0, LM), 1.0)
+    mset(ap("db", 0, PAD), 0.0)
+    mset(dbc(M[1], M[1] + 16), 0.0)
+    mset(ap("n2", 0, 1), 2.0 * (GH + L0N))
+    mset(ap("rs", L0N, LM), -1.0)
+    mw = PAR["mw"]
+    mset(ap("m1", 0, mw), 1.0)
+    mset(ap("m2", 0, mw), 0.0)
+    mset(ap("m1", 0, mw, 16), 0.0)
+    mset(ap("m2", 0, mw, 16), 4.0)
+    for w in range(mw, 4096, mw):
+        dma("y", ap("m2", w, w + mw), ap("m2", 0, mw))
+        dma("y", ap("m1", w, w + mw), ap("m1", 0, mw))
+    iota(ap("Bi", 0, 144), [[1, 144]], -16, 0)
     iota(ap("mk6", 0, 8), [[1, 8]], 0, 0)
     iota(ap("ew2", 0, 8), [[32, 8]], -2 * (GH + L0N), 0)
+    iota(ap("Am", 0, 128), [[0, 8], [1, 16]], 0, 0)
+    iota(ap("I1", 0, 128), [[0, 128]], 1, 0)
+    sel(ap("I1", 0, 128), ap("I1", 0, 128), [[-1, 128]], A.is_equal, 0, 1)
     iota(ap("cf", 8, 9), [[0, 1]], 1, 2)
     iota(ap("e2", 0, CAP), [[2, CAP]], 0, 0)
-    iota(ap("ones", 0, LM), [[0, LM]], 1, 0)
-    ts(ap("cf", 9, 11), ap("cf", 1, 3), 2.0, A.mult)
-    ts(ap("Iq", 0, 128), ap("I1", 0, 128), 0.25, A.mult)
-    ts(ap("cf", 10, 11), ap("cf", 10, 11), 8.0, A.mult)
+    ts(ap("cf", 9, 10), ap("cf", 1, 2), 2.0, A.mult)
+    ts(ap("cf", 10, 11), ap("cf", 2, 3), 16.0, A.mult)
+    ts(ap("Bm", 0, 144), ap("Bi", 0, 144), ap("cf", 10, 11), A.is_equal, float(BIG), A.mult)
     ts(ap("sX", 0, 4), ap("mk6", 0, 4), ap("cf", 1, 2), A.is_equal)
-    ts(ap("Bm", 0, 144), ap("Am", 0, 144), ap("cf", 10, 11), A.is_equal, float(BIG), A.mult)
-    iota(ap("Am", 0, 128), [[0, 8], [1, 16]], 0, 0)
     ts(ap("mk6", 0, 8), ap("mk6", 0, 8), ap("cf", 2, 3), A.is_equal)
     ts(ap("sR", 0, 4), ap("sX", 0, 4), -2.5, A.mult, 2.0, A.add)
     ts(ap("ew2", 0, 8), ap("ew2", 0, 8), ap("cf", 9, 10), A.add)
     ts(ap("sX", 0, 4), ap("sX", 0, 4), -3.0, A.mult, 4.0, A.add)
     ts(ap("Am", 0, 128), ap("Am", 0, 128), ap("cf", 1, 2), A.is_equal)
-    copy_x(0, 0)
-    copy_x(0, 1)
-    for a, b in ((M[0], late[0]), (0, M[0]), (late[0], L0N)):
-        start_s(0, a, b)
-    for cells in PAR["qv0"]:
-        gather2(0, cells, True)
-    iota(own("La", L0N, LM), [[1, LM - L0N]], GH + L0N, 0)
-    dma("y", ap("Lb", 0, BASE[1]), own("La", 0, BASE[1]))
-    for h in range(2):
-        sel(ap("Dm", 1024 * h, 1024 * h + 1024), ap("ones", 0, 1024), [[-256, 8], [16, 8], [257, 16]], A.is_equal,
-            -2048 * h, -1)
-    folds(0)
+    scaled("e_c0", 2, ap("Iq", 0, 128), ap("I1", 0, 128), 0.25)
+    if PAR["peb"]:
+        scaled("e_c0", 2, ap("Ib", 0, 128), ap("I1", 0, 128), -0.75)
+    for h in range(4):
+        sel(ap("Dm", 512 * h, 512 * h + 512), ap("ones", 0, 512), [[-256, 4], [16, 8], [257, 16]], A.is_equal,
+            -1024 * h, -1)
     for t in range(RO):
         iota(own(Wn[t + 1], BASE[t], BASE[t + 1]), [[0, CAP]], 0, 0)
-    iota(ap("IOT", 0, LM), [[1, LM]], GH, 0)
+    for h in range(2):
+        iota(ap("IOT", 512 * h, 512 * h + 512), [[1, 512]], GH + 512 * h, 0)
     iota(ap("Lc", 0, GH), [[1, GH]], 0, 0)
     iota(own("Lc", L0N, LM), [[1, LM - L0N]], GH + L0N, 0)
 
     offm, offc = ap("offm", 0, 6), ap("offc", 0, 6)
-    fills = PAR["fill"]
-
-    def child_gather(t):
-        tt(ap("CL", 0, CAP), ind(own(Ln[t + 1], 0, BASE[t + 1]), offm), ap("X1", 0, CAP), A.min)
-
-    def child_put(t):
-        if t == 0:
-            cp(own(Ln[1], L0N, BASE[1]), ap("CL", 0, CAP))
-        else:
-            cp(ind(own(Ln[t + 1], L0N, BASE[t + 1]), offc), ap("CL", 0, CAP))
-
     for t in range(RO):
         n, nn, m, lt = BASE[t], BASE[t + 1], M[t], late[t]
         last = t == RO - 1
-        W1 = Wn[t + 1]
+        W1, L1 = Wn[t + 1], Ln[t + 1]
         ch = nch[t]
-        nv = PAR["nv"][t]
-        q = PAR["q"][t]
         n2 = ap("n2", t, t + 1)
-        todo = [(r, k) for r in range(3) for k in range(16)]
-
-        def fill(cnt, upto=2):
-            while cnt > 0 and todo and todo[0][0] < upto:
-                r, k = todo.pop(0)
-                l_cmp(t, r, k)
-                cnt -= 1
-        gathered = [0]
-
-        def gathers(upto):
-            for c in range(max(nv, gathered[0]), len(ch)):
-                if ch[c][1] <= upto:
-                    gather(t, *ch[c])
-                    gathered[0] = c + 1
-        if nv > 0:
-            gather(t, *ch[0], True)
+        if t == 0:
+            stream("Q", t, [(m, PAR["q0"])])
+        stream("P", t, [(0, m)] + ch)
+        fold(t)
+        dma("y", ap("Lb", 0, nn), own(Ln[t], 0, nn), [("tie", t, t + 1, True)])
+        stream("Q", t, [(0, m), (PAR["q0"], n)] if t == 0 else rng[t])
+        copy_x(t, 0)
+        copy_x(t, 1)
+        for a, b in ((m, lt), (0, m), (lt, n)):
+            start_s(t, a, b)
+        ts(ap("cc", 0, 1), ap("cf", 8, 9), n2, A.add, float(-1 - nn - 2 * GH), A.add)
+        ts(ap("RV", 0, CAP), ap("e2", 0, CAP), n2, A.add, ap("sR", t, t + 1), A.mult)
         if t > 0:
-            gathers(cut[t - 1])
-            l_y(t - 1, 2)
-            l_off(t - 1, 2)
-            l_abs(t - 1, 2)
-        gathers(L0N)
-        fill(PAR["fa"][t][0])
-        for c, (a, b) in enumerate(ch):
-            if 0 < c < nv:
-                gather(t, a, b, True)
+            ts(offc, ap("ew2", 0, 6), n2, A.add, 0.5, A.mult)
+        for a, b in ch:
             s_min(a, b)
-            if c == 0:
-                ts(ap("cc", 0, 1), ap("cf", 8, 9), n2, A.add, float(-1 - nn - 2 * GH), A.add)
-                ts(ap("RV", 0, CAP), ap("e2", 0, CAP), n2, A.add, ap("sR", t, t + 1), A.mult)
-                if t > 0:
-                    child_gather(t - 1)
             u_a(t, a, b)
-            if c == 0 and t > 0:
-                child_put(t - 1)
-            if c == len(ch) - 2:
-                gather2(t, q[0])
-                u_b(m, lt)
-            if c == len(ch) - 1 and PAR["b_last_v"]:
-                u_b(a, b, False)
             s_max(t, a, b)
-            if c == 0 and t > 0:
-                cp(ap(On[t], L0N, n), own(Ln[t], L0N, n))
-                ts(offc, ap("ew2", 0, 6), n2, A.add, 0.5, A.mult)
-                gathers(n)
-                dma("y", ap("Lb", 0, nn), own(Ln[t], 0, nn))
-            if c == len(ch) - 2:
-                u_d(t, m, lt)
+            if b == lt:
+                u_d("e_b0", t, m, lt)
                 u_flag(t, m, lt)
                 vote(m, lt, 0)
-                gather2(t, q[1])
                 ready(m, lt, 0)
-        if not PAR["b_last_v"]:
-            u_b(lt, n)
-        u_d(t, lt, n)
+                u_clip(t, m, lt)
+        u_d("e_b1", t, lt, n)
         u_flag(t, lt, n)
-        u_clip(t, m, lt)
-        fill(PAR["fa"][t][1])
-        gather2(t, q[6])
-        for a, b in blk[t]:
-            u_a(t, a, b)
-            mm(scol(t, a, b), ap("Iq", 0, 128), ap("Y", a, b), False, False)
-        u_b(0, m)
-        u_d(t, 0, m)
-        vote(lt, n, m)
-        fill(fills[0])
-        u_clip(t, lt, n)
+        u_a(t, 0, m)
+        mm(scol(t, 0, m), ap("Iq", 0, 128), ap("Y", 0, m), False, False)
+        u_d("e_b2", t, 0, m)
         u_flag(t, 0, m)
+        vote(lt, n, m)
         vote(0, m, 0)
-        fill(fills[1])
+        u_clip(t, lt, n)
         u_clip(t, 0, m)
         ready(lt, n, m)
         ready(0, m, 0)
-        fill(fills[2])
         scan(ap("cum", 0, nn), ap("rs", 0, nn), ap("ones", 0, nn), A.add, A.add)
-        gather2(t, q[2])
         act(ap("fl", 0, nn), ap("cum", 0, nn), AF.Sign, bias=ap("cf", 8, 9), scale=-1.0, acc=ap("acc", 0, 1))
-        gather2(t, q[3])
-        fill(fills[3])
         ts(ap("B6", 0, 6), ap("mk6", 0, 6), ap("acc", 0, 1), A.mult, ap("cc", 0, 1), A.min)
         mm(ap("vo", 496, 502), ap("Am", 0, 128), ap("B6", 0, 6), True, True)
-        fill(fills[4])
         ts(offm, ap("vo", 496, 502), 0.5, A.mult, nn / 2.0, A.add)
-        fill(fills[5])
-        ts(ap("Cx", 0, CAP), ind(own(W1, 0, nn), offm), 0.5, A.mult)
-        tt(ap("LS", 0, CAP), ind(own(Ln[t], 0, nn), offm), ap("RV", 0, CAP), A.min)
+        scaled("e_cx", t, ap("Cx", 0, CAP), ind(own(W1, 0, nn), offm), 0.5)
         cp(ind(own(W1, 0, nn), offm), ap("Cx", 0, CAP))
         if t == 0:
-            cp(own(W1, L0N, nn), ap("Cx", 0, CAP))
+            scaled("e_c0", 0, own(W1, L0N, nn), ap("Cx", 0, CAP), 1.0)
         else:
             cp(ind(own(W1, L0N, nn), offc), ap("Cx", 0, CAP))
         if last:
             dma("y", hbm("yx", 0, LM), own(W1, 0, LM))
         else:
             send(t + 1)
+        tt(ap("LS", 0, CAP), ind(own(Ln[t], 0, nn), offm), ap("RV", 0, CAP), A.min)
         cp(ind(ap("Lb", 0, nn), offm), ap("LS", 0, CAP))
         ts(ap("n2", t + 1, t + 2), ap("cum", n - 1, n), 2.0 * CAP, A.min, n2, A.add)
-        l_diag(t, 0)
-        fill(16, 1)
-        gather2(t, q[4])
-        fill(fills[6])
-        if last:
-            ts(ap("se", 0, LM - L0N), ap("IOT", L0N, LM), 2.0, A.mult, ap("n2", RO, RO + 1), A.is_lt)
-        l_y(t, 0)
-        turn_after = 0 if M[t + 1] <= m else 1
-        if not last and turn_after == 0:
-            l_turn(t + 1, "db", PAD)
-        l_off(t, 0) if not last else None
-        l_abs(t, 0)
         act(ap("X1", 0, CAP), ind(ap("IOT", 0, nn), offm), AF.Copy, scale=ap("sX", t, t + 1))
-        fill(16, 2)
-        l_diag(t, 1)
-        gather2(t, q[5])
-        fill(fills[8], 3)
-        l_y(t, 1)
+        for r in range(3):
+            for k in range(16):
+                l_cmp(t, r, k)
+            l_diag(t, r)
+            l_y(t, r)
+            if not last:
+                l_off(t, r)
+                if r == (0 if M[t + 1] <= m else 1):
+                    l_list(t + 1, "db", PAD)
+            l_abs(t, r)
+            if last and r == 1:
+                dma("y", hbm("yn", 0, cut[t]), own(L1, 0, cut[t]))
+        tt(ap("CL", 0, CAP), ind(own(L1, 0, nn), offm), ap("X1", 0, CAP), A.min)
+        if t == 0:
+            scaled("e_c0", 1, own(L1, L0N, nn), ap("CL", 0, CAP), 1.0)
+        else:
+            cp(ind(own(L1, L0N, nn), offc), ap("CL", 0, CAP))
         if not last:
-            l_off(t, 1)
-            if turn_after == 1:
-                l_turn(t + 1, "db", PAD)
-            l_list(t + 1)
-        l_abs(t, 1)
-        if last:
-            dma("y", hbm("yn", 0, cut[t]), own(Ln[t + 1], 0, cut[t]))
-        fill(PAR["xk"], 3)
-        if not last:
-            copy_x(t + 1, 0)
-            for a, b in ((M[t + 1], late[t + 1]), (0, M[t + 1]), (late[t + 1], nn)):
-                start_s(t + 1, a, b)
-        fill(16, 3)
-        l_diag(t, 2)
-        if not last:
-            copy_x(t + 1, 1)
-            folds(t + 1)
-    l_y(RO - 1, 2)
-    l_abs(RO - 1, 2)
-    child_gather(RO - 1)
-    child_put(RO - 1)
+            scaled("e_oc", t, ap(On[t + 1], L0N, nn), own(L1, L0N, nn), 1.0)
+    ts(ap("se", 0, LM - L0N), ap("IOT", L0N, LM), 2.0, A.mult, ap("n2", RO, RO + 1), A.is_lt)
     tail = own(Ln[RO], L0N, LM)
     tt(tail, tail, ap("se", 0, LM - L0N), A.mult)
     dma("y", hbm("yn", cut[RO - 1], LM), own(Ln[RO], cut[RO - 1], LM))
     return ops
 
 
-def _meet(x, y):
-    return x[0] == y[0] and x[1] < y[2] and y[1] < x[2]
+def _deps(ops):
+    hist, bank, deps = {}, {}, []
+    for i, o in enumerate(ops):
+        d = set()
+        for kind in "rw":
+            for x in o[kind]:
+                for j, kj, y in hist.get(x[0], []):
+                    if (kind == "w" or kj == "w") and x[1] < y[2] and y[1] < x[2]:
+                        if "grp" not in o or o["grp"] != ops[j].get("grp") or ops[j]["start"]:
+                            d.add(j)
+                if x[0] in PSUM:
+                    for b in range(x[1] // 512, (x[2] - 1) // 512 + 1):
+                        q, now, before = bank.get((x[0], b), (None, [], []))
+                        if q != o["q"]:
+                            q, now, before = o["q"], [], now
+                        d.update(before)
+                        now.append(i)
+                        bank[x[0], b] = (q, now, before)
+        for kind in "rw":
+            for x in o[kind]:
+                h = hist.setdefault(x[0], [])
+                if kind == "w" and x[3] and "grp" not in o and o["q"] != "r":
+                    h[:] = [e for e in h if not (x[1] <= e[2][1] and e[2][2] <= x[2])]
+                h.append((i, kind, x))
+        d.discard(i)
+        deps.append({o["src"]} if o["q"] == "r" else d)
+    return deps
 
 
-def _banks(regs):
+def _order(ops):
+    n = len(ops)
+    deps = _deps(ops)
+    wake, beta = PAR["wake"], PAR["beta"]
+    succ = [[] for _ in ops]
+    for i, d in enumerate(deps):
+        for j in d:
+            succ[j].append(i)
+    nxt, prev, seen = {}, {}, {}
+    for i, o in enumerate(ops):
+        if "chain" in o:
+            if o["chain"] in seen:
+                nxt[seen[o["chain"]]] = i
+                prev[i] = seen[o["chain"]]
+            seen[o["chain"]] = i
+    rho = {"P": PAR["rho_p"], "Q": PAR["rho_q"], "scan": PAR["rho_s"], "cmp": PAR["rho_c"]}
+    lane = {"P": "s", "Q": "s", "scan": "v", "cmp": "v", "fold": "d"}
+    tail = [0.0] * n
+    seen = {}
+    for i in range(n - 1, -1, -1):
+        o = ops[i]
+        own = o["cost"] + o["lat"] + o["dma"]
+        tail[i] = own + max([wake + tail[j] for j in succ[i]] + [0.0])
+        if "chain" in o:
+            x = lane[o["chain"]]
+            if x in seen:
+                tail[i] = max(tail[i], rho.get(o["chain"], 1.0) * (o["cost"] + o["dma"]) + tail[seen[x]])
+            seen[x] = i
+    end, when = [None] * n, [None] * n
+    left = [len(d) for d in deps]
+    pool = {q: set() for q in "vspgy"}
+    todo = {q: sorted((i for i in range(n) if q in ops[i]["q"]), key=lambda i: -tail[i]) for q in "vspgy"}
+    free = {q: 0.0 for q in "vspgy"}
+    engines = [0.0]
+    share = {(x, t): PAR["share_" + x][t] for x in "PQ" for t in range(RO)}
     out = []
-    for name, a, b in regs:
-        if name in PSUM:
-            out.append((name, 512 * (a // 512), 512 * ((b - 1) // 512 + 1)))
+
+    def release(i):
+        if ops[i]["q"] == "r":
+            finish(i, end[ops[i]["src"]] + ops[i]["cost"])
+            out.append(([i], "r"))
+        else:
+            when[i] = max([end[j] + wake for j in deps[i]] + [0.0])
+            for q in ops[i]["q"]:
+                pool[q].add(i)
+
+    def finish(i, t):
+        end[i] = t
+        for j in succ[i]:
+            left[j] -= 1
+            if left[j] == 0:
+                release(j)
+
+    def at(i):
+        return when[i]
+
+    def head(i):
+        return "unit" not in ops[i] or i not in prev or end[prev[i]] is not None
+
+    def guess(i, t, memo, depth):
+        if i not in memo:
+            r = 0.0
+            for j in deps[i]:
+                if end[j] is not None:
+                    r = max(r, end[j] + wake)
+                elif depth == 0:
+                    r = 1e9
+                else:
+                    o = ops[j]
+                    s = max(guess(j, t, memo, depth - 1), min(free.get(q, 0.0) for q in o["q"]), t)
+                    r = max(r, s + o["cost"] + o["lat"] + o["dma"] + wake)
+                if r > t + 8.0:
+                    break
+            memo[i] = r
+        return memo[i]
+
+    for i in range(n):
+        if left[i] == 0:
+            release(i)
+    done = 0
+    total = sum(1 for o in ops if o["q"] != "r")
+    while done < total:
+        q = min((x for x in free if todo[x]), key=lambda x: free[x])
+        t = free[q]
+        can = [i for i in pool[q] if head(i) and at(i) <= t + 1e-9 and (
+            q != "v" or "unit" not in ops[i] or share[ops[i]["unit"][:2]] > 0)]
+        can.sort(key=lambda i: -(tail[i] - (PAR["vbias"][ops[i]["unit"][1]] if q == "v" and "unit" in ops[i] else 0.0)
+                                 + (0.0 if "chain" in ops[i] else PAR["small"])))
+        pick = None
+        soon = 1e9
+        if can:
+            memo, k = {}, 0
+            top = tail[can[0]] - (PAR["small"] if "chain" in ops[can[0]] else 0.0)
+            for c in todo[q]:
+                if tail[c] <= top or k == PAR["look"]:
+                    break
+                if end[c] is None and c not in can and ("chain" not in ops[c] or (
+                        "unit" not in ops[c] and tail[c] > tail[can[0]])):
+                    k += 1
+                    soon = min(soon, guess(c, t, memo, 6) + PAR["tol" + q])
+            for i in can:
+                if t + ops[i]["cost"] - soon <= beta * (soon - t):
+                    pick = i
+                    break
+        if pick is None:
+            later = [at(i) for i in pool[q] if head(i) and at(i) > t + 1e-9] + [free[x] for x in free if free[x] > t]
+            free[q] = max(t + 0.02, min(later + [soon, t + 0.3]))
+            continue
+        run = [pick]
+        cost = ops[pick]["cost"]
+        if "unit" in ops[pick]:
+            cost += 0.06
+            most = PAR["run_p" if ops[pick]["chain"] == "P" else "run_q"]
+            if q == "v":
+                most = min(PAR["run_v"], share[ops[pick]["unit"][:2]])
+            while run[-1] in nxt:
+                j = nxt[run[-1]]
+                u, w = ops[run[0]]["unit"], ops[j]["unit"]
+                if (left[j] > 0 or at(j) > t or w[1] != u[1] or w[2] != ops[run[-1]]["unit"][3] or w[3] - u[2] > most
+                        or t + cost + ops[j]["cost"] - soon > beta * ops[j]["cost"] / 2):
+                    break
+                run.append(j)
+                cost += ops[j]["cost"]
+            if q == "v":
+                share[ops[pick]["unit"][:2]] -= ops[run[-1]]["unit"][3] - ops[pick]["unit"][2]
+        free[q] = t + cost
+        e = t + cost + ops[pick]["lat"]
+        if ops[pick]["dma"]:
+            e = engines[0] = max(e, engines[0]) + ops[pick]["dma"]
+        out.append((run, q))
+        for i in run:
+            for x in ops[i]["q"]:
+                pool[x].discard(i)
+            end[i] = e
+        for i in run:
+            finish(i, e)
+            for x in ops[i]["q"]:
+                todo[x].remove(i)
+        done += len(run)
+    return out, max(e for e in end)
+
+
+def _arrange(ops, order):
+    out = []
+    closing = {}
+    for run, q in order:
+        o = ops[run[0]]
+        if "unit" in o:
+            name, t, a, _ = o["unit"]
+            b = ops[run[-1]]["unit"][3]
+            o = {"q": q, "tok": None, "r": [x for i in run for x in ops[i]["r"]], "w": [(name, 16 * a, 16 * b, True)],
+                 "fn": lambda x, f=o["fn"], arg=(name, t, a, b, q): f(*arg)}
+        if "grp" in o:
+            closing[o["grp"]] = o
+        if q == "r":
+            o["src"] = -1
+        out.append(o)
+    for o in closing.values():
+        o["stop"] = True
     return out
 
 
 def _emit(g, T, ops):
     queue = {"v": g.vector, "s": g.scalar, "p": g.tensor, "g": g, "y": g.sync}
     semq = {"v": "cv", "s": "cs", "p": "cp", "g": "cg"}
-    hist = {}
-    deps = []
-    for i, o in enumerate(ops):
-        bk = _banks(o["r"] + o["w"])
-        d = set()
-        for kind, regs in (("r", o["r"]), ("w", o["w"]), ("b", bk)):
-            for x in regs:
-                for j, kj, y in hist.get(x[0], []):
-                    p = ops[j]
-                    same = p["q"] == o["q"] and p["tok"] is None and o["tok"] is None
-                    if kind == "b" or kj == "b":
-                        hit = kind == kj and not same
-                    elif kind == "r" and kj == "r":
-                        hit = False
-                    else:
-                        hit = not (same and o["q"] == "p")
-                    if hit and _meet(x, y):
-                        d.add(j)
-        if o["q"] == "r":
-            d = set()
-        for kind, regs in (("r", o["r"]), ("w", o["w"]), ("b", bk)):
-            for x in regs:
-                hist.setdefault(x[0], []).append((i, kind, x))
-        top = {}
-        keep = []
-        for j in sorted(d):
-            if ops[j]["tok"] is None:
-                top[ops[j]["q"]] = j
-            else:
-                keep.append(j)
-        deps.append(keep + sorted(top.values()))
     known = {q: {} for q in queue}
-    seen = []
-    waits = []
-    needed = set()
-    for i, o in enumerate(ops):
+    seen, waits, needed = [], [], set()
+    for o in ops:
+        o.pop("grp", None)
+    for i, (o, d) in enumerate(zip(ops, _deps(ops))):
         w = []
         if o["q"] != "r":
             kn = known[o["q"]]
-            for j in sorted(deps[i], reverse=True):
+            for j in sorted(d, reverse=True):
+                if o["q"] == "p" and ops[j]["q"] == "p":
+                    continue
                 key = ops[j]["q"] if ops[j]["tok"] is None else ops[j]["tok"][0]
                 if kn.get(key, -1) >= j:
                     continue
@@ -688,10 +747,10 @@ def _emit(g, T, ops):
         for j in waits[i]:
             queue[o["q"]].wait_ge(T.sem[token[j][0]], token[j][1])
         if o["tok"] is not None:
-            o["fn"]()
+            o["fn"](o)
             token[i] = o["tok"]
         else:
-            ins = o["fn"]()
+            ins = o["fn"](o)
             if i in needed:
                 count[o["q"]] += 1
                 token[i] = (semq[o["q"]], count[o["q"]])
@@ -709,16 +768,16 @@ def _hand_back(g, core, T, topo):
             if h != core:
                 continue
             rid, pid = topo.addr(home, core)
-            got = PAR["feng"] if PAR["split"] else PAR["feng"] // 2
             eng = topo.engines(core, home)[:PAR["heng"]]
-            sent = 0
             for t in range(RO):
-                for i, (a, b) in enumerate(_blocks(t)):
-                    g.wait_ge(T.sem["fa%d%d%s" % (t, i, w)], got)
-                    g.remote_dma(T[w][:, a:b], T.P[:, MM * t + a:MM * t + b], T.sem["fb%d%d%s" % (t, i, w)],
-                                 T.sem.ho, pid, rid, _mask(eng))
-                    sent += len(eng)
-            g.wait_ge(T.sem.ho, sent)
+                m = PAR["m"][t]
+                g.wait_ge(T.sem["fa%d%s" % (t, w)], len(topo.engines(home, core)))
+                g.remote_dma(T[w][:, 0:m], T.P[:, MM * t:MM * t + m], T.sem["fb%d%s" % (t, w)], T.sem.ho,
+                             pid, rid, _mask(eng))
+            g.wait_ge(T.sem.ho, RO * len(eng))
+
+
+ORDER = {}
 
 
 def rank_program(g, core, T, topo):
@@ -726,4 +785,8 @@ def rank_program(g, core, T, topo):
     if rank is None:
         _hand_back(g, core, T, topo)
         return
-    _emit(g, T, _plan(g, core, T, topo, rank))
+    ops = _plan(g, core, T, topo, rank)
+    key = str(PAR)
+    if key not in ORDER:
+        ORDER[key] = _order(ops)
+    _emit(g, T, _arrange(ops, ORDER[key][0]))

@@ -5,7 +5,7 @@ L0N, CAP, RO, GH, LM = 640, 96, 4, 512, 1024
 BASE = [L0N + CAP * t for t in range(RO + 1)]
 PL = GH + LM
 BIG = 4096
-MM = 384
+MM = 416
 PAD = 16
 UNIT = 32
 PAR = {
@@ -18,14 +18,18 @@ PAR = {
     "run_p": 128, "run_q": 256, "run_v": 128, "vbias": 0.0, "beta": 1.0, "look": 4,
 }
 PAR.update({"early": 16, "peb": 0, "e_b0": "ssss", "e_b1": "svvv", "e_b2": "ssss", "e_cx": "svvv", "e_c0": "sss", "e_oc": "svvv", "share_P": [128, 160, 192, 192], "share_Q": [0, 64, 64, 64], "m": [160, 224, 256, 224], "nch": [[96, 128, 208, 48], [144, 144, 144, 80], [96, 128, 176, 176], [112, 160, 208, 224]], "ncut": [2, 2, 2, 2], "heng": 16, "mw": 4096, "dw": 128, "q0": 384, "rho_s": 1.0, "rho_c": 1.04, "small": 5, "tolv": 0.1, "tols": 0.25, "tolp": 0.05, "tolg": 0.0, "toly": 0.0, "gam": 1.56, "wake": 0.06, "fold": 0.035, "back": [5.0, 2.8], "ghost": [6, 3.8], "rho_p": 1.0, "rho_q": 1.0, "run_p": 128, "run_q": 256, "run_v": 128, "vbias": [5, 5, 5, 5], "beta": 1, "look": 4})
-PAR.update({"m": [128, 224, 256, 256], "nch": [[96, 144, 208, 64], [144, 144, 144, 80], [96, 160, 112, 208], [112, 128, 224, 208]], "ncut": [2, 1, 2, 2], "heng": 16, "mw": 4096, "dw": 64, "q0": 352, "rho_s": 1.16, "rho_c": 1.04, "small": 5, "tolv": 0.1, "tols": 0.25, "tolp": 0.1, "tolg": 0.0, "toly": 0.0, "gam": 1.56, "wake": 0.06, "fold": 0.035, "back": [5.0, 2.8], "ghost": [6, 4.05], "rho_p": 1.0, "rho_q": 0.92, "run_p": 128, "run_q": 256, "run_v": 128, "vbias": [5, 13, 5, 5], "beta": 1, "look": 4, "early": 0, "peb": 1, "e_b0": "ssss", "e_b1": "vvvv", "e_b2": "ssss", "e_cx": "svvs", "e_c0": "vss", "e_oc": "vsvv", "share_P": [128, 160, 192, 192], "share_Q": [0, 64, 64, 64]})
+PAR.update({"fv": [64, 96, 96, 96], "cv": [96, 32, 32, 64], "qa": [128, 0, 0, 0], "qv": [0, 0, 0, 0], "over": 0.02, "unit_P": 32, "unit_Q": 32, "run_P": 256, "run_Q": 256, "hold": 0.1, "turns": 3, "small2": 0.5})
+PAR.update({"fold0": 2.6, "r4": [0, 0, 0, 96], "ldq": "yy", "m": [128, 224, 256, 256], "nch": [[96, 144, 208, 64], [144, 144, 144, 80], [96, 160, 112, 208], [112, 128, 224, 208]], "ncut": [2, 1, 2, 2], "heng": 16, "mw": 4096, "dw": 64, "q0": 352, "rho_s": 1.16, "rho_c": 1.04, "small": 5, "tolv": 0.1, "tols": 0.25, "tolp": 0.1, "tolg": 0.0, "toly": 0.0, "gam": 1.56, "wake": 0.06, "fold": 0.035, "back": [5.0, 2.8], "ghost": [6, 4.05], "rho_p": 1.0, "rho_q": 0.92, "run_p": 128, "run_q": 256, "run_v": 128, "vbias": [5, 13, 5, 5], "beta": 1, "look": 4, "early": 0, "peb": 1, "e_b0": "ssss", "e_b1": "vvvv", "e_b2": "ssss", "e_cx": "svvs", "e_c0": "vss", "e_oc": "vsvv", "share_P": [128, 160, 192, 192], "share_Q": [0, 64, 64, 64]})
+PAR.update({"turn": [0, 0, 0, 0], "fix": 0.02, "q1": 192, "sched": 2, "yhold": 1.2, "ynr": 2, "nbw": 1, "m": [128, 224, 256, 320], "nch": [[160, 96, 176, 80], [96, 96, 144, 176], [144, 112, 144, 176], [144, 160, 176, 128]], "ncut": [2, 1, 1, 1], "heng": 16, "mw": 1024, "dw": 256, "q0": 384, "rho_s": 0.76, "rho_c": 1.08, "small": 4.0, "gam": 1.56, "wake": 0.06, "fold": 0.0255, "back": [5.4, 2.8], "ghost": [5.25, 3.75], "rho_p": 1.04, "rho_q": 0.92, "early": 8, "peb": 1, "e_cx": "svvv", "e_c0": "svs", "e_oc": "gggg", "fv": [64, 128, 128, 96], "cv": [64, 0, 32, 64], "qa": [128, 0, 0, 0], "qv": [0, 0, 32, 0], "over": 0.02, "unit_P": 32, "unit_Q": 64, "run_P": 192, "run_Q": 256, "hold": 0.325, "turns": 2, "small2": 0.3, "fold0": 3.0, "r4": [64, 0, 0, 96], "e_of": "gggggggggggg"})
+PAR.update({"m": [128, 224, 256, 352], "nch": [[80, 144, 160, 128], [128, 80, 160, 144], [128, 112, 128, 64, 144], [64, 64, 160, 192, 96]], "ncut": [2, 2, 2, 2], "heng": 16, "mw": 4096, "dw": 256, "q0": 416, "rho_s": 0.9, "rho_c": 1.24, "small": 5.0, "gam": 1.4, "wake": 0.15, "fold": 0.0245, "back": [5.4, 2.8], "ghost": [6, 4.0], "rho_p": 1.04, "rho_q": 0.82, "early": 8, "peb": 1, "e_cx": "svvv", "e_c0": "svs", "e_oc": "gggg", "fv": [64, 96, 160, 128], "cv": [32, 32, 0, 0], "qa": [128, 0, 128, 0], "qv": [0, 0, 0, 32], "over": 0.02, "unit_P": 32, "unit_Q": 64, "run_P": 192, "run_Q": 256, "hold": 0.175, "turns": 2, "small2": 0.3, "fold0": 2.6, "r4": [64, 0, 0, 64], "q1": 192, "e_of": "gggggggggggg"})
+PAR.update({"m": [160, 256, 320, 384], "nch": [[112, 112, 144, 112], [96, 144, 112, 128], [96, 144, 144, 128], [112, 144, 144, 144]], "ncut": [2, 1, 1, 1], "heng": 16, "mw": 4096, "dw": 256, "q0": 512, "rho_s": 0.98, "rho_c": 1.2, "small": 5.0, "gam": 1.4, "wake": 0.15, "fold": 0.02, "back": [5.2, 2.8], "ghost": [5.5, 4.0], "rho_p": 1.04, "rho_q": 0.82, "early": 0, "peb": 1, "e_cx": "vvvv", "e_c0": "svs", "e_oc": "ggvg", "fv": [64, 128, 160, 160], "cv": [32, 0, 0, 0], "qa": [128, 0, 192, 0], "qv": [0, 32, 0, 32], "over": 0.03, "unit_P": 32, "unit_Q": 64, "run_P": 192, "run_Q": 256, "hold": 0.175, "turns": 3, "small2": 0.5, "fold0": 2.0, "r4": [0, 0, 0, 96], "turn": [0, 0, 0, 0], "fix": 0.02, "q1": 256, "ynr": 2, "e_of": "gggggggggggg"})
 
 SCRATCH = {
     "W0": ("sbuf", [128, PL], "float32"), "W1": ("sbuf", [128, PL], "float32"),
     "W2": ("sbuf", [128, PL], "float32"), "W3": ("sbuf", [128, PL], "float32"),
     "La": ("sbuf", [128, PL], "float32"), "Lc": ("sbuf", [128, PL], "float32"),
     "Lb": ("sbuf", [128, LM], "float32"),
-    "nbi": ("sbuf", [128, L0N], "int32"),
+    "nbi": ("sbuf", [128, GH + L0N], "int32"),
     "off0": ("sbuf", [128, 928], "uint16"), "off1": ("sbuf", [128, 928], "uint16"),
     "P": ("sbuf", [128, 16 * 928], "float32"),
     "Q": ("sbuf", [128, 16 * 928], "float16"),
@@ -37,27 +41,27 @@ SCRATCH = {
     "lsf": ("sbuf", [128, MM // 4], "float32"), "lsj": ("sbuf", [128, MM // 4], "float32"),
     "lsk": ("sbuf", [128, MM // 4], "int32"), "Bi": ("sbuf", [128, 144], "float32"),
     "Y": ("sbuf", [128, MM], "float32"), "Z": ("sbuf", [128, MM], "float32"),
-    "fl": ("sbuf", [128, LM], "bfloat16"), "rs": ("sbuf", [128, LM], "bfloat16"),
-    "cum": ("sbuf", [128, LM], "bfloat16"), "ones": ("sbuf", [128, LM], "bfloat16"),
+    "fl": ("sbuf", [128, LM], "bfloat16"), "Gm": ("sbuf", [128, LM], "bfloat16"),
+    "rd": ("sbuf", [128, 48], "bfloat16"), "ones": ("sbuf", [128, 512], "bfloat16"),
+    "ie": ("sbuf", [128, 128], "bfloat16"), "Tri": ("sbuf", [128, 128], "bfloat16"),
     "Bm": ("sbuf", [128, 144], "bfloat16"), "Dm": ("sbuf", [128, 2048], "bfloat16"),
     "I1": ("sbuf", [128, 128], "float32"), "Iq": ("sbuf", [128, 128], "float32"),
     "Ib": ("sbuf", [128, 128], "float32"),
     "Am": ("sbuf", [128, 128], "float32"), "IOT": ("sbuf", [128, LM], "float32"),
     "ci": ("sbuf", [128, 8], "int32"), "cf": ("sbuf", [128, 12], "float32"),
-    "mk6": ("sbuf", [128, 8], "float32"), "ew2": ("sbuf", [128, 8], "float32"),
+    "mk6": ("sbuf", [128, 8], "float32"), "ew": ("sbuf", [128, 8], "float32"),
     "sR": ("sbuf", [128, 4], "float32"), "sX": ("sbuf", [128, 4], "float32"),
-    "e2": ("sbuf", [128, CAP], "float32"), "n2": ("sbuf", [128, 8], "float32"),
-    "cc": ("sbuf", [128, 4], "float32"), "acc": ("sbuf", [128, 4], "float32"),
+    "n1": ("sbuf", [128, 8], "float32"), "cc": ("sbuf", [128, 4], "float32"),
     "B6": ("sbuf", [128, 8], "float32"),
     "offm": ("sbuf", [128, 8], "uint16"), "offc": ("sbuf", [128, 8], "uint16"),
     "Cx": ("sbuf", [128, CAP], "float32"), "RV": ("sbuf", [128, CAP], "float32"),
     "LS": ("sbuf", [128, CAP], "float32"), "X1": ("sbuf", [128, CAP], "float32"),
     "CL": ("sbuf", [128, CAP], "float32"),
-    "xp": ("psum", [128, 1024], "float32"), "xq": ("psum", [128, 1024], "float32"),
+    "xp": ("psum", [128, 1024], "float32"), "xq": ("psum", [128, 1536], "float32"),
     "sf": ("psum", [128, 512], "float32"), "se": ("psum", [128, 512], "float32"),
-    "sl": ("psum", [128, 512], "float32"), "vo": ("psum", [128, 512], "float32"),
+    "sl": ("psum", [128, 512], "float32"),
 }
-PSUM = ("xp", "xq", "sf", "se", "sl", "vo")
+PSUM = ("xp", "xq", "sf", "se", "sl")
 NDMA = 16
 SEMAPHORES = (["cv", "cs", "cp", "cg", "ho"] + ["d%d" % i for i in range(NDMA)]
               + ["%s%d" % (s, t) for s in ("arr", "out") for t in range(RO)]
@@ -82,6 +86,8 @@ def _plan(g, core, T, topo, rank):
     ndma = [0]
 
     def ap(name, a, b, step=1):
+        if name == "vo":
+            name, a, b = "sl", 256 + a, 256 + b
         v = T[name][:, a:b] if step == 1 else T[name][:, a:b:step]
         return (v, [(name, a, b, step == 1)], (b - a + step - 1) // step)
 
@@ -106,12 +112,12 @@ def _plan(g, core, T, topo, rank):
         if len(ins[0][1]) > 1:
             return 0.06 + PAR["gam"] * CYC * out[2]
         half = all(kind(x)[2] in ("bfloat16", "float16", "uint16") for x in (out,) + ins)
-        return 0.01 + CYC * max(64, out[2] * (0.5 if half else 1))
+        return PAR["fix"] + CYC * max(64, out[2] * (0.5 if half else 1))
 
     def tt(out, a, b, op, **more):
         c = price(out, a)
         if len(a[1]) == 1 and kind(a)[0] == kind(b)[0]:
-            c = 0.01 + CYC * max(64, 2 * out[2])
+            c = PAR["fix"] + CYC * max(64, 2 * out[2])
         add("v", lambda o: V.tensor_tensor(out[0], a[0], b[0], op), a[1] + b[1], out[1], c, **more)
 
     def ts(out, a, s1, op0, s2=None, op1=None):
@@ -139,7 +145,7 @@ def _plan(g, core, T, topo, rank):
     def act(out, a, f, bias=0.0, scale=1.0, acc=None):
         cb, rb = col(bias)
         cs, rc = col(scale)
-        c = price(out, a) if len(a[1]) > 1 else 0.01 + CYC * max(64, out[2])
+        c = price(out, a) if len(a[1]) > 1 else PAR["fix"] + CYC * max(64, out[2])
         if acc is None:
             add("s", lambda o: S.activation(out[0], a[0], f, bias=cb, scale=cs), a[1] + rb + rc, out[1], c)
         else:
@@ -161,18 +167,19 @@ def _plan(g, core, T, topo, rank):
     def sel(out, a, pat, op, base, cm):
         add("g", lambda o: g.affine_select(out[0], a[0], pat, op, 0.0, base, cm), a[1], out[1], 0.17 + 2 * CYC * out[2])
 
-    def dma(q, out, a, tie=()):
+    def dma(q, out, a, tie=(), behind=0.0, **more):
         name = "d%d" % ndma[0]
         ndma[0] += 1
         eng = g.sync if q == "y" else S
-        add(q, lambda o: eng.dma_start(out[0], a[0]).then_inc(T.sem[name], 16), a[1], out[1] + list(tie), 0.1,
-            tok=(name, 16), lat=1.3, dma=0.2 + 0.0015 * out[2])
+        add(q, lambda o: eng.dma_start(out[0], a[0]).then_inc(T.sem[name], 16), a[1], out[1] + list(tie), PAR["yhold"],
+            tok=(name, 16), lat=1.5 - PAR["yhold"] + 0.0015 * out[2] + behind, **more)
 
     def hbm(name, a, b):
         return (T[name][:, a:b], [], b - a)
 
     Wn = ["W0", "W1", "W2", "W3", "W0"]
     Ln = ["La", "Lc", "La", "Lc", "La"]
+    Tn = ["nbi" if PAR["nbw"] else "La"] + Ln[1:]
     On = ["off0", "off1", "off0", "off1"]
     N = len(T.cores)
     dsts = [T.cores[(rank + 1) % N], T.cores[(rank + 4) % N]]
@@ -197,7 +204,7 @@ def _plan(g, core, T, topo, rank):
                                             remote_sem=T.sem["arr%d" % t], src=src[0],
                                             dst=T[Wn[t]][:, 256 * d:256 * d + 256]))
             g.remote_dma_fused(tr, local_sem=T.sem["out%d" % t])
-        i = add("g", fn, src[1], [], 0.5, tok=("out%d" % t, 8), lat=PAR["ghost"][min(t, 1)] - 0.5)
+        i = add("g", fn, src[1] + ([] if t else [("tie", 8, 9999, True)]), [], 0.5, tok=("out%d" % t, 8), lat=PAR["ghost"][min(t, 1)] - 0.5)
         add("r", None, [], [(Wn[t], 0, GH, True)], 0.3, tok=("arr%d" % t, 8), src=i)
 
     helper = _helpers(core, T, topo)
@@ -215,7 +222,7 @@ def _plan(g, core, T, topo, rank):
                                        dst=T.P[:, MM * t:MM * t + m], alu_op=3 if w == "Z" else 2)
                 g.remote_dma_fused([tr], local_sem=T.sem["fo%d%s" % (t, w)])
             i = add("g", fn, [("P", 0, 16 * m, True), ("tie", t, t + 1, True)], [], 0.5,
-                    tok=("fo%d%s" % (t, w), len(eng)), lat=0.7 if t else 1.3, dma=PAR["fold"] * m, chain="fold")
+                    tok=("fo%d%s" % (t, w), len(eng)), lat=0.7 if t else 1.3, dma=PAR["fold0"] + PAR["fold"] * m, chain="fold")
             add("r", None, [], [(w, 0, m, True)], PAR["back"][min(t, 1)], tok=("fb%d%s" % (t, w), PAR["heng"]), src=i)
 
     def bounds(sizes, a=0):
@@ -227,12 +234,14 @@ def _plan(g, core, T, topo, rank):
 
     M = PAR["m"] + [0]
     nch = [bounds(PAR["nch"][t], M[t]) for t in range(RO)]
-    cut = [nch[t][PAR["ncut"][t] - 1][1] for t in range(RO)]
+    cut = [nch[t][PAR["ncut"][t]][0] for t in range(RO)]
     late = [nch[t][-1][0] for t in range(RO)]
-    rng = [[(0, M[t]), (M[t], cut[t]), (cut[t], BASE[t])] for t in range(RO)]
+    ends = [[0, M[t], cut[t], BASE[t] - PAR["r4"][t], BASE[t]] for t in range(RO)]
+    rng = [[(a, b) for a, b in zip(e, e[1:]) if a < b] for e in ends]
+    assert all(e == sorted(e) for e in ends) and ends[RO - 1][3] >= L0N and M[0] <= PAR["q1"] <= PAR["q0"]
     for t in range(RO):
         assert nch[t][-1][1] == BASE[t] and cut[t] <= 512 and BASE[t] - cut[t] <= 512 and late[t] - M[t] <= 512
-        assert M[t + 1] <= cut[t] and M[t] + BASE[t] - late[t] <= 512 and len(nch[t]) > 1
+        assert len(nch[t]) > 1
 
     def xcol(t, a, b):
         return ap("xp", a, b) if b <= cut[t] else ap("xp", 512 + a - cut[t], 512 + b - cut[t])
@@ -243,7 +252,7 @@ def _plan(g, core, T, topo, rank):
         return ap("se", a - M[t], b - M[t]) if b <= late[t] else ap("sl", a - late[t], b - late[t])
 
     def qcol(t, r, a, b):
-        o = 512 * (r % 2) - rng[t][r][0]
+        o = 512 * (r % 3) - rng[t][r][0]
         return ap("xq", o + a, o + b)
 
     def own(name, a, b):
@@ -258,7 +267,7 @@ def _plan(g, core, T, topo, rank):
         return ap(name, 16 * a + k, 16 * b, 16)
 
     def gather(name, t, a, b, q):
-        win = Wn[t] if name == "P" else Ln[t]
+        win = Wn[t] if name == "P" else Tn[t]
         src = ind(ap(win, 0, GH + BASE[t]), ap(On[t], a, b))
         out = ap(name, 16 * a, 16 * b)
         sign = 1.0 if name == "P" else -1.0
@@ -266,13 +275,17 @@ def _plan(g, core, T, topo, rank):
             return V.tensor_scalar(out[0], src[0], sign, None, A.mult)
         return S.activation(out[0], src[0], AF.Copy, bias=0.0, scale=sign)
 
-    def stream(name, t, parts):
+    def stream(name, t, parts, first=False):
         for a0, b0 in parts:
-            for a in range(a0, b0, UNIT):
-                b = min(a + UNIT, b0)
-                win = Wn[t] if name == "P" else Ln[t]
-                add("vs", gather, ap(win, 0, GH + BASE[t])[1] + ap(On[t], a, b)[1], ap(name, 16 * a, 16 * b)[1],
-                    PAR["gam"] * CYC * 16 * (b - a), unit=(name, t, a, b), chain=name)
+            unit = PAR["unit_" + name]
+            for a in range(a0, b0, unit):
+                b = min(a + unit, b0)
+                win = Wn[t] if name == "P" else Tn[t]
+                v0 = M[t] - PAR["fv"][t] if name == "P" else PAR["qa"][t]
+                v1 = M[t] + PAR["cv"][t] if name == "P" else PAR["qa"][t] + PAR["qv"][t]
+                add("vs" if PAR["sched"] == 1 else "v" if v0 <= a and b <= v1 else "s", gather,
+                    ap(win, 0, GH + BASE[t])[1] + ap(On[t], a, b)[1], ap(name, 16 * a, 16 * b)[1],
+                    PAR["gam"] * CYC * 16 * (b - a) + PAR["over"], unit=(name, t, a, b), chain=name, first=first)
 
     def copy_x(t, bank):
         a, b = ((0, cut[t]), (cut[t], BASE[t]))[bank]
@@ -297,6 +310,8 @@ def _plan(g, core, T, topo, rank):
     def scaled(what, t, out, a, c):
         if PAR[what][t] == "s":
             act(out, a, AF.Copy, scale=c)
+        elif PAR[what][t] == "g":
+            sel(out, a, [[0, out[2]]], A.is_ge, 0, 0)
         else:
             ts(out, a, c, A.mult)
 
@@ -310,12 +325,6 @@ def _plan(g, core, T, topo, rank):
     def u_flag(t, a, b):
         act(ap("fl", a, b), scol(t, a, b), AF.Sign, bias=-(3.5 + 2.0 ** -22), scale=3.5)
 
-    def vote(a, b, at):
-        mm(ap("vo", at, at + b - a), ap("ones", 0, 128), ap("fl", a, b), True, True)
-
-    def ready(a, b, at):
-        act(ap("rs", a, b), ap("vo", at, at + b - a), AF.Sign, bias=1.0)
-
     def u_clip(t, a, b):
         ts(own(Wn[t + 1], a, b), scol(t, a, b), 0.0, A.max, 2.0, A.min)
 
@@ -324,7 +333,7 @@ def _plan(g, core, T, topo, rank):
         f = ap("F", 512 * k, 512 * k + b - a)
         if t == 0 and r == 0 and k < PAR["early"]:
             c = b // 16
-            tt(f, ind(own("W0", 0, L0N), ap("off1", k * c, k * c + c)), own("W0", a, b), A.is_gt)
+            tt(f, ind(own("W0", 0, L0N), ap("off1", k * c, k * c + c)), ap("TT", 576 + a, 576 + b), A.is_gt)
         else:
             tt(f, link("P", r, a, b, k), xcol(t, a, b), A.is_gt, chain="cmp")
         mm(qcol(t, r, a, b), ap("Bm", 16 - k, 144 - k), f, k == 0, False, grp=(t, r))
@@ -347,8 +356,10 @@ def _plan(g, core, T, topo, rank):
 
     def l_off(t, r):
         a, b = max(rng[t][r][0], M[t + 1]), min(rng[t][r][1], L0N)
-        if a < b:
+        if a < b and PAR["e_of"][4 * t + r] == "s":
             act(ap(On[t + 1], a, b), dbc(a, b), AF.Abs)
+        elif a < b:
+            scaled("e_of", 4 * t + r, ap(On[t + 1], a, b), own(Ln[t + 1], a, b), 1.0)
 
     lso = {}
     for m in sorted(set(M[:RO])):
@@ -360,9 +371,12 @@ def _plan(g, core, T, topo, rank):
         turn(ap("TT", m, 2 * m + 32), ap(name, o - 16, o + m + 16))
         act(ap(On[t], 0, m), ind(ap("TT", 0, 2 * m + 32), ap("lst", lso[m], lso[m] + m // 16)), AF.Abs)
 
-    dma("y", own("W0", 0, 256), hbm("x0", 0, 256))
-    dma("s", ap("nbi", 0, L0N), hbm("nb", 0, L0N))
-    dma("y", own("W0", 256, L0N), hbm("x0", 256, L0N))
+    dma("y", own("W0", 0, 256), hbm("x0", 0, 256), first=True)
+    mset(ap("ones", 0, 512), 1.0)
+    ops[-1]["first"] = True
+    ops[-1]["w"].append(("tie", 5, 6, True))
+    dma("s", own("nbi", 0, L0N), hbm("nb", 0, L0N), [("tie", 5, 6, True)], behind=0.5, first=True)
+    dma("y", own("W0", 256, L0N), hbm("x0", 256, L0N), behind=1.5, first=True)
     send(0)
     iota(ap("ci", 0, 1), [[0, 1]], 0, 1)
     ts(ap("ci", 1, 2), ap("ci", 0, 1), 15, A.bitwise_and)
@@ -384,39 +398,45 @@ def _plan(g, core, T, topo, rank):
     cp(ap("lst", 0, nl), ap("lsf", 0, nl))
     iota(ap("La", 0, GH), [[1, GH]], 0, 0)
     iota(own("La", L0N, LM), [[1, LM - L0N]], GH + L0N, 0)
-    cp(ap("off0", M[0], L0N), ap("nbi", M[0], L0N))
-    cp(own("La", 0, L0N), ap("nbi", 0, L0N))
+    iota(ap("nbi", 0, GH), [[1, GH]], 0, 0)
+    ops[-1]["first"] = True
+    cp(ap("off0", M[0], PAR["q0"]), own("nbi", M[0], PAR["q0"]))
+    ops[-1]["first"] = True
+    if PAR["q0"] < L0N:
+        cp(ap("off0", PAR["q0"], L0N), own("nbi", PAR["q0"], L0N))
+    cp(own("La", 0, L0N), own("nbi", 0, L0N))
     l_list(0, "La", GH)
     if PAR["early"]:
         ts(ap("off1", 0, M[0]), ap("off0", 0, M[0]), float(-GH), A.add)
-    mset(ap("ones", 0, LM), 1.0)
+        assert M[0] <= 224
+        act(ap("TT", 576, 576 + M[0]), own("W0", 0, M[0]), AF.Copy)
+    mset(ap("rd", 16, 17), 0.0)
     mset(ap("db", 0, PAD), 0.0)
     mset(dbc(M[1], M[1] + 16), 0.0)
-    mset(ap("n2", 0, 1), 2.0 * (GH + L0N))
-    mset(ap("rs", L0N, LM), -1.0)
-    mw = PAR["mw"]
+    mset(ap("n1", 0, 1), float(GH + L0N))
+    mset(ap("fl", L0N, LM), -1.0)
+    mw = min(PAR["mw"], 16 * max(b - a for ch in nch for a, b in ch))
     mset(ap("m1", 0, mw), 1.0)
     mset(ap("m2", 0, mw), 0.0)
     mset(ap("m1", 0, mw, 16), 0.0)
     mset(ap("m2", 0, mw, 16), 4.0)
-    for w in range(mw, 4096, mw):
-        dma("y", ap("m2", w, w + mw), ap("m2", 0, mw))
-        dma("y", ap("m1", w, w + mw), ap("m1", 0, mw))
+    for w in range(mw, 16 * max(b - a for ch in nch for a, b in ch), mw):
+        dma("y", ap("m2", w, w + mw), ap("m2", 0, mw), [("tie", 8 + w, 9 + w, True)])
+        dma("y", ap("m1", w, w + mw), ap("m1", 0, mw), [("tie", 9 + w, 10 + w, True)])
     iota(ap("Bi", 0, 144), [[1, 144]], -16, 0)
     iota(ap("mk6", 0, 8), [[1, 8]], 0, 0)
-    iota(ap("ew2", 0, 8), [[32, 8]], -2 * (GH + L0N), 0)
+    iota(ap("ew", 0, 8), [[16, 8]], -(GH + L0N), 0)
     iota(ap("Am", 0, 128), [[0, 8], [1, 16]], 0, 0)
     iota(ap("I1", 0, 128), [[0, 128]], 1, 0)
     sel(ap("I1", 0, 128), ap("I1", 0, 128), [[-1, 128]], A.is_equal, 0, 1)
-    iota(ap("cf", 8, 9), [[0, 1]], 1, 2)
-    iota(ap("e2", 0, CAP), [[2, CAP]], 0, 0)
-    ts(ap("cf", 9, 10), ap("cf", 1, 2), 2.0, A.mult)
+    iota(ap("ie", 0, 128), [[1, 128]], 0, 0)
+    sel(ap("Tri", 0, 128), ap("ones", 0, 128), [[1, 128]], A.is_ge, 0, -1)
     ts(ap("cf", 10, 11), ap("cf", 2, 3), 16.0, A.mult)
     ts(ap("Bm", 0, 144), ap("Bi", 0, 144), ap("cf", 10, 11), A.is_equal, float(BIG), A.mult)
     ts(ap("sX", 0, 4), ap("mk6", 0, 4), ap("cf", 1, 2), A.is_equal)
     ts(ap("mk6", 0, 8), ap("mk6", 0, 8), ap("cf", 2, 3), A.is_equal)
-    ts(ap("sR", 0, 4), ap("sX", 0, 4), -2.5, A.mult, 2.0, A.add)
-    ts(ap("ew2", 0, 8), ap("ew2", 0, 8), ap("cf", 9, 10), A.add)
+    ts(ap("sR", 0, 4), ap("sX", 0, 4), -3.0, A.mult, 2.0, A.add)
+    ts(ap("ew", 0, 8), ap("ew", 0, 8), ap("cf", 1, 2), A.add)
     ts(ap("sX", 0, 4), ap("sX", 0, 4), -3.0, A.mult, 4.0, A.add)
     ts(ap("Am", 0, 128), ap("Am", 0, 128), ap("cf", 1, 2), A.is_equal)
     scaled("e_c0", 2, ap("Iq", 0, 128), ap("I1", 0, 128), 0.25)
@@ -433,26 +453,29 @@ def _plan(g, core, T, topo, rank):
     iota(own("Lc", L0N, LM), [[1, LM - L0N]], GH + L0N, 0)
 
     offm, offc = ap("offm", 0, 6), ap("offc", 0, 6)
+    yn0 = min(L0N, rng[RO - 1][min(PAR["ynr"], len(rng[RO - 1]) - 1)][1])
     for t in range(RO):
         n, nn, m, lt = BASE[t], BASE[t + 1], M[t], late[t]
         last = t == RO - 1
         W1, L1 = Wn[t + 1], Ln[t + 1]
         ch = nch[t]
-        n2 = ap("n2", t, t + 1)
+        n1 = ap("n1", t, t + 1)
         if t == 0:
-            stream("Q", t, [(m, PAR["q0"])])
+            stream("Q", t, [(m, PAR["q1"])], True)
+            stream("Q", t, [(PAR["q1"], PAR["q0"])])
         stream("P", t, [(0, m)] + ch)
         fold(t)
         dma("y", ap("Lb", 0, nn), own(Ln[t], 0, nn), [("tie", t, t + 1, True)])
-        stream("Q", t, [(0, m), (PAR["q0"], n)] if t == 0 else rng[t])
+        stream("Q", t, [(0, m), (PAR["q0"], n)] if t == 0 else
+               rng[t][1:2] + rng[t][:1] + rng[t][2:] if PAR["turn"][t] else rng[t])
         copy_x(t, 0)
         copy_x(t, 1)
         for a, b in ((m, lt), (0, m), (lt, n)):
             start_s(t, a, b)
-        ts(ap("cc", 0, 1), ap("cf", 8, 9), n2, A.add, float(-1 - nn - 2 * GH), A.add)
-        ts(ap("RV", 0, CAP), ap("e2", 0, CAP), n2, A.add, ap("sR", t, t + 1), A.mult)
+        ts(ap("cc", 0, 1), ap("cf", 0, 1), n1, A.add, float(-GH), A.add)
+        ts(ap("RV", 0, CAP), ap("ie", 0, CAP), n1, A.add, ap("sR", t, t + 1), A.mult)
         if t > 0:
-            ts(offc, ap("ew2", 0, 6), n2, A.add, 0.5, A.mult)
+            ts(offc, ap("ew", 0, 6), n1, A.add)
         for a, b in ch:
             s_min(a, b)
             u_a(t, a, b)
@@ -460,8 +483,6 @@ def _plan(g, core, T, topo, rank):
             if b == lt:
                 u_d("e_b0", t, m, lt)
                 u_flag(t, m, lt)
-                vote(m, lt, 0)
-                ready(m, lt, 0)
                 u_clip(t, m, lt)
         u_d("e_b1", t, lt, n)
         u_flag(t, lt, n)
@@ -469,17 +490,25 @@ def _plan(g, core, T, topo, rank):
         mm(scol(t, 0, m), ap("Iq", 0, 128), ap("Y", 0, m), False, False)
         u_d("e_b2", t, 0, m)
         u_flag(t, 0, m)
-        vote(lt, n, m)
-        vote(0, m, 0)
         u_clip(t, lt, n)
         u_clip(t, 0, m)
-        ready(lt, n, m)
-        ready(0, m, 0)
-        scan(ap("cum", 0, nn), ap("rs", 0, nn), ap("ones", 0, nn), A.add, A.add)
-        act(ap("fl", 0, nn), ap("cum", 0, nn), AF.Sign, bias=ap("cf", 8, 9), scale=-1.0, acc=ap("acc", 0, 1))
-        ts(ap("B6", 0, 6), ap("mk6", 0, 6), ap("acc", 0, 1), A.mult, ap("cc", 0, 1), A.min)
-        mm(ap("vo", 496, 502), ap("Am", 0, 128), ap("B6", 0, 6), True, True)
-        ts(offm, ap("vo", 496, 502), 0.5, A.mult, nn / 2.0, A.add)
+        J = (nn + 127) // 128
+        one = ap("ones", 0, 1)
+        for j in range(J):
+            mm(ap("vo", j, j + 1), ap("fl", 128 * j, 128 * j + 128), one, True, True)
+        ts(ap("rd", 0, J), ap("vo", 0, J), 0.0, A.is_ge)
+        scan(ap("rd", 17, 17 + J), ap("rd", 0, J), ap("rd", 0, J), A.add, A.max)
+        mm(ap("vo", 16, 17 + J), ap("ones", 0, 128), ap("rd", 16, 17 + J), True, False)
+        mm(ap("vo", 16, 16 + J), ap("Tri", 0, 128), ap("rd", 0, J), False, True)
+        cp(ap("rd", 32, 32 + J), ap("vo", 16, 16 + J))
+        ts(ap("n1", t + 1, t + 2), ap("vo", 16 + J, 17 + J), float(CAP), A.min, n1, A.add)
+        for j in range(J):
+            ts(ap("Gm", 128 * j, 128 * j + 128), ap("ie", 0, 128), ap("rd", 32 + j, 33 + j), A.is_ge)
+        for j in range(J):
+            mm(ap("vo", 32, 33), ap("Gm", 128 * j, 128 * j + 128), one, j == 0, j == J - 1)
+        ts(ap("B6", 0, 6), ap("mk6", 0, 6), ap("vo", 32, 33), A.mult, ap("cc", 0, 1), A.min)
+        mm(ap("vo", 40, 46), ap("Am", 0, 128), ap("B6", 0, 6), True, True)
+        cp(offm, ap("vo", 40, 46))
         scaled("e_cx", t, ap("Cx", 0, CAP), ind(own(W1, 0, nn), offm), 0.5)
         cp(ind(own(W1, 0, nn), offm), ap("Cx", 0, CAP))
         if t == 0:
@@ -492,20 +521,26 @@ def _plan(g, core, T, topo, rank):
             send(t + 1)
         tt(ap("LS", 0, CAP), ind(own(Ln[t], 0, nn), offm), ap("RV", 0, CAP), A.min)
         cp(ind(ap("Lb", 0, nn), offm), ap("LS", 0, CAP))
-        ts(ap("n2", t + 1, t + 2), ap("cum", n - 1, n), 2.0 * CAP, A.min, n2, A.add)
         act(ap("X1", 0, CAP), ind(ap("IOT", 0, nn), offm), AF.Copy, scale=ap("sX", t, t + 1))
-        for r in range(3):
+        todo = list(range(len(rng[t])))
+        if PAR["turn"][t]:
+            todo = todo[1:2] + todo[:1] + todo[2:]
+        need = M[t + 1] if not last else yn0
+        while todo:
+            r = todo.pop(0)
             for k in range(16):
                 l_cmp(t, r, k)
             l_diag(t, r)
             l_y(t, r)
+            l_abs(t, r)
             if not last:
                 l_off(t, r)
-                if r == (0 if M[t + 1] <= m else 1):
+            if need and all(rng[t][x][0] >= need for x in todo):
+                if last:
+                    dma("y", hbm("yn", 0, yn0), own(L1, 0, yn0))
+                else:
                     l_list(t + 1, "db", PAD)
-            l_abs(t, r)
-            if last and r == 1:
-                dma("y", hbm("yn", 0, cut[t]), own(L1, 0, cut[t]))
+                need = 0
         tt(ap("CL", 0, CAP), ind(own(L1, 0, nn), offm), ap("X1", 0, CAP), A.min)
         if t == 0:
             scaled("e_c0", 1, own(L1, L0N, nn), ap("CL", 0, CAP), 1.0)
@@ -513,10 +548,10 @@ def _plan(g, core, T, topo, rank):
             cp(ind(own(L1, L0N, nn), offc), ap("CL", 0, CAP))
         if not last:
             scaled("e_oc", t, ap(On[t + 1], L0N, nn), own(L1, L0N, nn), 1.0)
-    ts(ap("se", 0, LM - L0N), ap("IOT", L0N, LM), 2.0, A.mult, ap("n2", RO, RO + 1), A.is_lt)
+    ts(ap("se", 0, LM - L0N), ap("IOT", L0N, LM), ap("n1", RO, RO + 1), A.is_lt)
     tail = own(Ln[RO], L0N, LM)
     tt(tail, tail, ap("se", 0, LM - L0N), A.mult)
-    dma("y", hbm("yn", cut[RO - 1], LM), own(Ln[RO], cut[RO - 1], LM))
+    dma("s", hbm("yn", yn0, LM), own(Ln[RO], yn0, LM))
     return ops
 
 
@@ -691,6 +726,110 @@ def _order(ops):
     return out, max(e for e in end)
 
 
+def _place(order_by, before, after, res, dur, lag, mirror=False):
+    n = len(res)
+    left = [len(b) for b in before]
+    start = [0.0] * n
+    busy = {}
+    ready = [(order_by[i], i) for i in range(n) if left[i] == 0]
+    while ready:
+        best = min(ready)
+        ready.remove(best)
+        i = best[1]
+        t = max([start[j] + dur[j] + lag[i if mirror else j] for j in before[i]] + [lag[i] if mirror else 0.0])
+        if res[i] != "r":
+            line = busy.setdefault(res[i], [])
+            lo, hi = 0, len(line)
+            while lo < hi:
+                mid = (lo + hi) // 2
+                if line[mid][1] <= t:
+                    lo = mid + 1
+                else:
+                    hi = mid
+            while lo < len(line) and line[lo][0] < t + dur[i]:
+                t = max(t, line[lo][1])
+                lo += 1
+            line.insert(lo, (t, t + dur[i]))
+        start[i] = t
+        for j in after[i]:
+            left[j] -= 1
+            if left[j] == 0:
+                ready.append((order_by[j], j))
+    return start
+
+
+def _order2(ops):
+    deps = _deps(ops)
+    wake = PAR["wake"]
+    res, dur, lag, before, done = [], [], [], [], []
+    last = {}
+    for i, o in enumerate(ops):
+        b = {done[j] for j in deps[i]}
+        if "unit" in o or o.get("chain") == "fold":
+            key = o["unit"][:2] + (o["q"],) if "unit" in o else "fold"
+            if key in last:
+                b.add(last[key])
+            last[key] = len(res)
+        o["node"] = len(res)
+        res.append(o["q"])
+        dur.append(o["cost"])
+        lag.append(o["lat"] + (0.0 if o["dma"] else wake))
+        before.append(b)
+        if o["dma"]:
+            before.append({len(res) - 1, last.get("d", len(res) - 1)})
+            last["d"] = len(res)
+            res.append("d")
+            dur.append(o["dma"])
+            lag.append(wake)
+        done.append(len(res) - 1)
+    n = len(res)
+    after = [[] for _ in res]
+    for i, b in enumerate(before):
+        for j in b:
+            after[j].append(i)
+    lane = {"P": PAR["rho_p"], "Q": PAR["rho_q"], "scan": PAR["rho_s"], "cmp": PAR["rho_c"]}
+    rho = {o["node"]: lane[o["chain"]] for o in ops if o.get("chain") in lane}
+    tail, seen, boost = [0.0] * n, {}, [0.0] * n
+    for i in range(n - 1, -1, -1):
+        tail[i] = dur[i] + lag[i] + max([tail[j] for j in after[i]] + [0.0])
+        if i in rho:
+            if res[i] in seen:
+                tail[i] = max(tail[i], rho[i] * dur[i] + tail[seen[res[i]]])
+            seen[res[i]] = i
+    for o in ops:
+        if o.get("first") or (o["q"] == "g" and o["tok"]):
+            boost[o["node"]] = 1000.0 - o["node"] / n
+    key = [-tail[i] - (0.0 if i in rho else PAR["small"]) - boost[i] for i in range(n)]
+    best = None
+    none = [0.0] * n
+    for _ in range(PAR["turns"]):
+        start = _place(key, before, after, res, dur, lag)
+        end = max(start[i] + dur[i] + lag[i] for i in range(n))
+        if best is None or end < best[0]:
+            best = (end, start)
+        back = _place([-(start[i] + dur[i] + lag[i]) for i in range(n)], after, before, res, dur, lag, True)
+        key = [-(back[i] + dur[i]) - (0.0 if i in rho else PAR["small2"]) - boost[i] for i in range(n)]
+    end, start = best
+    rank = sorted(range(len(ops)), key=lambda i: (start[ops[i]["node"]], i))
+    out, open_run = [], {}
+    for i in rank:
+        o = ops[i]
+        q, s = o["q"], start[o["node"]]
+        run = open_run.get(q)
+        if run and "unit" in o:
+            u, w = ops[run[0]]["unit"], o["unit"]
+            s0, prev = start[ops[run[0]]["node"]], ops[run[-1]]
+            if (u[:2] == w[:2] and prev["unit"][3] == w[2] and w[3] - u[2] <= PAR["run_" + u[0]]
+                    and all(start[j] + dur[j] <= s0 for j in before[o["node"]] if j != prev["node"])
+                    and all(start[j] >= s + dur[o["node"]] - PAR["hold"] for x in run for j in after[ops[x]["node"]]
+                            if j != o["node"] and j not in [ops[y]["node"] for y in run])):
+                run.append(i)
+                continue
+        out.append(([i], q))
+        open_run[q] = out[-1][0] if "unit" in o else None
+    return out, end
+
+
 def _arrange(ops, order):
     out = []
     closing = {}
@@ -788,5 +927,5 @@ def rank_program(g, core, T, topo):
     ops = _plan(g, core, T, topo, rank)
     key = str(PAR)
     if key not in ORDER:
-        ORDER[key] = _order(ops)
+        ORDER[key] = _order(ops) if PAR["sched"] == 1 else _order2(ops)
     _emit(g, T, _arrange(ops, ORDER[key][0]))

from concourse.bass import DstId, RemoteDMATransfer
from concourse.mybir import AluOpType, ActivationFunctionType

L0N, CAP, RO, GH, LM = 640, 96, 4, 512, 1024
BASE = [L0N + CAP * t for t in range(RO + 1)]
PL = GH + LM
BIG = 4096
MM = 416
PAD = 16
UNIT = 32
PAR = {
    "m": [128, 224, 224, 224],
    "nch": [[128, 128, 192, 64], [128, 128, 128, 128], [128, 128, 192, 160], [128, 160, 224, 192]],
    "ncut": [2, 2, 2, 2],
    "heng": 8, "mw": 4096, "dw": 128, "q0": 448, "rho_s": 1.0, "rho_c": 1.0,
    "small": 10.0, "tolv": 0.3, "tols": 0.3, "tolp": 0.1, "tolg": 0.2, "toly": 0.0,
    "gam": 1.56, "wake": 0.06, "fold": 0.033, "back": 2.6, "ghost": [6.5, 3.8], "rho_p": 0.6, "rho_q": 0.8,
    "run_p": 128, "run_q": 256, "run_v": 128, "vbias": 0.0, "beta": 1.0, "look": 4,
}
PAR.update({"early": 16, "peb": 0, "e_b0": "ssss", "e_b1": "svvv", "e_b2": "ssss", "e_cx": "svvv", "e_c0": "sss", "e_oc": "svvv", "share_P": [128, 160, 192, 192], "share_Q": [0, 64, 64, 64], "m": [160, 224, 256, 224], "nch": [[96, 128, 208, 48], [144, 144, 144, 80], [96, 128, 176, 176], [112, 160, 208, 224]], "ncut": [2, 2, 2, 2], "heng": 16, "mw": 4096, "dw": 128, "q0": 384, "rho_s": 1.0, "rho_c": 1.04, "small": 5, "tolv": 0.1, "tols": 0.25, "tolp": 0.05, "tolg": 0.0, "toly": 0.0, "gam": 1.56, "wake": 0.06, "fold": 0.035, "back": [5.0, 2.8], "ghost": [6, 3.8], "rho_p": 1.0, "rho_q": 1.0, "run_p": 128, "run_q": 256, "run_v": 128, "vbias": [5, 5, 5, 5], "beta": 1, "look": 4})
PAR.update({"fv": [64, 96, 96, 96], "cv": [96, 32, 32, 64], "qa": [128, 0, 0, 0], "qv": [0, 0, 0, 0], "over": 0.02, "unit_P": 32, "unit_Q": 32, "run_P": 256, "run_Q": 256, "hold": 0.1, "turns": 3, "small2": 0.5})
PAR.update({"fold0": 2.6, "r4": [0, 0, 0, 96], "ldq": "yy", "m": [128, 224, 256, 256], "nch": [[96, 144, 208, 64], [144, 144, 144, 80], [96, 160, 112, 208], [112, 128, 224, 208]], "ncut": [2, 1, 2, 2], "heng": 16, "mw": 4096, "dw": 64, "q0": 352, "rho_s": 1.16, "rho_c": 1.04, "small": 5, "tolv": 0.1, "tols": 0.25, "tolp": 0.1, "tolg": 0.0, "toly": 0.0, "gam": 1.56, "wake": 0.06, "fold": 0.035, "back": [5.0, 2.8], "ghost": [6, 4.05], "rho_p": 1.0, "rho_q": 0.92, "run_p": 128, "run_q": 256, "run_v": 128, "vbias": [5, 13, 5, 5], "beta": 1, "look": 4, "early": 0, "peb": 1, "e_b0": "ssss", "e_b1": "vvvv", "e_b2": "ssss", "e_cx": "svvs", "e_c0": "vss", "e_oc": "vsvv", "share_P": [128, 160, 192, 192], "share_Q": [0, 64, 64, 64]})
PAR.update({"turn": [0, 0, 0, 0], "fix": 0.02, "q1": 192, "sched": 2, "yhold": 1.2, "ynr": 2, "nbw": 1, "m": [128, 224, 256, 320], "nch": [[160, 96, 176, 80], [96, 96, 144, 176], [144, 112, 144, 176], [144, 160, 176, 128]], "ncut": [2, 1, 1, 1], "heng": 16, "mw": 1024, "dw": 256, "q0": 384, "rho_s": 0.76, "rho_c": 1.08, "small": 4.0, "gam": 1.56, "wake": 0.06, "fold": 0.0255, "back": [5.4, 2.8], "ghost": [5.25, 3.75], "rho_p": 1.04, "rho_q": 0.92, "early": 8, "peb": 1, "e_cx": "svvv", "e_c0": "svs", "e_oc": "gggg", "fv": [64, 128, 128, 96], "cv": [64, 0, 32, 64], "qa": [128, 0, 0, 0], "qv": [0, 0, 32, 0], "over": 0.02, "unit_P": 32, "unit_Q": 64, "run_P": 192, "run_Q": 256, "hold": 0.325, "turns": 2, "small2": 0.3, "fold0": 3.0, "r4": [64, 0, 0, 96], "e_of": "gggggggggggg"})
PAR.update({"m": [128, 224, 256, 352], "nch": [[80, 144, 160, 128], [128, 80, 160, 144], [128, 112, 128, 64, 144], [64, 64, 160, 192, 96]], "ncut": [2, 2, 2, 2], "heng": 16, "mw": 4096, "dw": 256, "q0": 416, "rho_s": 0.9, "rho_c": 1.24, "small": 5.0, "gam": 1.4, "wake": 0.15, "fold": 0.0245, "back": [5.4, 2.8], "ghost": [6, 4.0], "rho_p": 1.04, "rho_q": 0.82, "early": 8, "peb": 1, "e_cx": "svvv", "e_c0": "svs", "e_oc": "gggg", "fv": [64, 96, 160, 128], "cv": [32, 32, 0, 0], "qa": [128, 0, 128, 0], "qv": [0, 0, 0, 32], "over": 0.02, "unit_P": 32, "unit_Q": 64, "run_P": 192, "run_Q": 256, "hold": 0.175, "turns": 2, "small2": 0.3, "fold0": 2.6, "r4": [64, 0, 0, 64], "q1": 192, "e_of": "gggggggggggg"})
PAR.update({"m": [160, 256, 320, 384], "nch": [[112, 112, 144, 112], [96, 144, 112, 128], [96, 144, 144, 128], [112, 144, 144, 144]], "ncut": [2, 1, 1, 1], "heng": 16, "mw": 4096, "dw": 256, "q0": 512, "rho_s": 0.98, "rho_c": 1.2, "small": 5.0, "gam": 1.4, "wake": 0.15, "fold": 0.02, "back": [5.2, 2.8], "ghost": [5.5, 4.0], "rho_p": 1.04, "rho_q": 0.82, "early": 0, "peb": 1, "e_cx": "vvvv", "e_c0": "svs", "e_oc": "ggvg", "fv": [64, 128, 160, 160], "cv": [32, 0, 0, 0], "qa": [128, 0, 192, 0], "qv": [0, 32, 0, 32], "over": 0.03, "unit_P": 32, "unit_Q": 64, "run_P": 192, "run_Q": 256, "hold": 0.175, "turns": 3, "small2": 0.5, "fold0": 2.0, "r4": [0, 0, 0, 96], "turn": [0, 0, 0, 0], "fix": 0.02, "q1": 256, "ynr": 2, "e_of": "gggggggggggg"})

SCRATCH = {
    "W0": ("sbuf", [128, PL], "float32"), "W1": ("sbuf", [128, PL], "float32"),
    "W2": ("sbuf", [128, PL], "float32"), "W3": ("sbuf", [128, PL], "float32"),
    "La": ("sbuf", [128, PL], "float32"), "Lc": ("sbuf", [128, PL], "float32"),
    "Lb": ("sbuf", [128, LM], "float32"),
    "nbi": ("sbuf", [128, GH + L0N], "int32"),
    "off0": ("sbuf", [128, 928], "uint16"), "off1": ("sbuf", [128, 928], "uint16"),
    "P": ("sbuf", [128, 16 * 928], "float32"),
    "Q": ("sbuf", [128, 16 * 928], "float16"),
    "F": ("sbuf", [128, 16 * 512], "bfloat16"),
    "SX": ("sbuf", [128, 4096], "float32"), "SN": ("sbuf", [128, 4096], "float32"),
    "m1": ("sbuf", [128, 4096], "bfloat16"), "m2": ("sbuf", [128, 4096], "bfloat16"),
    "ab": ("sbuf", [128, 928], "float32"), "db": ("sbuf", [128, PAD + 928], "float32"),
    "TT": ("sbuf", [128, 2 * MM + 32], "float32"), "lst": ("sbuf", [128, MM // 4], "uint16"),
    "lsf": ("sbuf", [128, MM // 4], "float32"), "lsj": ("sbuf", [128, MM // 4], "float32"),
    "lsk": ("sbuf", [128, MM // 4], "int32"), "Bi": ("sbuf", [128, 144], "float32"),
    "Y": ("sbuf", [128, MM], "float32"), "Z": ("sbuf", [128, MM], "float32"),
    "fl": ("sbuf", [128, LM], "bfloat16"), "Gm": ("sbuf", [128, LM], "bfloat16"),
    "rd": ("sbuf", [128, 48], "bfloat16"), "ones": ("sbuf", [128, 512], "bfloat16"),
    "ie": ("sbuf", [128, 128], "bfloat16"), "Tri": ("sbuf", [128, 128], "bfloat16"),
    "Bm": ("sbuf", [128, 144], "bfloat16"), "Dm": ("sbuf", [128, 2048], "bfloat16"),
    "I1": ("sbuf", [128, 128], "float32"), "Iq": ("sbuf", [128, 128], "float32"),
    "Ib": ("sbuf", [128, 128], "float32"),
    "Am": ("sbuf", [128, 128], "float32"), "IOT": ("sbuf", [128, LM], "float32"),
    "ci": ("sbuf", [128, 8], "int32"), "cf": ("sbuf", [128, 12], "float32"),
    "mk6": ("sbuf", [128, 8], "float32"), "ew": ("sbuf", [128, 8], "float32"),
    "sR": ("sbuf", [128, 4], "float32"), "sX": ("sbuf", [128, 4], "float32"),
    "n1": ("sbuf", [128, 8], "float32"), "cc": ("sbuf", [128, 4], "float32"),
    "B6": ("sbuf", [128, 8], "float32"),
    "offm": ("sbuf", [128, 8], "uint16"), "offc": ("sbuf", [128, 8], "uint16"),
    "Cx": ("sbuf", [128, CAP], "float32"), "RV": ("sbuf", [128, CAP], "float32"),
    "LS": ("sbuf", [128, CAP], "float32"), "X1": ("sbuf", [128, CAP], "float32"),
    "CL": ("sbuf", [128, CAP], "float32"),
    "xp": ("psum", [128, 1024], "float32"), "xq": ("psum", [128, 1536], "float32"),
    "sf": ("psum", [128, 512], "float32"), "se": ("psum", [128, 512], "float32"),
    "sl": ("psum", [128, 512], "float32"),
}
PSUM = ("xp", "xq", "sf", "se", "sl")
NDMA = 16
SEMAPHORES = (["cv", "cs", "cp", "cg", "ho"] + ["d%d" % i for i in range(NDMA)]
              + ["%s%d" % (s, t) for s in ("arr", "out") for t in range(RO)]
              + ["%s%d%s" % (s, t, w) for s in ("fo", "fa", "fb") for t in range(RO) for w in "ZY"])
CYC, PECYC = 0.83e-3, 0.42e-3


def _helpers(core, T, topo):
    near = [c for c in topo.cores_of(core) if topo.die(c) == topo.die(core) and T.rank_of(c) is None]
    return {"Z": near[-1], "Y": near[-2]}


def _mask(engines):
    return sum(1 << e for e in engines)


def _plan(g, core, T, topo, rank):
    A = AluOpType
    AF = ActivationFunctionType
    V, S, PE = g.vector, g.scalar, g.tensor
    ops = []
    ndma = [0]

    def ap(name, a, b, step=1):
        if name == "vo":
            name, a, b = "sl", 256 + a, 256 + b
        v = T[name][:, a:b] if step == 1 else T[name][:, a:b:step]
        return (v, [(name, a, b, step == 1)], (b - a + step - 1) // step)

    def ind(win, off):
        return (win[0].indirect(off[0]), win[1] + off[1], 16 * off[2])

    def add(q, fn, r, w, cost, **more):
        o = {"q": q, "fn": fn, "r": r, "w": w, "cost": cost, "tok": None, "lat": 0.0, "dma": 0.0}
        o.update(more)
        ops.append(o)
        return len(ops) - 1

    def col(x):
        return (x[0], x[1]) if isinstance(x, tuple) else (x, [])

    def kind(x):
        return SCRATCH[x[1][0][0]]

    def price(out, *ins):
        if len(out[1]) > 1:
            return 0.05 + 3.0 * CYC * out[2]
        if len(ins[0][1]) > 1:
            return 0.06 + PAR["gam"] * CYC * out[2]
        half = all(kind(x)[2] in ("bfloat16", "float16", "uint16") for x in (out,) + ins)
        return PAR["fix"] + CYC * max(64, out[2] * (0.5 if half else 1))

    def tt(out, a, b, op, **more):
        c = price(out, a)
        if len(a[1]) == 1 and kind(a)[0] == kind(b)[0]:
            c = PAR["fix"] + CYC * max(64, 2 * out[2])
        add("v", lambda o: V.tensor_tensor(out[0], a[0], b[0], op), a[1] + b[1], out[1], c, **more)

    def ts(out, a, s1, op0, s2=None, op1=None):
        c1, r1 = col(s1)
        c2, r2 = col(s2)
        if op1 is None:
            add("v", lambda o: V.tensor_scalar(out[0], a[0], c1, None, op0), a[1] + r1, out[1], price(out, a))
        else:
            add("v", lambda o: V.tensor_scalar(out[0], a[0], c1, c2, op0, op1), a[1] + r1 + r2, out[1], price(out, a))

    def cp(out, a):
        add("v", lambda o: V.tensor_copy(out[0], a[0]), a[1] + out[1][1:],
            [out[1][0][:3] + (len(out[1]) == 1,)], price(out, a))

    def turn(out, a):
        add("v", lambda o: V.transpose(out[0], a[0]), a[1], out[1], price(out, a))

    def scan(out, d0, d1, op0, op1, **more):
        add("v", lambda o: V.tensor_tensor_scan(out[0], d0[0], d1[0], 0.0, op0, op1), d0[1] + d1[1], out[1],
            price(out, d0, d1), **more)

    def mset(out, c):
        add("v", lambda o: V.memset(out[0], c), [], out[1], price(out, out))

    def act(out, a, f, bias=0.0, scale=1.0, acc=None):
        cb, rb = col(bias)
        cs, rc = col(scale)
        c = price(out, a) if len(a[1]) > 1 else PAR["fix"] + CYC * max(64, out[2])
        if acc is None:
            add("s", lambda o: S.activation(out[0], a[0], f, bias=cb, scale=cs), a[1] + rb + rc, out[1], c)
        else:
            add("s", lambda o: S.activation(out[0], a[0], f, bias=cb, scale=cs, accum_out=acc[0]),
                a[1] + rb + rc, out[1] + acc[1], c)

    def mm(out, l, r, start, stop, **more):
        c = PECYC * max(64, out[2]) * (4 if kind(l)[2] == "float32" else 1)
        add("p", lambda o: PE.matmul(out[0], l[0], r[0], start, o["stop"]), l[1] + r[1], out[1], c,
            stop=stop, start=start, **more)

    def iota(out, pat, base, cm):
        c = 0.15 + 2 * CYC * out[2]
        if kind(out)[2] == "int32":
            add("g", lambda o: g.iota(out[0], pat, base, cm), [], out[1], c)
        else:
            add("g", lambda o: g.iota(out[0], pat, base, cm, allow_small_or_imprecise_dtypes=True), [], out[1], c)

    def sel(out, a, pat, op, base, cm):
        add("g", lambda o: g.affine_select(out[0], a[0], pat, op, 0.0, base, cm), a[1], out[1], 0.17 + 2 * CYC * out[2])

    def dma(q, out, a, tie=(), behind=0.0, **more):
        name = "d%d" % ndma[0]
        ndma[0] += 1
        eng = g.sync if q == "y" else S
        add(q, lambda o: eng.dma_start(out[0], a[0]).then_inc(T.sem[name], 16), a[1], out[1] + list(tie), PAR["yhold"],
            tok=(name, 16), lat=1.5 - PAR["yhold"] + 0.0015 * out[2] + behind, **more)

    def hbm(name, a, b):
        return (T[name][:, a:b], [], b - a)

    Wn = ["W0", "W1", "W2", "W3", "W0"]
    Ln = ["La", "Lc", "La", "Lc", "La"]
    Tn = ["nbi" if PAR["nbw"] else "La"] + Ln[1:]
    On = ["off0", "off1", "off0", "off1"]
    N = len(T.cores)
    dsts = [T.cores[(rank + 1) % N], T.cores[(rank + 4) % N]]
    order = sorted(range(2), key=lambda d: len(topo.engines(core, dsts[d])))
    masks = [0, 0]
    used = []
    for d in order:
        free = [e for e in topo.engines(core, dsts[d]) if e not in used]
        spare = [e for e in free if e not in topo.engines(core, dsts[order[0]])]
        take = (spare[::2] if len(spare) >= 8 else (free[::2] if len(free) >= 8 else free))[:4]
        used += take
        masks[d] = _mask(take)

    def send(t):
        src = ap(Wn[t], GH, GH + 256)

        def fn(o):
            tr = []
            for d in range(2):
                rid, pid = topo.addr(dsts[d], core)
                tr.append(RemoteDMATransfer(dst_ids=[DstId(rid=rid, pnc=pid)], dma_engine_mask=masks[d],
                                            remote_sem=T.sem["arr%d" % t], src=src[0],
                                            dst=T[Wn[t]][:, 256 * d:256 * d + 256]))
            g.remote_dma_fused(tr, local_sem=T.sem["out%d" % t])
        i = add("g", fn, src[1] + ([] if t else [("tie", 8, 9999, True)]), [], 0.5, tok=("out%d" % t, 8), lat=PAR["ghost"][min(t, 1)] - 0.5)
        add("r", None, [], [(Wn[t], 0, GH, True)], 0.3, tok=("arr%d" % t, 8), src=i)

    helper = _helpers(core, T, topo)

    def fold(t):
        m = M[t]
        for w in "ZY":
            eng = topo.engines(core, helper[w])

            def fn(o, w=w, eng=eng):
                rid, pid = topo.addr(helper[w], core)
                tr = RemoteDMATransfer(dst_ids=[DstId(rid=rid, pnc=pid)], dma_engine_mask=_mask(eng),
                                       remote_sem=T.sem["fa%d%s" % (t, w)],
                                       srcs=[T.P[:, k * m:(k + 1) * m] for k in range(16)],
                                       dst=T.P[:, MM * t:MM * t + m], alu_op=3 if w == "Z" else 2)
                g.remote_dma_fused([tr], local_sem=T.sem["fo%d%s" % (t, w)])
            i = add("g", fn, [("P", 0, 16 * m, True), ("tie", t, t + 1, True)], [], 0.5,
                    tok=("fo%d%s" % (t, w), len(eng)), lat=0.7 if t else 1.3, dma=PAR["fold0"] + PAR["fold"] * m, chain="fold")
            add("r", None, [], [(w, 0, m, True)], PAR["back"][min(t, 1)], tok=("fb%d%s" % (t, w), PAR["heng"]), src=i)

    def bounds(sizes, a=0):
        out = []
        for s in sizes:
            out.append((a, a + s))
            a += s
        return out

    M = PAR["m"] + [0]
    nch = [bounds(PAR["nch"][t], M[t]) for t in range(RO)]
    cut = [nch[t][PAR["ncut"][t]][0] for t in range(RO)]
    late = [nch[t][-1][0] for t in range(RO)]
    ends = [[0, M[t], cut[t], BASE[t] - PAR["r4"][t], BASE[t]] for t in range(RO)]
    rng = [[(a, b) for a, b in zip(e, e[1:]) if a < b] for e in ends]
    assert all(e == sorted(e) for e in ends) and ends[RO - 1][3] >= L0N and M[0] <= PAR["q1"] <= PAR["q0"]
    for t in range(RO):
        assert nch[t][-1][1] == BASE[t] and cut[t] <= 512 and BASE[t] - cut[t] <= 512 and late[t] - M[t] <= 512
        assert len(nch[t]) > 1

    def xcol(t, a, b):
        return ap("xp", a, b) if b <= cut[t] else ap("xp", 512 + a - cut[t], 512 + b - cut[t])

    def scol(t, a, b):
        if b <= M[t]:
            return ap("sf", a, b)
        return ap("se", a - M[t], b - M[t]) if b <= late[t] else ap("sl", a - late[t], b - late[t])

    def qcol(t, r, a, b):
        o = 512 * (r % 3) - rng[t][r][0]
        return ap("xq", o + a, o + b)

    def own(name, a, b):
        return ap(name, GH + a, GH + b)

    def dbc(a, b):
        return ap("db", PAD + a, PAD + b)

    def link(name, r, a, b, k):
        if r == 0:
            return ap(name, k * b, (k + 1) * b)
        return ap(name, 16 * a + k, 16 * b, 16)

    def gather(name, t, a, b, q):
        win = Wn[t] if name == "P" else Tn[t]
        src = ind(ap(win, 0, GH + BASE[t]), ap(On[t], a, b))
        out = ap(name, 16 * a, 16 * b)
        sign = 1.0 if name == "P" else -1.0
        if q == "v":
            return V.tensor_scalar(out[0], src[0], sign, None, A.mult)
        return S.activation(out[0], src[0], AF.Copy, bias=0.0, scale=sign)

    def stream(name, t, parts, first=False):
        for a0, b0 in parts:
            unit = PAR["unit_" + name]
            for a in range(a0, b0, unit):
                b = min(a + unit, b0)
                win = Wn[t] if name == "P" else Tn[t]
                v0 = M[t] - PAR["fv"][t] if name == "P" else PAR["qa"][t]
                v1 = M[t] + PAR["cv"][t] if name == "P" else PAR["qa"][t] + PAR["qv"][t]
                add("vs" if PAR["sched"] == 1 else "v" if v0 <= a and b <= v1 else "s", gather,
                    ap(win, 0, GH + BASE[t])[1] + ap(On[t], a, b)[1], ap(name, 16 * a, 16 * b)[1],
                    PAR["gam"] * CYC * 16 * (b - a) + PAR["over"], unit=(name, t, a, b), chain=name, first=first)

    def copy_x(t, bank):
        a, b = ((0, cut[t]), (cut[t], BASE[t]))[bank]
        mm(xcol(t, a, b), ap("I1", 0, 128), own(Wn[t], a, b), True, True)

    def start_s(t, a, b):
        mm(scol(t, a, b), ap("I1", 0, 128), own(Wn[t], a, b), True, False)

    def s_min(a, b):
        n = 16 * (b - a)
        scan(ap("SN", 0, n), ap("m2", 0, n), ap("P", 16 * a, 16 * b), A.add, A.min, chain="scan")

    def s_max(t, a, b):
        n = 16 * (b - a)
        scan(ap("SX", 0, n), ap("m1", 0, n), ap("P", 16 * a, 16 * b), A.mult, A.max, chain="scan")
        mm(scol(t, a, b), ap("Iq", 0, 128), ap("SX", 15, n, 16), False, False)

    def u_a(t, a, b):
        z = ap("Z", a, b) if b <= M[t] else ap("SN", 15, 16 * (b - a), 16)
        tt(ap("ab", a, b), z, xcol(t, a, b), A.mult)

    def scaled(what, t, out, a, c):
        if PAR[what][t] == "s":
            act(out, a, AF.Copy, scale=c)
        elif PAR[what][t] == "g":
            sel(out, a, [[0, out[2]]], A.is_ge, 0, 0)
        else:
            ts(out, a, c, A.mult)

    def u_d(what, t, a, b):
        if PAR["peb"]:
            mm(scol(t, a, b), ap("Ib", 0, 128), ap("ab", a, b), False, True)
        else:
            scaled(what, t, ap("ab", a, b), ap("ab", a, b), -0.75)
            mm(scol(t, a, b), ap("I1", 0, 128), ap("ab", a, b), False, True)

    def u_flag(t, a, b):
        act(ap("fl", a, b), scol(t, a, b), AF.Sign, bias=-(3.5 + 2.0 ** -22), scale=3.5)

    def u_clip(t, a, b):
        ts(own(Wn[t + 1], a, b), scol(t, a, b), 0.0, A.max, 2.0, A.min)

    def l_cmp(t, r, k):
        a, b = rng[t][r]
        f = ap("F", 512 * k, 512 * k + b - a)
        if t == 0 and r == 0 and k < PAR["early"]:
            c = b // 16
            tt(f, ind(own("W0", 0, L0N), ap("off1", k * c, k * c + c)), ap("TT", 576 + a, 576 + b), A.is_gt)
        else:
            tt(f, link("P", r, a, b, k), xcol(t, a, b), A.is_gt, chain="cmp")
        mm(qcol(t, r, a, b), ap("Bm", 16 - k, 144 - k), f, k == 0, False, grp=(t, r))

    def l_diag(t, r):
        a0, b0 = rng[t][r]
        w = b0 if r == 0 else PAR["dw"]
        for a in range(a0, b0, w):
            b = min(a + w, b0)
            for k in range(16):
                mm(qcol(t, r, a, b), ap("Dm", 128 * k, 128 * k + 128), link("Q", r, a, b, k), False, False, grp=(t, r))

    def l_y(t, r):
        a, b = rng[t][r]
        tt(dbc(a, b), qcol(t, r, a, b), ap("Lb", a, b), A.min)

    def l_abs(t, r):
        a, b = rng[t][r]
        act(own(Ln[t + 1], a, b), dbc(a, b), AF.Abs)

    def l_off(t, r):
        a, b = max(rng[t][r][0], M[t + 1]), min(rng[t][r][1], L0N)
        if a < b and PAR["e_of"][4 * t + r] == "s":
            act(ap(On[t + 1], a, b), dbc(a, b), AF.Abs)
        elif a < b:
            scaled("e_of", 4 * t + r, ap(On[t + 1], a, b), own(Ln[t + 1], a, b), 1.0)

    lso = {}
    for m in sorted(set(M[:RO])):
        lso[m] = sum(lso) // 16

    def l_list(t, name, o):
        m = M[t]
        turn(ap("TT", 0, m), ap(name, o, o + m))
        turn(ap("TT", m, 2 * m + 32), ap(name, o - 16, o + m + 16))
        act(ap(On[t], 0, m), ind(ap("TT", 0, 2 * m + 32), ap("lst", lso[m], lso[m] + m // 16)), AF.Abs)

    dma("y", own("W0", 0, 256), hbm("x0", 0, 256), first=True)
    mset(ap("ones", 0, 512), 1.0)
    ops[-1]["first"] = True
    ops[-1]["w"].append(("tie", 5, 6, True))
    dma("s", own("nbi", 0, L0N), hbm("nb", 0, L0N), [("tie", 5, 6, True)], behind=0.5, first=True)
    dma("y", own("W0", 256, L0N), hbm("x0", 256, L0N), behind=1.5, first=True)
    send(0)
    iota(ap("ci", 0, 1), [[0, 1]], 0, 1)
    ts(ap("ci", 1, 2), ap("ci", 0, 1), 15, A.bitwise_and)
    ts(ap("ci", 2, 3), ap("ci", 0, 1), 4, A.logical_shift_right)
    tt(ap("ci", 3, 4), ap("ci", 0, 1), ap("ci", 2, 3), A.add)
    ts(ap("ci", 3, 4), ap("ci", 3, 4), 1, A.bitwise_and)
    cp(ap("cf", 0, 4), ap("ci", 0, 4))
    nl = sum(lso) // 16
    for m in lso:
        iota(ap("lsj", lso[m], lso[m] + m // 16), [[16, m // 16]], 0, 0)
    ts(ap("lsj", 0, nl), ap("lsj", 0, nl), ap("cf", 1, 2), A.add)
    for j, m in enumerate(lso):
        c, o = m // 16, lso[m]
        ts(ap("lsk", o, o + c), ap("lsj", o, o + c), 1.0 / c, A.mult, 0.5 / c - 0.5, A.add)
        ts(ap("cf", 4 + j, 5 + j), ap("cf", 3, 4), m + 16.0, A.mult)
        ts(ap("lsf", o, o + c), ap("lsk", o, o + c), 1.0 - m, A.mult, ap("cf", 4 + j, 5 + j), A.add)
    ts(ap("lsj", 0, nl), ap("lsj", 0, nl), 16.0, A.mult)
    tt(ap("lsf", 0, nl), ap("lsf", 0, nl), ap("lsj", 0, nl), A.add)
    cp(ap("lst", 0, nl), ap("lsf", 0, nl))
    iota(ap("La", 0, GH), [[1, GH]], 0, 0)
    iota(own("La", L0N, LM), [[1, LM - L0N]], GH + L0N, 0)
    iota(ap("nbi", 0, GH), [[1, GH]], 0, 0)
    ops[-1]["first"] = True
    cp(ap("off0", M[0], PAR["q0"]), own("nbi", M[0], PAR["q0"]))
    ops[-1]["first"] = True
    if PAR["q0"] < L0N:
        cp(ap("off0", PAR["q0"], L0N), own("nbi", PAR["q0"], L0N))
    cp(own("La", 0, L0N), own("nbi", 0, L0N))
    l_list(0, "La", GH)
    if PAR["early"]:
        ts(ap("off1", 0, M[0]), ap("off0", 0, M[0]), float(-GH), A.add)
        assert M[0] <= 224
        act(ap("TT", 576, 576 + M[0]), own("W0", 0, M[0]), AF.Copy)
    mset(ap("rd", 16, 17), 0.0)
    mset(ap("db", 0, PAD), 0.0)
    mset(dbc(M[1], M[1] + 16), 0.0)
    mset(ap("n1", 0, 1), float(GH + L0N))
    mset(ap("fl", L0N, LM), -1.0)
    mw = min(PAR["mw"], 16 * max(b - a for ch in nch for a, b in ch))
    mset(ap("m1", 0, mw), 1.0)
    mset(ap("m2", 0, mw), 0.0)
    mset(ap("m1", 0, mw, 16), 0.0)
    mset(ap("m2", 0, mw, 16), 4.0)
    for w in range(mw, 16 * max(b - a for ch in nch for a, b in ch), mw):
        dma("y", ap("m2", w, w + mw), ap("m2", 0, mw), [("tie", 8 + w, 9 + w, True)])
        dma("y", ap("m1", w, w + mw), ap("m1", 0, mw), [("tie", 9 + w, 10 + w, True)])
    iota(ap("Bi", 0, 144), [[1, 144]], -16, 0)
    iota(ap("mk6", 0, 8), [[1, 8]], 0, 0)
    iota(ap("ew", 0, 8), [[16, 8]], -(GH + L0N), 0)
    iota(ap("Am", 0, 128), [[0, 8], [1, 16]], 0, 0)
    iota(ap("I1", 0, 128), [[0, 128]], 1, 0)
    sel(ap("I1", 0, 128), ap("I1", 0, 128), [[-1, 128]], A.is_equal, 0, 1)
    iota(ap("ie", 0, 128), [[1, 128]], 0, 0)
    sel(ap("Tri", 0, 128), ap("ones", 0, 128), [[1, 128]], A.is_ge, 0, -1)
    ts(ap("cf", 10, 11), ap("cf", 2, 3), 16.0, A.mult)
    ts(ap("Bm", 0, 144), ap("Bi", 0, 144), ap("cf", 10, 11), A.is_equal, float(BIG), A.mult)
    ts(ap("sX", 0, 4), ap("mk6", 0, 4), ap("cf", 1, 2), A.is_equal)
    ts(ap("mk6", 0, 8), ap("mk6", 0, 8), ap("cf", 2, 3), A.is_equal)
    ts(ap("sR", 0, 4), ap("sX", 0, 4), -3.0, A.mult, 2.0, A.add)
    ts(ap("ew", 0, 8), ap("ew", 0, 8), ap("cf", 1, 2), A.add)
    ts(ap("sX", 0, 4), ap("sX", 0, 4), -3.0, A.mult, 4.0, A.add)
    ts(ap("Am", 0, 128), ap("Am", 0, 128), ap("cf", 1, 2), A.is_equal)
    scaled("e_c0", 2, ap("Iq", 0, 128), ap("I1", 0, 128), 0.25)
    if PAR["peb"]:
        scaled("e_c0", 2, ap("Ib", 0, 128), ap("I1", 0, 128), -0.75)
    for h in range(4):
        sel(ap("Dm", 512 * h, 512 * h + 512), ap("ones", 0, 512), [[-256, 4], [16, 8], [257, 16]], A.is_equal,
            -1024 * h, -1)
    for t in range(RO):
        iota(own(Wn[t + 1], BASE[t], BASE[t + 1]), [[0, CAP]], 0, 0)
    for h in range(2):
        iota(ap("IOT", 512 * h, 512 * h + 512), [[1, 512]], GH + 512 * h, 0)
    iota(ap("Lc", 0, GH), [[1, GH]], 0, 0)
    iota(own("Lc", L0N, LM), [[1, LM - L0N]], GH + L0N, 0)

    offm, offc = ap("offm", 0, 6), ap("offc", 0, 6)
    yn0 = min(L0N, rng[RO - 1][min(PAR["ynr"], len(rng[RO - 1]) - 1)][1])
    for t in range(RO):
        n, nn, m, lt = BASE[t], BASE[t + 1], M[t], late[t]
        last = t == RO - 1
        W1, L1 = Wn[t + 1], Ln[t + 1]
        ch = nch[t]
        n1 = ap("n1", t, t + 1)
        if t == 0:
            stream("Q", t, [(m, PAR["q1"])], True)
            stream("Q", t, [(PAR["q1"], PAR["q0"])])
        stream("P", t, [(0, m)] + ch)
        fold(t)
        dma("y", ap("Lb", 0, nn), own(Ln[t], 0, nn), [("tie", t, t + 1, True)])
        stream("Q", t, [(0, m), (PAR["q0"], n)] if t == 0 else
               rng[t][1:2] + rng[t][:1] + rng[t][2:] if PAR["turn"][t] else rng[t])
        copy_x(t, 0)
        copy_x(t, 1)
        for a, b in ((m, lt), (0, m), (lt, n)):
            start_s(t, a, b)
        ts(ap("cc", 0, 1), ap("cf", 0, 1), n1, A.add, float(-GH), A.add)
        ts(ap("RV", 0, CAP), ap("ie", 0, CAP), n1, A.add, ap("sR", t, t + 1), A.mult)
        if t > 0:
            ts(offc, ap("ew", 0, 6), n1, A.add)
        for a, b in ch:
            s_min(a, b)
            u_a(t, a, b)
            s_max(t, a, b)
            if b == lt:
                u_d("e_b0", t, m, lt)
                u_flag(t, m, lt)
                u_clip(t, m, lt)
        u_d("e_b1", t, lt, n)
        u_flag(t, lt, n)
        u_a(t, 0, m)
        mm(scol(t, 0, m), ap("Iq", 0, 128), ap("Y", 0, m), False, False)
        u_d("e_b2", t, 0, m)
        u_flag(t, 0, m)
        u_clip(t, lt, n)
        u_clip(t, 0, m)
        J = (nn + 127) // 128
        one = ap("ones", 0, 1)
        for j in range(J):
            mm(ap("vo", j, j + 1), ap("fl", 128 * j, 128 * j + 128), one, True, True)
        ts(ap("rd", 0, J), ap("vo", 0, J), 0.0, A.is_ge)
        scan(ap("rd", 17, 17 + J), ap("rd", 0, J), ap("rd", 0, J), A.add, A.max)
        mm(ap("vo", 16, 17 + J), ap("ones", 0, 128), ap("rd", 16, 17 + J), True, False)
        mm(ap("vo", 16, 16 + J), ap("Tri", 0, 128), ap("rd", 0, J), False, True)
        cp(ap("rd", 32, 32 + J), ap("vo", 16, 16 + J))
        ts(ap("n1", t + 1, t + 2), ap("vo", 16 + J, 17 + J), float(CAP), A.min, n1, A.add)
        for j in range(J):
            ts(ap("Gm", 128 * j, 128 * j + 128), ap("ie", 0, 128), ap("rd", 32 + j, 33 + j), A.is_ge)
        for j in range(J):
            mm(ap("vo", 32, 33), ap("Gm", 128 * j, 128 * j + 128), one, j == 0, j == J - 1)
        ts(ap("B6", 0, 6), ap("mk6", 0, 6), ap("vo", 32, 33), A.mult, ap("cc", 0, 1), A.min)
        mm(ap("vo", 40, 46), ap("Am", 0, 128), ap("B6", 0, 6), True, True)
        cp(offm, ap("vo", 40, 46))
        scaled("e_cx", t, ap("Cx", 0, CAP), ind(own(W1, 0, nn), offm), 0.5)
        cp(ind(own(W1, 0, nn), offm), ap("Cx", 0, CAP))
        if t == 0:
            scaled("e_c0", 0, own(W1, L0N, nn), ap("Cx", 0, CAP), 1.0)
        else:
            cp(ind(own(W1, L0N, nn), offc), ap("Cx", 0, CAP))
        if last:
            dma("y", hbm("yx", 0, LM), own(W1, 0, LM))
        else:
            send(t + 1)
        tt(ap("LS", 0, CAP), ind(own(Ln[t], 0, nn), offm), ap("RV", 0, CAP), A.min)
        cp(ind(ap("Lb", 0, nn), offm), ap("LS", 0, CAP))
        act(ap("X1", 0, CAP), ind(ap("IOT", 0, nn), offm), AF.Copy, scale=ap("sX", t, t + 1))
        todo = list(range(len(rng[t])))
        if PAR["turn"][t]:
            todo = todo[1:2] + todo[:1] + todo[2:]
        need = M[t + 1] if not last else yn0
        while todo:
            r = todo.pop(0)
            for k in range(16):
                l_cmp(t, r, k)
            l_diag(t, r)
            l_y(t, r)
            l_abs(t, r)
            if not last:
                l_off(t, r)
            if need and all(rng[t][x][0] >= need for x in todo):
                if last:
                    dma("y", hbm("yn", 0, yn0), own(L1, 0, yn0))
                else:
                    l_list(t + 1, "db", PAD)
                need = 0
        tt(ap("CL", 0, CAP), ind(own(L1, 0, nn), offm), ap("X1", 0, CAP), A.min)
        if t == 0:
            scaled("e_c0", 1, own(L1, L0N, nn), ap("CL", 0, CAP), 1.0)
        else:
            cp(ind(own(L1, L0N, nn), offc), ap("CL", 0, CAP))
        if not last:
            scaled("e_oc", t, ap(On[t + 1], L0N, nn), own(L1, L0N, nn), 1.0)
    ts(ap("se", 0, LM - L0N), ap("IOT", L0N, LM), ap("n1", RO, RO + 1), A.is_lt)
    tail = own(Ln[RO], L0N, LM)
    tt(tail, tail, ap("se", 0, LM - L0N), A.mult)
    dma("s", hbm("yn", yn0, LM), own(Ln[RO], yn0, LM))
    return ops


def _deps(ops):
    hist, bank, deps = {}, {}, []
    for i, o in enumerate(ops):
        d = set()
        for kind in "rw":
            for x in o[kind]:
                for j, kj, y in hist.get(x[0], []):
                    if (kind == "w" or kj == "w") and x[1] < y[2] and y[1] < x[2]:
                        if "grp" not in o or o["grp"] != ops[j].get("grp") or ops[j]["start"]:
                            d.add(j)
                if x[0] in PSUM:
                    for b in range(x[1] // 512, (x[2] - 1) // 512 + 1):
                        q, now, before = bank.get((x[0], b), (None, [], []))
                        if q != o["q"]:
                            q, now, before = o["q"], [], now
                        d.update(before)
                        now.append(i)
                        bank[x[0], b] = (q, now, before)
        for kind in "rw":
            for x in o[kind]:
                h = hist.setdefault(x[0], [])
                if kind == "w" and x[3] and "grp" not in o and o["q"] != "r":
                    h[:] = [e for e in h if not (x[1] <= e[2][1] and e[2][2] <= x[2])]
                h.append((i, kind, x))
        d.discard(i)
        deps.append({o["src"]} if o["q"] == "r" else d)
    return deps


def _order(ops):
    n = len(ops)
    deps = _deps(ops)
    wake, beta = PAR["wake"], PAR["beta"]
    succ = [[] for _ in ops]
    for i, d in enumerate(deps):
        for j in d:
            succ[j].append(i)
    nxt, prev, seen = {}, {}, {}
    for i, o in enumerate(ops):
        if "chain" in o:
            if o["chain"] in seen:
                nxt[seen[o["chain"]]] = i
                prev[i] = seen[o["chain"]]
            seen[o["chain"]] = i
    rho = {"P": PAR["rho_p"], "Q": PAR["rho_q"], "scan": PAR["rho_s"], "cmp": PAR["rho_c"]}
    lane = {"P": "s", "Q": "s", "scan": "v", "cmp": "v", "fold": "d"}
    tail = [0.0] * n
    seen = {}
    for i in range(n - 1, -1, -1):
        o = ops[i]
        own = o["cost"] + o["lat"] + o["dma"]
        tail[i] = own + max([wake + tail[j] for j in succ[i]] + [0.0])
        if "chain" in o:
            x = lane[o["chain"]]
            if x in seen:
                tail[i] = max(tail[i], rho.get(o["chain"], 1.0) * (o["cost"] + o["dma"]) + tail[seen[x]])
            seen[x] = i
    end, when = [None] * n, [None] * n
    left = [len(d) for d in deps]
    pool = {q: set() for q in "vspgy"}
    todo = {q: sorted((i for i in range(n) if q in ops[i]["q"]), key=lambda i: -tail[i]) for q in "vspgy"}
    free = {q: 0.0 for q in "vspgy"}
    engines = [0.0]
    share = {(x, t): PAR["share_" + x][t] for x in "PQ" for t in range(RO)}
    out = []

    def release(i):
        if ops[i]["q"] == "r":
            finish(i, end[ops[i]["src"]] + ops[i]["cost"])
            out.append(([i], "r"))
        else:
            when[i] = max([end[j] + wake for j in deps[i]] + [0.0])
            for q in ops[i]["q"]:
                pool[q].add(i)

    def finish(i, t):
        end[i] = t
        for j in succ[i]:
            left[j] -= 1
            if left[j] == 0:
                release(j)

    def at(i):
        return when[i]

    def head(i):
        return "unit" not in ops[i] or i not in prev or end[prev[i]] is not None

    def guess(i, t, memo, depth):
        if i not in memo:
            r = 0.0
            for j in deps[i]:
                if end[j] is not None:
                    r = max(r, end[j] + wake)
                elif depth == 0:
                    r = 1e9
                else:
                    o = ops[j]
                    s = max(guess(j, t, memo, depth - 1), min(free.get(q, 0.0) for q in o["q"]), t)
                    r = max(r, s + o["cost"] + o["lat"] + o["dma"] + wake)
                if r > t + 8.0:
                    break
            memo[i] = r
        return memo[i]

    for i in range(n):
        if left[i] == 0:
            release(i)
    done = 0
    total = sum(1 for o in ops if o["q"] != "r")
    while done < total:
        q = min((x for x in free if todo[x]), key=lambda x: free[x])
        t = free[q]
        can = [i for i in pool[q] if head(i) and at(i) <= t + 1e-9 and (
            q != "v" or "unit" not in ops[i] or share[ops[i]["unit"][:2]] > 0)]
        can.sort(key=lambda i: -(tail[i] - (PAR["vbias"][ops[i]["unit"][1]] if q == "v" and "unit" in ops[i] else 0.0)
                                 + (0.0 if "chain" in ops[i] else PAR["small"])))
        pick = None
        soon = 1e9
        if can:
            memo, k = {}, 0
            top = tail[can[0]] - (PAR["small"] if "chain" in ops[can[0]] else 0.0)
            for c in todo[q]:
                if tail[c] <= top or k == PAR["look"]:
                    break
                if end[c] is None and c not in can and ("chain" not in ops[c] or (
                        "unit" not in ops[c] and tail[c] > tail[can[0]])):
                    k += 1
                    soon = min(soon, guess(c, t, memo, 6) + PAR["tol" + q])
            for i in can:
                if t + ops[i]["cost"] - soon <= beta * (soon - t):
                    pick = i
                    break
        if pick is None:
            later = [at(i) for i in pool[q] if head(i) and at(i) > t + 1e-9] + [free[x] for x in free if free[x] > t]
            free[q] = max(t + 0.02, min(later + [soon, t + 0.3]))
            continue
        run = [pick]
        cost = ops[pick]["cost"]
        if "unit" in ops[pick]:
            cost += 0.06
            most = PAR["run_p" if ops[pick]["chain"] == "P" else "run_q"]
            if q == "v":
                most = min(PAR["run_v"], share[ops[pick]["unit"][:2]])
            while run[-1] in nxt:
                j = nxt[run[-1]]
                u, w = ops[run[0]]["unit"], ops[j]["unit"]
                if (left[j] > 0 or at(j) > t or w[1] != u[1] or w[2] != ops[run[-1]]["unit"][3] or w[3] - u[2] > most
                        or t + cost + ops[j]["cost"] - soon > beta * ops[j]["cost"] / 2):
                    break
                run.append(j)
                cost += ops[j]["cost"]
            if q == "v":
                share[ops[pick]["unit"][:2]] -= ops[run[-1]]["unit"][3] - ops[pick]["unit"][2]
        free[q] = t + cost
        e = t + cost + ops[pick]["lat"]
        if ops[pick]["dma"]:
            e = engines[0] = max(e, engines[0]) + ops[pick]["dma"]
        out.append((run, q))
        for i in run:
            for x in ops[i]["q"]:
                pool[x].discard(i)
            end[i] = e
        for i in run:
            finish(i, e)
            for x in ops[i]["q"]:
                todo[x].remove(i)
        done += len(run)
    return out, max(e for e in end)


def _place(order_by, before, after, res, dur, lag, mirror=False):
    n = len(res)
    left = [len(b) for b in before]
    start = [0.0] * n
    busy = {}
    ready = [(order_by[i], i) for i in range(n) if left[i] == 0]
    while ready:
        best = min(ready)
        ready.remove(best)
        i = best[1]
        t = max([start[j] + dur[j] + lag[i if mirror else j] for j in before[i]] + [lag[i] if mirror else 0.0])
        if res[i] != "r":
            line = busy.setdefault(res[i], [])
            lo, hi = 0, len(line)
            while lo < hi:
                mid = (lo + hi) // 2
                if line[mid][1] <= t:
                    lo = mid + 1
                else:
                    hi = mid
            while lo < len(line) and line[lo][0] < t + dur[i]:
                t = max(t, line[lo][1])
                lo += 1
            line.insert(lo, (t, t + dur[i]))
        start[i] = t
        for j in after[i]:
            left[j] -= 1
            if left[j] == 0:
                ready.append((order_by[j], j))
    return start


def _order2(ops):
    deps = _deps(ops)
    wake = PAR["wake"]
    res, dur, lag, before, done = [], [], [], [], []
    last = {}
    for i, o in enumerate(ops):
        b = {done[j] for j in deps[i]}
        if "unit" in o or o.get("chain") == "fold":
            key = o["unit"][:2] + (o["q"],) if "unit" in o else "fold"
            if key in last:
                b.add(last[key])
            last[key] = len(res)
        o["node"] = len(res)
        res.append(o["q"])
        dur.append(o["cost"])
        lag.append(o["lat"] + (0.0 if o["dma"] else wake))
        before.append(b)
        if o["dma"]:
            before.append({len(res) - 1, last.get("d", len(res) - 1)})
            last["d"] = len(res)
            res.append("d")
            dur.append(o["dma"])
            lag.append(wake)
        done.append(len(res) - 1)
    n = len(res)
    after = [[] for _ in res]
    for i, b in enumerate(before):
        for j in b:
            after[j].append(i)
    lane = {"P": PAR["rho_p"], "Q": PAR["rho_q"], "scan": PAR["rho_s"], "cmp": PAR["rho_c"]}
    rho = {o["node"]: lane[o["chain"]] for o in ops if o.get("chain") in lane}
    tail, seen, boost = [0.0] * n, {}, [0.0] * n
    for i in range(n - 1, -1, -1):
        tail[i] = dur[i] + lag[i] + max([tail[j] for j in after[i]] + [0.0])
        if i in rho:
            if res[i] in seen:
                tail[i] = max(tail[i], rho[i] * dur[i] + tail[seen[res[i]]])
            seen[res[i]] = i
    for o in ops:
        if o.get("first") or (o["q"] == "g" and o["tok"]):
            boost[o["node"]] = 1000.0 - o["node"] / n
    key = [-tail[i] - (0.0 if i in rho else PAR["small"]) - boost[i] for i in range(n)]
    best = None
    none = [0.0] * n
    for _ in range(PAR["turns"]):
        start = _place(key, before, after, res, dur, lag)
        end = max(start[i] + dur[i] + lag[i] for i in range(n))
        if best is None or end < best[0]:
            best = (end, start)
        back = _place([-(start[i] + dur[i] + lag[i]) for i in range(n)], after, before, res, dur, lag, True)
        key = [-(back[i] + dur[i]) - (0.0 if i in rho else PAR["small2"]) - boost[i] for i in range(n)]
    end, start = best
    rank = sorted(range(len(ops)), key=lambda i: (start[ops[i]["node"]], i))
    out, open_run = [], {}
    for i in rank:
        o = ops[i]
        q, s = o["q"], start[o["node"]]
        run = open_run.get(q)
        if run and "unit" in o:
            u, w = ops[run[0]]["unit"], o["unit"]
            s0, prev = start[ops[run[0]]["node"]], ops[run[-1]]
            if (u[:2] == w[:2] and prev["unit"][3] == w[2] and w[3] - u[2] <= PAR["run_" + u[0]]
                    and all(start[j] + dur[j] <= s0 for j in before[o["node"]] if j != prev["node"])
                    and all(start[j] >= s + dur[o["node"]] - PAR["hold"] for x in run for j in after[ops[x]["node"]]
                            if j != o["node"] and j not in [ops[y]["node"] for y in run])):
                run.append(i)
                continue
        out.append(([i], q))
        open_run[q] = out[-1][0] if "unit" in o else None
    return out, end


def _arrange(ops, order):
    out = []
    closing = {}
    for run, q in order:
        o = ops[run[0]]
        if "unit" in o:
            name, t, a, _ = o["unit"]
            b = ops[run[-1]]["unit"][3]
            o = {"q": q, "tok": None, "r": [x for i in run for x in ops[i]["r"]], "w": [(name, 16 * a, 16 * b, True)],
                 "fn": lambda x, f=o["fn"], arg=(name, t, a, b, q): f(*arg)}
        if "grp" in o:
            closing[o["grp"]] = o
        if q == "r":
            o["src"] = -1
        out.append(o)
    for o in closing.values():
        o["stop"] = True
    return out


def _emit(g, T, ops):
    queue = {"v": g.vector, "s": g.scalar, "p": g.tensor, "g": g, "y": g.sync}
    semq = {"v": "cv", "s": "cs", "p": "cp", "g": "cg"}
    known = {q: {} for q in queue}
    seen, waits, needed = [], [], set()
    for o in ops:
        o.pop("grp", None)
    for i, (o, d) in enumerate(zip(ops, _deps(ops))):
        w = []
        if o["q"] != "r":
            kn = known[o["q"]]
            for j in sorted(d, reverse=True):
                if o["q"] == "p" and ops[j]["q"] == "p":
                    continue
                key = ops[j]["q"] if ops[j]["tok"] is None else ops[j]["tok"][0]
                if kn.get(key, -1) >= j:
                    continue
                w.append(j)
                needed.add(j)
                kn[key] = j
                for k2, v2 in seen[j].items():
                    if kn.get(k2, -1) < v2:
                        kn[k2] = v2
            seen.append(dict(kn))
        else:
            seen.append({})
        waits.append(w)
    count = {q: 0 for q in semq}
    token = {}
    for i, o in enumerate(ops):
        if o["q"] == "r":
            token[i] = o["tok"]
            continue
        for j in waits[i]:
            queue[o["q"]].wait_ge(T.sem[token[j][0]], token[j][1])
        if o["tok"] is not None:
            o["fn"](o)
            token[i] = o["tok"]
        else:
            ins = o["fn"](o)
            if i in needed:
                count[o["q"]] += 1
                token[i] = (semq[o["q"]], count[o["q"]])
                ins.then_inc(T.sem[semq[o["q"]]], 1)
    for i, o in enumerate(ops):
        if o["tok"] is not None and i not in needed:
            queue["g" if o["q"] == "g" else "y"].wait_ge(T.sem[o["tok"][0]], o["tok"][1])


def _hand_back(g, core, T, topo):
    for home in topo.cores_of(core):
        if T.rank_of(home) is None:
            continue
        for w, h in _helpers(home, T, topo).items():
            if h != core:
                continue
            rid, pid = topo.addr(home, core)
            eng = topo.engines(core, home)[:PAR["heng"]]
            for t in range(RO):
                m = PAR["m"][t]
                g.wait_ge(T.sem["fa%d%s" % (t, w)], len(topo.engines(home, core)))
                g.remote_dma(T[w][:, 0:m], T.P[:, MM * t:MM * t + m], T.sem["fb%d%s" % (t, w)], T.sem.ho,
                             pid, rid, _mask(eng))
            g.wait_ge(T.sem.ho, RO * len(eng))


ORDER = {}


def rank_program(g, core, T, topo):
    rank = T.rank_of(core)
    if rank is None:
        _hand_back(g, core, T, topo)
        return
    ops = _plan(g, core, T, topo, rank)
    key = str(PAR)
    if key not in ORDER:
        ORDER[key] = _order(ops) if PAR["sched"] == 1 else _order2(ops)
    _emit(g, T, _arrange(ops, ORDER[key][0]))
